import numpy as np, ml_dtypes
CORES = [113,118,241,246]
N = 4
BF = ml_dtypes.bfloat16
def gentries(a):
    return np.ascontiguousarray(a.reshape(8, 16, -1).transpose(0, 2, 1)).reshape(8, -1)
def gtable(e):
    e = np.asarray(e); return np.ascontiguousarray(e.reshape(8, -1, 16).transpose(0, 2, 1)).reshape(128, -1).astype(np.int32)
B, J, CAP, RO, Q = 3072, 4096, 96, 2, 4096
LN, LJ = 2, 12
M = N * CAP; W = B + RO * M
WT = (14 * np.arange(16) + 9)[:, None]
def decode(n):
    C = np.add.accumulate((n * n[..., ::-1]) >> 12, axis=-1)
    x = (C[..., -1:] * np.arange(J)) >> LJ
    return np.add.reduce((C[..., None] <= x[..., None, :]).astype(np.int64), axis=-2)
def combine(x, y, z):
    q = x.shape[-1] // 4
    k = np.concatenate([np.minimum(x[..., :q], y[..., :q]), np.maximum(x[..., q:2 * q], y[..., q:2 * q]), np.abs(x[..., 2 * q:3 * q] - y[..., 2 * q:3 * q]), x[..., 3 * q:] + y[..., 3 * q:]], axis=-1)
    return np.minimum(k, z)
def sizes(c):
    c = np.sort(c, axis=-1); z = np.zeros(c.shape[:-1] + (1,), np.int64)
    return np.diff(np.concatenate([z, c, z + B - 256], axis=-1), axis=-1) + 64
def span(rng, v, share):
    o = rng.integers(0, B, (3, N, 8, 1, 2048)); x, y, z = [np.take_along_axis(v, i, 3) for i in o]
    s = np.sort(np.add.reduce(combine(x, y, z), axis=2), axis=-1)
    m = np.minimum(np.maximum((2048 * share).astype(np.int64), 1), 2048); k = (rng.random((N, 8)) * (2048 - m)).astype(np.int64)
    return np.concatenate([np.take_along_axis(s, k[..., None], 2), np.take_along_axis(s, (k + m - 1)[..., None], 2)], axis=2)
def shares(rng):
    return CAP * N * 2.0 ** -LJ * rng.choice(np.array([0.4, 0.8, 1.0, 1.5]), (N, 8))
def parts(rng):
    e = rng.choice(np.array([0.5, 1.0, 1.0, 2.0]), (N, 8, 16, 1))
    v = np.minimum((256 * rng.random((N, 8, 16, B)) ** e).astype(np.int64), 255)
    n = sizes(rng.integers(0, B - 255, (N, 8, 3))); r = rng.integers(0, 4096, (3, N, 8, RO, J))
    u = (rng.random((N, 8, Q)) < rng.choice(np.array([0.05, 0.2, 0.5]), (N, 8, 1))).astype(np.int64)
    return v, n, span(rng, v, shares(rng)), r, u
def pack(v, n, lim, r, u):
    t = [np.stack([gtable(a.reshape(8, -1)) for a in b]) for b in r]
    return {"bank": np.ascontiguousarray(v.reshape(N, 128, B)).astype(np.float32).astype(BF), "ncl": n.astype(np.int32), "lim": lim.astype(np.int32),
            "ra": t[0], "rb": t[1], "rc": t[2], "used": u.astype(np.int32)}
def goals(rng, k):
    return np.stack([rng.permutation(Q - 1)[:k] + 1 for p in range(N)]) * N + np.arange(N)[:, None]
def keyed(rng, d):
    c = rng.integers(1, 256, (16, d.size)); c[[0, 1, 15]] = rng.integers(40, 101, (3, d.size))
    e = (d - np.add.reduce(c * WT, axis=0)) & (N * Q - 1)
    c[15] += e // 219; e = e % 219; c[0] += e // 9 - 5 * (e % 9); c[1] += 2 * (e % 9)
    return c
def put(rng, v, n, q, g, d):
    s = np.add.accumulate(n[q, g]) - n[q, g]; v[q, g][:, s] = 255; v[q, g][:, s + 1] = 0
    w = rng.permutation(np.setdiff1d(np.arange(B), np.concatenate([s, s + 1])))[:d.size]
    v[q, g][:, w] = keyed(rng, d.reshape(-1)); return w.reshape(d.shape)
def deal(rng, col, at, w):
    o = rng.permutation(np.repeat(np.arange(N), CAP)); at = np.sort(rng.permutation(at)[:M])
    for p in range(N): col[at[o == p]] = w[p]
def play(r, n, q, g, t, col):
    h = J // 4; k = B + t * M; r[:2, q, g, t] = 0; r[2, q, g, t] = (col * 4096 + k - 1) // k
    if t == 0:
        m = n[q, g][3 - decode(n[q, g])[2 * h:3 * h]]; r[1, q, g, 0, 2 * h:3 * h] = (4096 + m - 1) // m
def setup_inputs(rng):
    return pack(*parts(rng))
def setup_inputs_room(rng):
    v, n, lim, r, u = parts(rng); lim[:] = (1500, 2600)
    for q in range(N):
        for g in range(8):
            m = n[q, g]; p = np.concatenate([np.arange(k) for k in m]); live = p >= np.repeat(m // 2, m)
            c = np.where(live, rng.integers(110, 150, (16, B)), rng.integers(0, 90, (16, B)))
            c[0] += (p - np.add.reduce(c * WT, axis=0)) & (N - 1)
            c[:, p == 0] = 0; c[:, p == 1] = 255; v[q, g] = c
            t = rng.choice(np.array([0, 1, CAP - 1, CAP, CAP + 1, 2 * CAP]), N)
            if q == 0: t[1] = (CAP, CAP + 1, CAP - 1, CAP, 0, 1, 2 * CAP, CAP)[g]
            if g == 6: t[2] = 0
            own = np.full(J, -1); own[rng.permutation(J)[:int(np.sum(t))]] = rng.permutation(np.repeat(np.arange(N), t))
            a = decode(m); na = m[a]; nb = m[3 - a]; h = na // 2
            dead = 2 + (rng.random(J) * (h - 2)).astype(np.int64)
            good = h + (own - h) % N + N * (rng.random(J) * ((na - h - N) // N + 1)).astype(np.int64)
            i = np.where(own < 0, dead, good); y = (np.arange(J) < J // 4).astype(np.int64)
            r[0, q, g, 0] = (i * 4096 + na - 1) // na; r[1, q, g, 0] = (y * 4096 + nb - 1) // nb; r[2, q, g, 0] = (4096 + B - 1) // B
    return pack(v, n, lim, r, u)
def setup_inputs_ends(rng):
    v, n, lim, r, u = parts(rng); v[..., 0] = 0; v[..., B - 1] = 255
    for g in range(4):
        n[:, g] = 64; n[:, g, g] = B - 192
    n[:, 5] = n[:, 2]; lim[0, 5] = (1, 4080)
    for g in (0, 2, 4): r[:, :, g] = rng.choice(np.array([0, 1, 4094, 4095]), (3, N, RO, J))
    lim[:, 0] = (0, 4080); lim[:, 2] = (4080, 4080); lim[:, 4] = (0, 0); lim[:, 6, 0] = lim[:, 6, 1]
    r[:, :, 2, 0, J - 1] = 4095; r[2, :, 4, 0, :8] = 0; u[:, 2] = 0; u[:, 4] = 0
    r[2, :, 0, 0, :8] = 0; u[:, 0] = 0
    lim[:, 1] = (1, 4080); lim[:, 3] = (1, 4080); lim[:, 7] = (0, 4079); u[:, 1] = 0; u[:, 3] = 0; u[:, 7] = 0
    full = goals(rng, RO * M).reshape(N, RO, N, CAP)
    grid = goals(rng, M).reshape(N, N, CAP); grid[1:, N - 1, CAP - 1] = grid[1:, 0, 0]
    many = goals(rng, 2 * CAP); at = np.concatenate([np.arange(J // 4, J // 2), np.arange(3 * J // 4, J)])
    for q in range(N):
        w = put(rng, v, n, q, 3, full[:, :, q])
        for t in range(RO):
            col = np.full(J, 1); deal(rng, col, at, w[:, t]); play(r, n, q, 3, t, col)
        i = J // 8 + rng.permutation(J // 8)[:4]; r[0, q, 3, RO - 1, i] = rng.integers(1000, 4096, 4); r[2, q, 3, RO - 1, i] = 0
        w = put(rng, v, n, q, 7, grid[:, q])
        if q == N - 1: w[0, CAP - 1] = 1
        col = np.zeros(J, np.int64); deal(rng, col, np.arange(J), w); play(r, n, q, 7, 0, col)
        w = put(rng, v, n, q, 1, many[(q + 1) % N]); col = np.full(J, 1); k = J // 4
        if q > 0: k += int(rng.integers(0, CAP))
        i = np.sort(rng.permutation(J // 2)[:k]); col[i] = w[rng.integers(0, CAP, k)]; col[i[:CAP]] = w[:CAP]
        col[J // 2 + rng.permutation(J // 2)[:2 * CAP]] = np.tile(w[CAP:], 2); play(r, n, q, 1, 0, col)
    return pack(v, n, lim, r, u)
def setup_inputs_alike(rng):
    v, n, lim, r, u = parts(rng)
    a = rng.integers(1, 255, (8, 16, 3)); tw = np.zeros((16, 1), np.int64); tw[:4, 0] = (1, -1, -1, 1)
    pool = np.concatenate([a, a + tw], axis=2)
    for g in range(1, 8, 2):
        v[:, g] = pool[g][:, rng.integers(0, 6, (N, B))].transpose(1, 0, 2)
        for q in range(N):
            e = np.add.accumulate(n[q, g]); v[q, g][:, e - n[q, g]] = pool[g][:, :1]; v[q, g][:, e - 1] = pool[g][:, 3:4]
    lim[:, 1::2] = (0, 4080); u[:, 1::2] = 0; r[:, :, 1::2, 0, 0] = 0; r[:, :, 1::2, 0, 1] = 4095
    v[:, 2] = v[0, 2]; n[:, 2] = n[0, 2]; lim[:, 2] = lim[0, 2]; r[:, :, 2] = r[:, :1, 2]
    return pack(v, n, lim, r, u)
def setup_inputs_cold(rng):
    v, n, lim, r, u = parts(rng); o = rng.permutation(N); g = int(rng.integers(0, 8))
    lim[o[0]] = (1, 0); lim[o[0], 1::2] = (1600, 1000); lim[o[1]] = (0, 4080)
    lim[:, g] = (1700, 1100); lim[o[0], g] = (2000, 1999); lim[o[1], g] = (4080, 0); u[:, (g + 1) % 8] = 1; u[:, (g + 2) % 8] = 0
    u[o[2], (g + 3) % 8] = 1
    return pack(v, n, lim, r, u)
def setup_inputs_spread(rng):
    v, n, lim, r, u = parts(rng)
    v = np.minimum((np.exp2(8 * rng.random((N, 8, 1, B))) * rng.random((N, 8, 16, B))).astype(np.int64), 255)
    n = sizes(((B - 256) * rng.random((N, 8, 3)) ** 4).astype(np.int64))
    e = rng.choice(np.array([0.5, 1.0, 2.0, 3.0]), (3, N, 8, RO, 1)); r = np.minimum((4096 * rng.random((3, N, 8, RO, J)) ** e).astype(np.int64), 4095)
    u = (rng.random((N, 8, Q)) < 0.8 * rng.random((N, 8, 1))).astype(np.int64)
    return pack(v, n, span(rng, v, shares(rng)), r, u)
def check_inputs(d):
    bad = []; b = np.asarray(d["bank"]).astype(np.float32)
    if not np.all((b >= 0) & (b <= 255) & (b == np.floor(b))): bad.append("bank: whole numbers from 0 to 255")
    for k, lo, hi in (("ncl", 64, B), ("lim", 0, 4080), ("ra", 0, 4095), ("rb", 0, 4095), ("rc", 0, 4095), ("used", 0, 1)):
        if np.min(d[k]) < lo or np.max(d[k]) > hi: bad.append("range of " + k)
    if np.any(np.sum(np.asarray(d["ncl"]).astype(np.int64), axis=-1) != B): bad.append("sums of ncl")
    return bad
def reference(bank, ncl, lim, ra, rb, rc, used):
    v = np.zeros((N, 8, 16, W), np.int32); v[..., :B] = bank.astype(np.float32).astype(np.int32).reshape(N, 8, 16, B)
    n = np.zeros((N, 8, 4 + RO), np.int64); n[:, :, :4] = ncl
    la, lb, lc = [np.stack([gentries(a) for a in b]).astype(np.int64).reshape(N, 8, RO, J) for b in (ra, rb, rc)]
    free = used == 0; lo = lim[:, :, :1]; hi = lim[:, :, 1:]; take = np.take_along_axis
    for t in range(RO):
        s = 4 + t; m = n[:, :, :s].copy(); start = np.add.accumulate(m, axis=2) - m; tot = np.add.reduce(m, axis=2)
        a = decode(m); b = s - 1 - a
        ix = take(start, a, 2) + ((take(m, a, 2) * la[:, :, t]) >> 12)
        iy = take(start, b, 2) + ((take(m, b, 2) * lb[:, :, t]) >> 12)
        iz = (tot[:, :, None] * lc[:, :, t]) >> 12
        x, y, z = [take(v, i[:, :, None, :], 3) for i in (ix, iy, iz)]
        k = combine(x, y, z)
        total = np.add.reduce(k, axis=2); key = np.add.reduce(k * WT, axis=2)
        alive = (total >= lo) & (total <= hi); owner = key & (N - 1); bucket = (key >> LN) & (Q - 1)
        for p in range(N):
            for g in range(8):
                got = [np.flatnonzero(alive[q, g] & (owner[q, g] == p))[:CAP] for q in range(N)]
                c = np.concatenate([k[q, g][:, got[q]] for q in range(N)], axis=1); bu = np.concatenate([bucket[q, g, got[q]] for q in range(N)])
                first = np.sort(np.unique(bu, return_index=True)[1])
                keep = first[free[p, g, bu[first]]]; e = int(tot[p, g])
                v[p, g][:, e:e + len(keep)] = c[:, keep]; free[p, g, bu[keep]] = False; n[p, g, s] = len(keep)
    return {"y": np.ascontiguousarray(v[..., B:]).reshape(N, 128, RO * M).astype(np.float32).astype(BF)}

@@ -1,0 +1,583 @@
+from concourse.bass import DstId, RemoteDMATransfer
+from concourse.mybir import AluOpType as A, ActivationFunctionType as F
+
+F32, BF, I32, U16 = "float32", "bfloat16", "int32", "uint16"
+B, J, CAP, N = 3072, 4096, 96, 4
+M = N * CAP
+MAGIC = 12582912.0
+HALF = -2047.5 / 4096
+MID = 1728
+BIAS = HALF - MID
+DEAD = 524288
+PAIR = 272
+INV = 1048576
+UNIT = 32
+
+SCRATCH = {}
+ALIAS, COLS, SIZE = {}, {}, {F32: 0, BF: 0, I32: 0}
+for _n, _c, _d in [
+    ("nl", 8, I32), ("nf", 8, F32), ("sc", 8, F32), ("nq", 8, F32), ("cs4", 8, F32), ("ub", 8, F32), ("pr", 4, F32), ("wq", 4, F32), ("w", 4, F32),
+    ("one8", 128, F32), ("b8a", 128, F32), ("b8", 128, F32), ("on4", 8, F32),
+    ("pid", 1, I32), ("ri", 1, I32), ("rf", 1, F32), ("wk", 1, F32), ("wl0", 1, F32), ("wl", 1, F32),
+    ("jc0", 256, F32), ("jc", 256, F32), ("trx0", 64, F32), ("tk0", 24, F32), ("tk", 24, F32), ("tb0", 24, F32), ("tb", 24, F32),
+    ("ob", 128, BF), ("ba", 128, BF), ("blk", 128, BF), ("nb", 128, BF), ("nblk", 128, BF), ("tri", 128, BF), ("neg", 128, BF), ("stri", 128, BF),
+    ("kib", 128, BF), ("idn", 128, BF), ("kblk", 128, BF), ("mob", 128, BF), ("idp", 128, BF), ("idm", 128, BF), ("z16", 16, BF),
+    ("onx", 2048, BF), ("kwx", 2048, BF), ("lwx", 2048, BF), ("tx", 2048, BF),
+    ("vd", 512, BF), ("vdb", 512, F32), ("rst", 64, BF), ("one", 384, BF), ("p6", 64, BF), ("cap", 64, F32), ("p272", 24, BF), ("mone", 24, BF), ("ud", 384, I32),
+    ("nmid", 1, F32), ("nhl", 1, F32), ("qd", 1, F32), ("q1", 1, F32), ("b75", 1, F32), ("bia", 1, F32), ("b4", 1, F32),
+    ("bx0", 4, F32), ("by0", 4, F32), ("bx1", 4, F32), ("by1", 4, F32), ("wb", 1, F32), ("k1", 1, F32),
+    ("scx0", 1, F32), ("scy0", 1, F32), ("scx1", 1, F32), ("scy1", 1, F32),
+    ("n4", 1, F32), ("n4q", 1, F32), ("tq", 1, F32), ("wx", 1, F32), ("w0", 1, F32),
+    ("la", 512, I32), ("lb", 512, I32), ("lc", 512, I32), ("laf", 512, F32), ("lbf", 512, F32), ("lcf", 512, F32),
+    ("ux0", 1024, F32), ("uy0", 1024, F32), ("ux1", 1280, F32), ("uy1", 1280, F32),
+    ("hx0", 1024, BF), ("hy0", 1024, BF), ("hx1", 1280, BF), ("hy1", 1280, BF), ("sox", 1280, F32), ("soy", 1280, F32),
+    ("zf", 256, F32), ("lx", 256, U16), ("ly", 256, U16), ("lz", 256, U16),
+    ("bk", B + 4 * M, BF), ("yv", J, BF), ("xv", 1024, BF), ("fv", J, BF), ("cand", J + 16, BF),
+    ("ab", 256, F32), ("dead", 256, F32), ("zt", 256, I32), ("z2", 256, I32), ("zb", 256, BF), ("ind", 1024, BF),
+    ("clb", 64, BF), ("csb", 64, BF), ("e0", 64, BF), ("iv", 64, F32), ("t1", 64, F32), ("t3", 64, F32), ("off", 64, U16),
+    ("win0", 704, BF), ("win1", 704, BF), ("wib0", 704, F32), ("wib1", 704, F32),
+    ("ns", 384, BF), ("c1", 384, BF), ("cnt", 384, BF), ("po", 24, U16), ("pref", 4 * PAIR, BF),
+    ("ll", 384, BF), ("jl", 24, U16), ("snd0", 288, BF), ("snd1", 288, BF), ("arr0", M, BF), ("arr1", M, BF),
+    ("ki", 24, I32), ("kb", 24, I32), ("kf", 24, F32), ("kb2", 24, I32), ("bm", 24, F32), ("bo", 24, U16), ("r32", M, I32), ("r33", M, I32), ("r16", M, U16),
+    ("tbl", J + 16 + M, I32), ("us", M, BF), ("eq", 24 * M, BF), ("dm", M, BF),
+    ("nk", 24, BF), ("kp", 24, BF), ("ks", 24, BF), ("tn", 24, F32), ("om", 24, F32), ("mo", 24, U16), ("tn2", 24, F32), ("om2", 24, F32), ("mo2", 24, U16),
+]:
+    COLS[_n] = _c
+    if _c <= 128 and _d != U16 and _n != "nl":
+        ALIAS[_n] = ({F32: "pf", BF: "pb", I32: "pi"}[_d], SIZE[_d])
+        SIZE[_d] += -(-_c // 8) * 8
+    else:
+        SCRATCH[_n] = ("sbuf", [128, _c], _d)
+SCRATCH["pf"] = ("sbuf", [128, SIZE[F32]], F32)
+SCRATCH["pb"] = ("sbuf", [128, SIZE[BF]], BF)
+SCRATCH["pi"] = ("sbuf", [128, SIZE[I32]], I32)
+for _n in range(8):
+    SCRATCH["ps%d" % _n] = ("psum", [128, 512], F32)
+
+DMAS = ["d_ncl", "d_lim", "d_la0", "d_lb0", "d_lc0", "d_la1", "d_lb1", "d_lc1", "d_bk", "d_used", "d_y"]
+SEMAPHORES = ["cv", "cs", "ct", "cg", "arrv0", "arrv1", "snt0", "snt1"] + DMAS
+
+
+def plan(src, cores, topo):
+    own = topo.cores_of(src)
+    far = [c for c in cores if c not in own]
+    out = {}
+    taken = []
+    for i, d in enumerate(far):
+        e = topo.engines(src, d)
+        n = len(e) // len(far)
+        out[d] = e[i * n:(i + 1) * n]
+        taken += e
+    for d in cores:
+        if d in own and d != src:
+            out[d] = [e for e in topo.engines(src, d) if e not in taken][:4]
+    return out
+
+
+def overlap(a, b):
+    if a.start >= b.stop or b.start >= a.stop:
+        return False
+    if a.step == b.step and a.step > 1 and (a.start - b.start) % a.step:
+        return False
+    return True
+
+
+def covers(a, b):
+    return a.step == 1 and a.start <= b.start and b.stop <= a.stop
+
+
+def rank_program(g, core, T, topo):
+    rank = T.rank_of(core)
+    if rank is None:
+        return
+    cores = list(T.cores)
+    queues = {"v": g.vector, "s": g.scalar, "t": g.tensor, "g": g, "y": g.sync}
+    qsem = {"v": "cv", "s": "cs", "t": "ct", "g": "cg"}
+    count = {"v": 0, "s": 0, "t": 0, "g": 0}
+    known = {q: {} for q in queues}
+    wrote, read = {}, {}
+    order = [0]
+
+    def need(q, toks):
+        for t in sorted(toks, key=lambda t: -t["n"]):
+            if known[q].get(t["sem"], 0) < t["val"]:
+                queues[q].wait_ge(T.sem[t["sem"]], t["val"])
+                for k, v in t["snap"].items():
+                    if known[q].get(k, 0) < v:
+                        known[q][k] = v
+                known[q][t["sem"]] = max(known[q].get(t["sem"], 0), t["val"])
+
+    def prepare(q, outs, ins):
+        toks = []
+        for n, r in ins:
+            for r2, t in wrote.get(n, []):
+                if overlap(r, r2):
+                    toks.append(t)
+            if n.startswith("ps"):
+                toks += [t for r2, t in wrote.get(n, []) + read.get(n, []) if t["q"] != q]
+        for n, r in outs:
+            ps = n.startswith("ps")
+            for r2, t in wrote.get(n, []):
+                if ps and t["q"] != q or (overlap(r, r2) and not (ps and q == "t")):
+                    toks.append(t)
+            for r2, t in read.get(n, []):
+                if t["q"] != q and (ps or overlap(r, r2)):
+                    toks.append(t)
+        need(q, toks)
+
+    def record(q, outs, ins, sem, val):
+        order[0] += 1
+        tok = {"n": order[0], "sem": sem, "val": val, "q": q, "snap": dict(known[q])}
+        for n, r in outs:
+            wrote[n] = [x for x in wrote.get(n, []) if not covers(r, x[0]) or n.startswith("ps")] + [(r, tok)]
+            if not n.startswith("ps"):
+                read[n] = [x for x in read.get(n, []) if not covers(r, x[0])]
+        for n, r in ins:
+            read[n] = [x for x in read.get(n, []) if not (x[1]["q"] == q and x[0] == r)] + [(r, tok)]
+        for n, r in outs + ins:
+            if n.startswith("ps"):
+                for d in (wrote, read):
+                    d[n] = list({(x[1]["q"], x[0].start, x[0].stop): x for x in d.get(n, [])}.values())
+
+    def R(name, a=0, b=None, st=1, rows=None):
+        b = COLS.get(name, 512) if b is None else b
+        if name in ALIAS:
+            name, o = ALIAS[name]
+            a, b = a + o, b + o
+        cols = slice(a, b) if st == 1 else slice(a, b, st)
+        ap = T[name][:, cols] if rows is None else T[name][rows, cols]
+        return (ap, [(name, range(a, b, st))])
+
+    def X(w, o):
+        return (w[0].indirect(o[0]), w[1] + o[1])
+
+    def emit(q, outs, ins, f):
+        prepare(q, outs, ins)
+        inst = f(queues[q])
+        count[q] += 1
+        inst.then_inc(T.sem[qsem[q]], 1)
+        record(q, outs, ins, qsem[q], count[q])
+
+    def scal(x):
+        return (x[0], x[1]) if isinstance(x, tuple) else (x, [])
+
+    def ts(o, i, s1, s2, op0, op1=None):
+        a, ra_ = scal(s1)
+        b, rb_ = scal(s2)
+        if op1 is None:
+            emit("v", o[1], i[1] + ra_, lambda e: e.tensor_scalar(o[0], i[0], a, None, op0))
+        else:
+            emit("v", o[1], i[1] + ra_ + rb_, lambda e: e.tensor_scalar(o[0], i[0], a, b, op0, op1))
+
+    def tt(o, a, b, op):
+        emit("v", o[1], a[1] + b[1], lambda e: e.tensor_tensor(o[0], a[0], b[0], op))
+
+    def cp(o, i):
+        emit("v", o[1], i[1], lambda e: e.tensor_copy(o[0], i[0]))
+
+    def scatter(w, o, i):
+        emit("v", w[1], i[1] + o[1], lambda e: e.tensor_copy(w[0].indirect(o[0]), i[0]))
+
+    def scan(o, a, b, op0, op1):
+        emit("v", o[1], a[1] + b[1], lambda e: e.tensor_tensor_scan(o[0], a[0], b[0], 0.0, op0, op1))
+
+    def fill(o, c):
+        emit("v", o[1], [], lambda e: e.memset(o[0], c))
+
+    def act(o, i, func, scale=None, bias=None):
+        kw, more = {}, []
+        for k, x in (("scale", scale), ("bias", bias)):
+            if x is not None:
+                kw[k] = x[0]
+                more = more + x[1]
+        emit("s", o[1], i[1] + more, lambda e: e.activation(o[0], i[0], func, **kw))
+
+    def mm(o, l, r, start, stop):
+        emit("t", o[1], l[1] + r[1], lambda e: e.matmul(o[0], l[0], r[0], start, stop))
+
+    def iota(o, pattern, base, cm=0):
+        emit("g", o[1], [], lambda e: e.iota(o[0], pattern, base, cm, allow_small_or_imprecise_dtypes=True))
+
+    def sel(o, i, pattern, op, base, cm):
+        emit("g", o[1], i[1], lambda e: e.affine_select(o[0], i[0], pattern, op, 0.0, base, cm))
+
+    def dma(q, sem, o, i, total=16):
+        if total == 16:
+            prepare(q, o[1], i[1])
+        queues[q].dma_start(o[0], i[0]).then_inc(T.sem[sem], 16)
+        record(q, o[1], i[1], sem, total)
+
+    def ext(ap):
+        return (ap, [])
+
+    def listify(o, wname, src, ncols, start, stop, st=16):
+        for x in range(16):
+            mm(o, R(wname, 128 * x, 128 * x + 128), R(src, x, ncols, st), start and x == 0, stop and x == 15)
+
+    def P(k, a, b):
+        return R("ps%d" % k, a, b)
+
+    def spread(name, src, xs=range(16)):
+        for x in xs:
+            act(R(name, 129 * x, 128 * x + 128, 16), R(src, x, 128, 16), F.Copy)
+
+    first8 = slice(0, 8)
+    dma("y", "d_ncl", R("nl", 0, 4, rows=first8), ext(T.ncl[:, :]))
+    dma("s", "d_lim", R("nl", 4, 6, rows=first8), ext(T.lim[:, :]))
+    dma("y", "d_lb0", R("lb", 0, 256), ext(T.rb[:, 0:256]))
+    dma("s", "d_la0", R("la", 0, 256), ext(T.ra[:, 0:256]))
+    dma("y", "d_lc0", R("lc", 0, 256), ext(T.rc[:, 0:256]))
+    dma("y", "d_bk", R("bk", 0, B), ext(T.bank[:, :]))
+    dma("y", "d_lb1", R("lb", 256, 512), ext(T.rb[:, 256:512]))
+    dma("y", "d_la1", R("la", 256, 512), ext(T.ra[:, 256:512]))
+    dma("y", "d_lc1", R("lc", 256, 512), ext(T.rc[:, 256:512]))
+    for r in range(16):
+        dma("y", "d_used", R("tbl", 0, J, rows=slice(r, 128, 16)), ext(T.used[:, :]), 256)
+
+    fill(R("ob"), 1.0)
+    fill(R("one8"), 1.0)
+    iota(R("pid"), [[0, 1]], 0, 1)
+    ts(R("ri"), R("pid"), 15, None, A.bitwise_and)
+    cp(R("rf"), R("ri"))
+    fill(R("onx"), 0.0)
+    ts(R("wk"), R("rf"), 14.0, 9.0, A.mult, A.add)
+    ts(R("wl0"), R("rf"), 15.0, 8191.0 * UNIT, A.is_equal, A.mult)
+    sel(R("ba"), R("ob"), [[-16, 8], [0, 16]], A.is_ge, 0, 1)
+    sel(R("blk"), R("ba"), [[16, 8], [0, 16]], A.is_ge, 15, -1)
+    sel(R("b8a", rows=first8), R("one8", rows=first8), [[1, 128]], A.is_ge, 0, -16)
+    sel(R("b8", rows=first8), R("b8a", rows=first8), [[-1, 128]], A.is_ge, 15, 16)
+    iota(R("jc0"), [[16, 256]], -2048)
+    for h in ("hy0", "hx0"):
+        iota(R(h, 0, 1024, 4), [[0, 256]], -4096)
+    spread("onx", "blk", range(10))
+
+    cp(R("nf", 0, 6, rows=first8), R("nl", 0, 6, rows=first8))
+    mm(P(7, 0, 6), R("b8", rows=first8), R("nf", 0, 6, rows=first8), True, True)
+    for x in range(10, 16):
+        cp(R("onx", 129 * x, 128 * x + 128, 16), R("blk", x, 128, 16))
+    act(R("kwx"), R("onx"), F.Copy, scale=R("wk"))
+    cp(R("sc", 0, 6), P(7, 0, 6))
+
+    def pairs(k, ab):
+        for i, (a, b) in enumerate(ab):
+            tt(R("pr", k + i, k + i + 1), R("sc", a, a + 1), R("sc", b, b + 1), A.mult)
+        ts(R("wq", k, k + 2), R("pr", k, k + 2), 1.0 / 4096, HALF, A.mult, A.add)
+
+    pairs(0, ((0, 3), (1, 2)))
+    ts(R("jc"), R("jc0"), R("rf"), None, A.add)
+    ts(R("w", 0, 2), R("wq", 0, 2), MAGIC, MAGIC, A.add, A.subtract)
+    fill(R("by0", 1, 2), -2048.0)
+    fill(R("on4"), 1.0)
+    ts(R("by0", 0, 1), R("w", 1, 2), -16777216.0, -2048.0, A.mult, A.add)
+    ts(R("by0", 2, 3), R("w", 1, 2), 16777216.0, -2048.0, A.mult, A.add)
+    ts(R("scy0"), R("w", 0, 1), R("w", 1, 2), -8192.0, A.add, A.mult)
+    ts(R("nq", 0, 4), R("sc", 0, 4), 1.0 / 4096, None, A.mult)
+    scan(R("cs4", 0, 4), R("on4", 0, 4), R("sc", 0, 4), A.mult, A.add)
+    fill(R("ub", 0, 1), BIAS)
+    ts(R("scx0"), R("w", 0, 1), R("w", 1, 2), 8192.0, A.add, A.mult)
+    ts(R("ub", 1, 4), R("cs4", 0, 3), BIAS, None, A.add)
+    ts(R("wl"), R("wl0"), float(UNIT), None, A.add)
+    ts(R("bx0", 0, 3), R("by0", 0, 3), -1.0, None, A.mult)
+
+    def affine(t, who, k, s):
+        i = s - 1 - k
+        act(R("u%s%d" % (who, t), i, 256 * s, s), R("l%sf" % ("a" if who == "x" else "b"), 256 * t, 256 * t + 256), F.Identity,
+            scale=R("nq", k, k + 1), bias=R("ub", k, k + 1))
+
+    def hmask(t, who, i, s):
+        k = s - 1 - i if who == "x" else i - 1
+        act(R("h%s%d" % (who, t), i, 256 * s, s), R("jc"), F.Identity, scale=R("sc%s%d" % (who, t)), bias=R("b%s%d" % (who, t), k, k + 1))
+
+    def places(t, who, s):
+        o = "so" + who
+        scan(R(o, 0, 256 * s), R("h%s%d" % (who, t)), R("u%s%d" % (who, t)), A.min, A.max)
+        ts(R("l" + who), R(o, s - 1, 256 * s, s), MAGIC, MAGIC - MID, A.add, A.subtract)
+
+    def gather_y(q, wid):
+        act(R("yv", 1024 * q, 1024 * q + 1024), X(R("bk", 0, wid), R("ly", 64 * q, 64 * q + 64)), F.Copy)
+
+    def first(q, wid):
+        tt(R("fv", 1024 * q, 1024 * q + 1024), X(R("bk", 0, wid), R("lx", 64 * q, 64 * q + 64)), R("yv", 1024 * q, 1024 * q + 1024),
+           (A.min, A.max, None, A.add)[q])
+
+    def third(q, wid):
+        tt(R("cand", 1024 * q, 1024 * q + 1024), X(R("bk", 0, wid), R("lz", 64 * q, 64 * q + 64)), R("fv", 1024 * q, 1024 * q + 1024), A.min)
+
+    def sums(q):
+        o = ((0, 64 * q), (0, 128 + 64 * q)) if q < 2 else ((1, 64 * q - 128), (6, 64 * q))
+        for w, (k, c) in zip(("onx", "kwx"), o):
+            for x in range(16):
+                mm(P(k, c, c + 64), R(w, 128 * x, 128 * x + 128), R("cand", 1024 * q + x, 1024 * q + 1024, 16), x == 0, x == 15)
+
+    owners = [(rank + 1 + i) % N for i in range(N)]
+
+    def classify(k, c, n, cs, k2, ck):
+        act(R("ab", c, c + n), P(k, cs, cs + n), F.Abs, bias=R("nmid"))
+        act(R("dead", c, c + n), R("ab", c, c + n), F.Relu, scale=R("qd"), bias=R("nhl"))
+        tt(R("zt", c, c + n), R("dead", c, c + n), P(k2, ck, ck + n), A.add)
+        ts(R("z2", c, c + n), R("zt", c, c + n), 2 ** 31 - DEAD + 3, None, A.bitwise_and)
+        cp(R("zb", c, c + n), R("z2", c, c + n))
+        for i, p in enumerate(owners):
+            ts(R("ind", 256 * i + c, 256 * i + c + n), R("zb", c, c + n), float(p), None, A.is_equal)
+
+    def build(t, wid, later, last):
+        for q in (0, 1, 2):
+            gather_y(q, wid)
+        act(R("xv"), X(R("bk", 0, wid), R("lx", 128, 192)), F.Copy)
+        first(0, wid)
+        gather_y(3, wid)
+        third(0, wid)
+        sums(0)
+        for h in range(2):
+            mm(P(2 + h, 0, 512), R("idp"), R("xv", 512 * h, 512 * h + 512), True, False)
+            mm(P(2 + h, 0, 512), R("idm"), R("yv", 2048 + 512 * h, 2560 + 512 * h), False, True)
+            act(R("fv", 2048 + 512 * h, 2560 + 512 * h), P(2 + h, 0, 512), F.Abs)
+        later()
+        first(1, wid)
+        third(1, wid)
+        sums(1)
+        first(3, wid)
+        third(2, wid)
+        sums(2)
+        third(3, wid)
+        last()
+        sums(3)
+        classify(0, 0, 128, 0, 0, 128)
+        classify(1, 128, 128, 0, 6, 128)
+
+    def send(t, gap1, gap2, gap3):
+        win, wib, arr, snd = "win%d" % t, "wib%d" % t, "arr%d" % t, "snd%d" % t
+        listify(P(4, 0, 64), "onx", "ind", 1024, True, True)
+        gap1()
+        cp(R("clb"), P(4, 0, 64))
+        scan(R("csb"), R("rst"), R("clb"), A.mult, A.add)
+        ts(R("e0"), R("clb"), 0.0, None, A.is_equal)
+        mm(P(5, 0, 64), R("blk"), R("p6"), True, False)
+        mm(P(5, 0, 64), R("neg"), R("clb"), False, False)
+        mm(P(5, 0, 64), R("blk"), R("csb"), False, False)
+        mm(P(5, 0, 64), R("idn"), R("e0"), False, True)
+        tt(R("iv"), P(5, 0, 64), R("cap"), A.is_ge)
+        ts(P(7, 128, 192), P(5, 0, 64), 191.0, None, A.min)
+        tt(R("t1"), R("iv"), P(7, 64, 128), A.mult)
+        tt(R("t3"), R("t1"), P(7, 128, 192), A.max)
+        cp(R("off"), R("t3"))
+        for h in range(2):
+            mm(P(2 + h, 0, 512), R("tri"), R("ind", 512 * h, 512 * h + 512), True, True)
+        scatter(R(win), R("off", 0, 32), R("vd"))
+        act(X(R(wib), R("off", 32, 64)), R("vdb"), F.Silu)
+        for i in range(4):
+            act(R("pref", PAIR * i + 1, PAIR * i + 257), P(2 + i // 2, 256 * (i % 2), 256 * (i % 2) + 256), F.Copy)
+        for i, w in enumerate((win, wib)):
+            ts(R("ns", 192 * i, 192 * i + 192), R(w, 0, 192), 0.0, None, A.is_equal)
+            scan(R("c1", 192 * i, 192 * i + 192), R("ns", 192 * i, 192 * i + 192), R(w, 0, 192), A.mult, A.add)
+        mm(P(5, 64, 88), R("blk"), R("p272"), True, False)
+        listify(P(5, 64, 88), "onx", "c1", 384, False, True)
+        scan(R("cnt"), R("ns"), R("one"), A.mult, A.add)
+        gap2()
+        ts(R("po"), P(5, 64, 88), 1.0 / (16 * UNIT), None, A.mult)
+        mm(P(6, 0, 24), R("blk"), R("mone"), True, False)
+        listify(P(6, 0, 24), "onx", "c1", 384, False, False)
+        tt(R("ll"), X(R("pref"), R("po")), R("cnt"), A.is_lt)
+        gap3()
+        listify(P(6, 0, 24), "lwx", "ll", 384, False, True)
+        ts(R("jl"), P(6, 0, 24), 1.0 / UNIT, float(J), A.mult, A.min)
+        cp(R(snd, 0, 192), X(R("cand"), R("jl", 0, 12)))
+        act(R(snd, 192, 288), X(R("cand"), R("jl", 12, 18)), F.Copy)
+        mine = plan(core, cores, topo)
+        src = [R(snd, CAP * i, CAP * i + CAP) for i in range(N - 1)]
+        prepare("g", [], [x for s in src for x in s[1]])
+        tr = []
+        for i in range(N - 1):
+            d = cores[owners[i]]
+            rid, pid = topo.addr(d, core)
+            tr.append(RemoteDMATransfer(dst_ids=[DstId(rid=rid, pnc=pid)], dma_engine_mask=sum(1 << e for e in mine[d]),
+                                        remote_sem=T.sem["arrv%d" % t], src=src[i][0], dst=T[arr][:, CAP * rank:CAP * rank + CAP]))
+        g.remote_dma_fused(tr, local_sem=T.sem["snt%d" % t])
+        act(R(arr, CAP * rank, CAP * rank + CAP), X(R("cand"), R("jl", 18, 24)), F.Copy)
+        total = sum(len(plan(c, cores, topo)[core]) for c in cores if c != core)
+        order[0] += 1
+        tok = {"n": order[0], "sem": "arrv%d" % t, "val": total, "q": "r", "snap": {}}
+        for q in range(N):
+            if q != rank:
+                wrote.setdefault(arr, []).append((range(CAP * q, CAP * q + CAP), tok))
+        return sum(len(e) for e in mine.values()), total
+
+    def keep(t, base):
+        arr = "arr%d" % t
+        mm(P(2, 0, M), R("kblk"), R(arr), True, True)
+        listify(P(3, 0, 24), "kwx", arr, M, True, True)
+        cp(R("r32"), P(2, 0, M))
+        ts(R("r33"), R("r32"), INV + 16383, None, A.bitwise_and)
+        cp(R("ki"), P(3, 0, 24))
+        cp(R("r16"), R("r33"))
+        ts(R("kb"), R("ki"), INV + 16383, None, A.bitwise_and)
+        cp(R("kf"), R("kb"))
+        mm(P(0, 0, 16), R("blk"), R("z16"), True, True)
+        for q in range(24):
+            ts(R("eq", 400 * q, M * q + M), R("r16", 16 * q, M), R("kf", q, q + 1), None, A.is_equal)
+            if q == 0:
+                ts(R("kb2"), R("kb"), 2, None, A.arith_shift_right)
+            if q == 1:
+                ts(R("bo"), R("kb2"), J, None, A.min)
+            if q < 23:
+                mm(P(0, 16 * q + 16, M), R("blk"), R("eq", 400 * q + 16, M * q + M), q == 0, q == 22)
+        listify(P(1, 0, 24), "tx", "eq", 24 * M, True, False, 400)
+        cp(R("us"), X(R("tbl", 0, J + 16), R("bo")))
+        tt(R("dm"), R("us"), P(0, 0, M), A.add)
+        listify(P(1, 0, 24), "onx", "dm", M, False, True)
+        ts(R("kp"), P(1, 0, 24), 0.0, None, A.is_equal)
+        scan(R("ks"), R("one", 0, 24), R("kp"), A.mult, A.add)
+        ts(R("nk"), P(1, 0, 24), 0.0, None, A.is_gt)
+        if t == 0:
+            mm(P(5, 100, 101), R("blk"), R("ks", 23, 24), True, True)
+        mm(P(4, 64, 88), R("neg"), R("kp"), True, False)
+        mm(P(4, 64, 88), R("blk"), R("ks"), False, True)
+        if t == 0:
+            ts(R("wx"), P(5, 100, 101), R("nq", 0, 1), HALF, A.mult, A.add)
+            cp(R("n4"), P(5, 100, 101))
+            ts(R("w0"), R("wx"), MAGIC, MAGIC, A.add, A.subtract)
+            ts(R("n4q"), R("n4"), 1.0 / 4096, None, A.mult)
+            ts(R("scy1"), R("w0"), -8192.0, R("k1"), A.mult, A.subtract)
+            ts(R("scx1"), R("w0"), 8192.0, R("k1"), A.mult, A.add)
+        tt(R("tn"), R("nk"), R("tk"), A.mult)
+        tt(R("om"), R("tn"), P(4, 64, 88), A.max)
+        if base is None:
+            cp(R("mo"), R("om"))
+        else:
+            ts(R("mo"), R("om"), base, None, A.add)
+
+    def append(t):
+        scatter(R("bk", B, B + 4 * M), R("mo"), R("arr%d" % t))
+
+    for i in range(1, 4):
+        hmask(0, "y", i, 4)
+    for i in range(1, 4):
+        hmask(0, "x", i, 4)
+    cp(R("laf", 0, 256), R("la", 0, 256))
+    for k in range(4):
+        affine(0, "x", k, 4)
+    for k in range(4):
+        ts(R("uy0", 3 - k, 1024, 4), R("lb", 0, 256), R("nq", k, k + 1), R("ub", k, k + 1), A.mult, A.add)
+    places(0, "y", 4)
+    places(0, "x", 4)
+    ts(R("zf"), R("lc", 0, 256), B / 4096.0, BIAS, A.mult, A.add)
+    ts(R("lz"), R("zf"), MAGIC, MAGIC - MID, A.add, A.subtract)
+    iota(R("mob"), [[0, 128]], -1)
+    iota(R("kib"), [[0, 128]], 1024)
+    sel(R("idp"), R("ob"), [[-1, 128]], A.is_equal, 0, 1)
+    sel(R("idm"), R("mob"), [[-1, 128]], A.is_equal, 0, 1)
+    sel(R("nb"), R("mob"), [[-16, 8], [0, 16]], A.is_ge, 0, 1)
+    sel(R("nblk"), R("nb"), [[16, 8], [0, 16]], A.is_ge, 15, -1)
+    sel(R("neg"), R("nblk"), [[-1, 128]], A.is_ge, 0, 1)
+    sel(R("tri"), R("blk"), [[1, 128]], A.is_ge, 0, -1)
+    sel(R("idn"), R("kib"), [[-1, 128]], A.is_equal, 0, 1)
+    iota(R("cand", J, J + 16), [[0, 16]], -1)
+    iota(R("trx0"), [[0, 2], [16, 32]], 192)
+    iota(R("rst"), [[0, 64]], 1)
+    iota(R("cap"), [[0, 2], [CAP, 2], [0, 16]], CAP)
+    iota(R("p6"), [[0, 2], [6, 2], [0, 16]], 0)
+    iota(R("rst", 0, 64, 16), [[0, 4]], 0)
+    for w in ("win0", "wib0"):
+        iota(R(w, 0, 192), [[0, 192]], 0)
+    iota(R("vdb"), [[0, 2], [UNIT, 256]], UNIT)
+    iota(R("vd"), [[0, 2], [UNIT, 256]], UNIT)
+    for w in ("win0", "wib0"):
+        iota(R(w, 0, 192, CAP), [[0, 2]], -UNIT)
+    iota(R("pref"), [[0, 4 * PAIR]], 0)
+    iota(R("p272"), [[UNIT * PAIR, 4], [0, 6]], 0)
+    iota(R("one"), [[0, 384]], 1)
+    iota(R("mone"), [[0, 24]], -UNIT)
+    iota(R("tk0"), [[16, 24]], 2 * M)
+    iota(R("tb0"), [[16, 24]], J + 16)
+    sel(R("stri"), R("blk"), [[1, 128]], A.is_ge, -1, -1)
+    iota(R("z16"), [[0, 16]], 0)
+    iota(R("tx"), [[0, 2048]], 0)
+
+    def limits():
+        ts(R("nmid"), R("sc", 4, 5), R("sc", 5, 6), -0.5, A.add, A.mult)
+        ts(R("nhl"), R("sc", 5, 6), R("sc", 4, 5), -0.5 * DEAD, A.subtract, A.mult)
+        fill(R("qd"), float(DEAD))
+
+    build(0, B, lambda: act(R("lwx"), R("onx"), F.Silu, scale=R("wl")), limits)
+
+    def gap0a():
+        ts(P(7, 64, 128), R("trx0"), R("rf"), None, A.add)
+        ts(R("tk"), R("tk0"), R("rf"), None, A.add)
+        ts(R("kblk"), R("blk"), R("wk"), None, A.mult)
+        cp(R("lbf", 256, 512), R("lb", 256, 512))
+
+    def gap0b():
+        fill(R("tbl", J, J + 16), 1)
+        for k in range(4):
+            affine(1, "y", k, 5)
+
+    def gap0c():
+        cp(R("laf", 256, 512), R("la", 256, 512))
+        cp(R("lcf", 256, 512), R("lc", 256, 512))
+
+    sent0, got0 = send(0, gap0a, gap0b, gap0c)
+
+    for h in ("hy1", "hx1"):
+        iota(R(h, 0, 1280, 5), [[0, 256]], -4096)
+    iota(R("bk", B, B + 4 * M), [[0, 4 * M]], 0)
+    for k in range(4):
+        affine(1, "x", k, 5)
+    fill(R("q1"), 1.0 / 4096)
+    fill(R("b75"), B / 4096.0)
+    fill(R("bia"), BIAS)
+    fill(R("b4"), B + BIAS)
+    pairs(2, ((1, 3), (2, 2)))
+    ts(R("w", 2, 4), R("wq", 2, 4), MAGIC, MAGIC, A.add, A.subtract)
+    spread("tx", "stri")
+    for i in range(2):
+        for w in ("win1", "wib1"):
+            iota(R(w, 0, 192, CAP if i else 1), [[0, 2 if i else 192]], -UNIT * i)
+    ts(R("wb"), R("w", 2, 3), 2.0, R("w", 3, 4), A.mult, A.add)
+    ts(R("by1", 1, 2), R("w", 3, 4), -8388608.0, -2048.0, A.mult, A.add)
+    ts(R("by1", 2, 3), R("w", 3, 4), 8388608.0, -2048.0, A.mult, A.add)
+    ts(R("k1"), R("wb"), 4096.0, None, A.mult)
+    ts(R("by1", 0, 1), R("wb"), -8388608.0, -2048.0, A.mult, A.add)
+    ts(R("by1", 3, 4), R("wb"), 8388608.0, -2048.0, A.mult, A.add)
+    ts(R("bx1"), R("by1"), -1.0, None, A.mult)
+
+    keep(0, None)
+
+    for i in range(1, 5):
+        hmask(1, "y", i, 5)
+    act(R("uy1", 0, 1280, 5), R("lbf", 256, 512), F.Identity, scale=R("n4q"), bias=R("b4"))
+    act(R("ux1", 0, 1280, 5), R("laf", 256, 512), F.Identity, scale=R("n4q"), bias=R("b4"))
+    for i in range(1, 5):
+        hmask(1, "x", i, 5)
+    act(R("tq"), R("n4"), F.Identity, scale=R("q1"), bias=R("b75"))
+    act(R("zf"), R("lcf", 256, 512), F.Identity, scale=R("tq"), bias=R("bia"))
+    append(0)
+    places(1, "y", 5)
+    places(1, "x", 5)
+    ts(R("lz"), R("zf"), MAGIC, MAGIC - MID, A.add, A.subtract)
+    build(1, B + M, lambda: None, lambda: None)
+
+    def gap1a():
+        cp(R("ud"), R("one"))
+        ts(R("tb"), R("tb0"), R("rf"), None, A.add)
+
+    def gap1b():
+        ts(R("bm"), R("kb2"), float(J), None, A.min)
+        tt(R("tn2"), R("nk"), R("tb"), A.mult)
+        tt(R("om2"), R("tn2"), R("bm"), A.max)
+        cp(R("mo2"), R("om2"))
+
+    sent1, got1 = send(1, gap1a, gap1b, lambda: None)
+    scatter(R("tbl"), R("mo2"), R("ud"))
+
+    keep(1, R("n4"))
+    append(1)
+    dma("y", "d_y", ext(T.y[:, :]), R("bk", B, B + 2 * M))
+
+    g.wait_ge(T.sem.snt0, sent0)
+    g.wait_ge(T.sem.snt1, sent1)
+    g.wait_ge(T.sem.arrv0, got0)
+    g.wait_ge(T.sem.arrv1, got1)
+    for d in DMAS:
+        g.wait_ge(T.sem[d], 256 if d == "d_used" else 16)
+    for q in qsem:
+        g.wait_ge(T.sem[qsem[q]], count[q])

@@ -8,36 +8,40 @@ MAGIC = 12582912.0
 HALF = -2047.5 / 4096
 MID = 1728
 BIAS = HALF - MID
-DEAD = 524288
-PAIR = 272
 INV = 1048576
-UNIT = 32
+OWN = 4128
+TRASH = 2 * OWN
+WIN = TRASH + 544
+BIG = 16384.0
+LIFT = 32
+STEP = 1.0 / 32
 
 SCRATCH = {}
 ALIAS, COLS, SIZE = {}, {}, {F32: 0, BF: 0, I32: 0}
 for _n, _c, _d in [
     ("nl", 8, I32), ("nf", 8, F32), ("sc", 8, F32), ("nq", 8, F32), ("cs4", 8, F32), ("ub", 8, F32), ("pr", 4, F32), ("wq", 4, F32), ("w", 4, F32),
     ("one8", 128, F32), ("b8a", 128, F32), ("b8", 128, F32), ("on4", 8, F32),
-    ("pid", 1, I32), ("ri", 1, I32), ("rf", 1, F32), ("wk", 1, F32), ("wl0", 1, F32), ("wl", 1, F32),
-    ("jc0", 256, F32), ("jc", 256, F32), ("trx0", 64, F32), ("tk0", 24, F32), ("tk", 24, F32), ("tb0", 24, F32), ("tb", 24, F32),
-    ("ob", 128, BF), ("ba", 128, BF), ("blk", 128, BF), ("nb", 128, BF), ("nblk", 128, BF), ("tri", 128, BF), ("neg", 128, BF), ("stri", 128, BF),
-    ("kib", 128, BF), ("idn", 128, BF), ("kblk", 128, BF), ("mob", 128, BF), ("idp", 128, BF), ("idm", 128, BF), ("z16", 16, BF),
-    ("onx", 2048, BF), ("kwx", 2048, BF), ("lwx", 2048, BF), ("tx", 2048, BF),
-    ("vd", 512, BF), ("vdb", 512, F32), ("rst", 64, BF), ("one", 384, BF), ("p6", 64, BF), ("cap", 64, F32), ("p272", 24, BF), ("mone", 24, BF), ("ud", 384, I32),
-    ("nmid", 1, F32), ("nhl", 1, F32), ("qd", 1, F32), ("q1", 1, F32), ("b75", 1, F32), ("bia", 1, F32), ("b4", 1, F32),
+    ("pid", 1, I32), ("ri", 4, I32), ("rf", 4, F32), ("pf1", 1, F32), ("wk", 1, F32), ("w4", 1, F32), ("srow", 1, F32), ("krow", 1, F32), ("gp", 1, F32),
+    ("cv", 1, F32), ("b3", 1, F32), ("pm", 1, F32), ("lh", 8, F32), ("lo", 1, F32), ("hi", 1, F32), ("vb", 1, F32), ("bse", 1, F32), ("bmk", 2, F32),
+    ("jc0", 256, F32), ("jc", 256, F32), ("tk0", 24, F32), ("tk", 24, F32), ("tb0", 24, F32), ("tb", 24, F32),
+    ("i8", 8, F32), ("i68", 68, F32), ("n68", 68, F32), ("trs0", 68, F32), ("trs", 68, F32), ("ci", 144, F32), ("se0", M, F32), ("se1", M, BF),
+    ("ob", 128, BF), ("ba", 128, BF), ("blk", 128, BF), ("nb", 128, BF), ("nblk", 128, BF), ("trin", 128, BF), ("tri", 128, BF), ("neg", 128, BF), ("stri", 128, BF),
+    ("kblk", 128, BF), ("mob", 128, BF), ("idp", 128, BF), ("idm", 128, BF), ("z16", 16, BF), ("blk8", 8, BF), ("cb", 128, BF),
+    ("mx", 144, BF), ("wc", 144, BF), ("onx", 144, BF), ("kwx", 144, BF), ("tx", 2048, BF),
+    ("r1", 68, BF), ("r2", 68, BF), ("r3", 68, BF), ("ra0", 68, BF), ("rb0", 68, BF), ("btab", 68, BF), ("rst", 128, BF), ("ctab", 512, BF), ("selm", M, BF), ("stp", CAP, F32),
+    ("one", 384, BF), ("ud", 384, I32),
+    ("q1", 1, F32), ("b75", 1, F32), ("bia", 1, F32), ("b4", 1, F32),
     ("bx0", 4, F32), ("by0", 4, F32), ("bx1", 4, F32), ("by1", 4, F32), ("wb", 1, F32), ("k1", 1, F32),
     ("scx0", 1, F32), ("scy0", 1, F32), ("scx1", 1, F32), ("scy1", 1, F32),
     ("n4", 1, F32), ("n4q", 1, F32), ("tq", 1, F32), ("wx", 1, F32), ("w0", 1, F32),
     ("la", 512, I32), ("lb", 512, I32), ("lc", 512, I32), ("laf", 512, F32), ("lbf", 512, F32), ("lcf", 512, F32),
-    ("ux0", 1024, F32), ("uy0", 1024, F32), ("ux1", 1280, F32), ("uy1", 1280, F32),
-    ("hx0", 1024, BF), ("hy0", 1024, BF), ("hx1", 1280, BF), ("hy1", 1280, BF), ("sox", 1280, F32), ("soy", 1280, F32),
+    ("ux0", 512, F32), ("uy0", 512, F32), ("ux1", 768, F32), ("uy1", 768, F32),
+    ("hx0", 512, BF), ("hy0", 512, BF), ("hx1", 768, BF), ("hy1", 768, BF), ("sox", 768, F32), ("soy", 768, F32),
     ("zf", 256, F32), ("lx", 256, U16), ("ly", 256, U16), ("lz", 256, U16),
-    ("bk", B + 4 * M, BF), ("yv", J, BF), ("xv", 1024, BF), ("fv", J, BF), ("cand", J + 16, BF),
-    ("ab", 256, F32), ("dead", 256, F32), ("zt", 256, I32), ("z2", 256, I32), ("zb", 256, BF), ("ind", 1024, BF),
-    ("clb", 64, BF), ("csb", 64, BF), ("e0", 64, BF), ("iv", 64, F32), ("t1", 64, F32), ("t3", 64, F32), ("off", 64, U16),
-    ("win0", 704, BF), ("win1", 704, BF), ("wib0", 704, F32), ("wib1", 704, F32),
-    ("ns", 384, BF), ("c1", 384, BF), ("cnt", 384, BF), ("po", 24, U16), ("pref", 4 * PAIR, BF),
-    ("ll", 384, BF), ("jl", 24, U16), ("snd0", 288, BF), ("snd1", 288, BF), ("arr0", M, BF), ("arr1", M, BF),
+    ("bk", B + 4 * M, BF), ("sv", 3072, BF), ("xv", 1024, BF), ("xa", 1024, BF), ("fv", J, BF), ("cand", J + 16, BF),
+    ("cl", 128, I32), ("dd", 128, BF), ("ind", 1024, BF), ("t1", 128, BF), ("t2", 128, BF), ("t3", 128, BF), ("of", 68, F32), ("off", 68, U16),
+    ("vin0", 528, F32), ("vin1", 528, F32), ("win0", WIN, F32), ("win1", WIN, F32), ("sx", M, F32), ("fr", M, BF), ("sj", M, F32),
+    ("jl", 24, U16), ("snd0", 288, BF), ("snd1", 288, BF), ("arr0", M, BF), ("arr1", M, BF),
     ("ki", 24, I32), ("kb", 24, I32), ("kf", 24, F32), ("kb2", 24, I32), ("bm", 24, F32), ("bo", 24, U16), ("r32", M, I32), ("r33", M, I32), ("r16", M, U16),
     ("tbl", J + 16 + M, I32), ("us", M, BF), ("eq", 24 * M, BF), ("dm", M, BF),
     ("nk", 24, BF), ("kp", 24, BF), ("ks", 24, BF), ("tn", 24, F32), ("om", 24, F32), ("mo", 24, U16), ("tn2", 24, F32), ("om2", 24, F32), ("mo2", 24, U16),
@@ -54,7 +58,7 @@ SCRATCH["pi"] = ("sbuf", [128, SIZE[I32]], I32)
 for _n in range(8):
     SCRATCH["ps%d" % _n] = ("psum", [128, 512], F32)
 
-DMAS = ["d_ncl", "d_lim", "d_la0", "d_lb0", "d_lc0", "d_la1", "d_lb1", "d_lc1", "d_bk", "d_used", "d_y"]
+DMAS = ["d_ncl", "d_lim", "d_la0", "d_lb0", "d_lc0", "d_la1", "d_lb1", "d_lc1", "d_bk", "d_used", "d_y", "d_add0", "d_add1"]
 SEMAPHORES = ["cv", "cs", "ct", "cg", "arrv0", "arrv1", "snt0", "snt1"] + DMAS
 
 
@@ -212,10 +216,11 @@ def rank_program(g, core, T, topo):
 
     def listify(o, wname, src, ncols, start, stop, st=16):
         for x in range(16):
-            mm(o, R(wname, 128 * x, 128 * x + 128), R(src, x, ncols, st), start and x == 0, stop and x == 15)
+            w = R(wname, 128 * x, 128 * x + 128) if wname == "tx" else R(wname, 16 - x, 144 - x)
+            mm(o, w, R(src, x, ncols, st), start and x == 0, stop and x == 15)
 
-    def P(k, a, b):
-        return R("ps%d" % k, a, b)
+    def P(k, a, b, st=1, rows=None):
+        return R("ps%d" % k, a, b, st, rows)
 
     def spread(name, src, xs=range(16)):
         for x in xs:
@@ -224,8 +229,8 @@ def rank_program(g, core, T, topo):
     first8 = slice(0, 8)
     dma("y", "d_ncl", R("nl", 0, 4, rows=first8), ext(T.ncl[:, :]))
     dma("s", "d_lim", R("nl", 4, 6, rows=first8), ext(T.lim[:, :]))
-    dma("y", "d_lb0", R("lb", 0, 256), ext(T.rb[:, 0:256]))
-    dma("s", "d_la0", R("la", 0, 256), ext(T.ra[:, 0:256]))
+    dma("y", "d_la0", R("la", 0, 256), ext(T.ra[:, 0:256]))
+    dma("s", "d_lb0", R("lb", 0, 256), ext(T.rb[:, 0:256]))
     dma("y", "d_lc0", R("lc", 0, 256), ext(T.rc[:, 0:256]))
     dma("y", "d_bk", R("bk", 0, B), ext(T.bank[:, :]))
     dma("y", "d_lb1", R("lb", 256, 512), ext(T.rb[:, 256:512]))
@@ -234,28 +239,41 @@ def rank_program(g, core, T, topo):
     for r in range(16):
         dma("y", "d_used", R("tbl", 0, J, rows=slice(r, 128, 16)), ext(T.used[:, :]), 256)
 
-    fill(R("ob"), 1.0)
+    def clear(o):
+        return R("win%d" % (o // 2), OWN * (o % 2), OWN * (o % 2) + CAP)
+
     fill(R("one8"), 1.0)
+    fill(R("q1"), 0.0)
+    fill(R("ob"), 1.0)
+    for o in (2, 3):
+        act(clear(o), R("one8", 0, CAP), F.Silu, scale=R("q1"))
     iota(R("pid"), [[0, 1]], 0, 1)
-    ts(R("ri"), R("pid"), 15, None, A.bitwise_and)
-    cp(R("rf"), R("ri"))
-    fill(R("onx"), 0.0)
-    ts(R("wk"), R("rf"), 14.0, 9.0, A.mult, A.add)
-    ts(R("wl0"), R("rf"), 15.0, 8191.0 * UNIT, A.is_equal, A.mult)
-    sel(R("ba"), R("ob"), [[-16, 8], [0, 16]], A.is_ge, 0, 1)
-    sel(R("blk"), R("ba"), [[16, 8], [0, 16]], A.is_ge, 15, -1)
     sel(R("b8a", rows=first8), R("one8", rows=first8), [[1, 128]], A.is_ge, 0, -16)
     sel(R("b8", rows=first8), R("b8a", rows=first8), [[-1, 128]], A.is_ge, 15, 16)
     iota(R("jc0"), [[16, 256]], -2048)
-    for h in ("hy0", "hx0"):
-        iota(R(h, 0, 1024, 4), [[0, 256]], -4096)
-    spread("onx", "blk", range(10))
+    sel(R("ba"), R("ob"), [[-16, 8], [0, 16]], A.is_ge, 0, 1)
+    sel(R("blk"), R("ba"), [[16, 8], [0, 16]], A.is_ge, 15, -1)
+    for i, bits in enumerate((15, 1, 8, 7)):
+        ts(R("ri", i, i + 1), R("pid"), bits, None, A.bitwise_and)
+    for h in ("hx0", "hy0"):
+        fill(R(h, 0, 512, 2), -4096.0)
+    cp(R("rf"), R("ri"))
+    cp(R("pf1"), R("pid"))
+    row = R("rf", 0, 1)
+    for w in ("mx", "onx", "kwx"):
+        fill(R(w), 0.0)
+    ts(R("wk"), row, 14.0, 9.0, A.mult, A.add)
+    ts(R("w4"), R("rf", 1, 2), 0.5, 0.25, A.mult, A.add)
+    ts(R("srow"), R("rf", 2, 3), 0.0, None, A.is_equal)
+    ts(R("krow"), R("rf", 2, 3), 0.0, None, A.not_equal)
+    ts(R("cv"), R("pf1"), R("rf", 2, 3), 8.0, A.subtract, A.add)
+    fill(R("on4"), 1.0)
+    fill(R("by0", 1, 2), -2048.0)
+    fill(R("ub", 0, 1), BIAS)
 
     cp(R("nf", 0, 6, rows=first8), R("nl", 0, 6, rows=first8))
     mm(P(7, 0, 6), R("b8", rows=first8), R("nf", 0, 6, rows=first8), True, True)
-    for x in range(10, 16):
-        cp(R("onx", 129 * x, 128 * x + 128, 16), R("blk", x, 128, 16))
-    act(R("kwx"), R("onx"), F.Copy, scale=R("wk"))
+    ts(R("jc"), R("jc0"), row, None, A.add)
     cp(R("sc", 0, 6), P(7, 0, 6))
 
     def pairs(k, ab):
@@ -264,125 +282,172 @@ def rank_program(g, core, T, topo):
         ts(R("wq", k, k + 2), R("pr", k, k + 2), 1.0 / 4096, HALF, A.mult, A.add)
 
     pairs(0, ((0, 3), (1, 2)))
-    ts(R("jc"), R("jc0"), R("rf"), None, A.add)
-    ts(R("w", 0, 2), R("wq", 0, 2), MAGIC, MAGIC, A.add, A.subtract)
-    fill(R("by0", 1, 2), -2048.0)
-    fill(R("on4"), 1.0)
-    ts(R("by0", 0, 1), R("w", 1, 2), -16777216.0, -2048.0, A.mult, A.add)
-    ts(R("by0", 2, 3), R("w", 1, 2), 16777216.0, -2048.0, A.mult, A.add)
-    ts(R("scy0"), R("w", 0, 1), R("w", 1, 2), -8192.0, A.add, A.mult)
     ts(R("nq", 0, 4), R("sc", 0, 4), 1.0 / 4096, None, A.mult)
     scan(R("cs4", 0, 4), R("on4", 0, 4), R("sc", 0, 4), A.mult, A.add)
-    fill(R("ub", 0, 1), BIAS)
-    ts(R("scx0"), R("w", 0, 1), R("w", 1, 2), 8192.0, A.add, A.mult)
+    ts(R("w", 0, 2), R("wq", 0, 2), MAGIC, MAGIC, A.add, A.subtract)
     ts(R("ub", 1, 4), R("cs4", 0, 3), BIAS, None, A.add)
-    ts(R("wl"), R("wl0"), float(UNIT), None, A.add)
-    ts(R("bx0", 0, 3), R("by0", 0, 3), -1.0, None, A.mult)
+    ts(R("bx0", 0, 1), R("w", 1, 2), 16777216.0, 2048.0, A.mult, A.add)
+    ts(R("scx0"), R("w", 0, 1), R("w", 1, 2), 8192.0, A.add, A.mult)
+    ts(R("by0", 2, 3), R("w", 1, 2), 16777216.0, -2048.0, A.mult, A.add)
+    ts(R("scy0"), R("w", 0, 1), R("w", 1, 2), -8192.0, A.add, A.mult)
+    ts(R("by0", 0, 1), R("w", 1, 2), -16777216.0, -2048.0, A.mult, A.add)
+    ts(R("bx0", 2, 3), R("w", 1, 2), -16777216.0, 2048.0, A.mult, A.add)
 
-    def affine(t, who, k, s):
-        i = s - 1 - k
-        act(R("u%s%d" % (who, t), i, 256 * s, s), R("l%sf" % ("a" if who == "x" else "b"), 256 * t, 256 * t + 256), F.Identity,
-            scale=R("nq", k, k + 1), bias=R("ub", k, k + 1))
+    def step(t, who, half, i):
+        m = 2 + t
+        k = 2 * half + m - 1 - i if who == "x" else 3 + t - 2 * half - i
+        return k, (k if who == "x" else 2 * half + i - 1), (128 * m * half + i, 128 * m * (half + 1), m)
 
-    def hmask(t, who, i, s):
-        k = s - 1 - i if who == "x" else i - 1
-        act(R("h%s%d" % (who, t), i, 256 * s, s), R("jc"), F.Identity, scale=R("sc%s%d" % (who, t)), bias=R("b%s%d" % (who, t), k, k + 1))
+    def affine(t, who, half, i, q="s"):
+        k, _, cols = step(t, who, half, i)
+        sc_, bi = (R("nq", k, k + 1), R("ub", k, k + 1)) if k < 4 else (R("n4q"), R("b4"))
+        name, a = "l" + ("a" if who == "x" else "b"), 256 * t + 128 * half
+        if q == "s":
+            act(R("u%s%d" % (who, t), *cols), R(name + "f", a, a + 128), F.Identity, scale=sc_, bias=bi)
+        else:
+            ts(R("u%s%d" % (who, t), *cols), R(name, a, a + 128), sc_, bi, A.mult, A.add)
 
-    def places(t, who, s):
-        o = "so" + who
-        scan(R(o, 0, 256 * s), R("h%s%d" % (who, t)), R("u%s%d" % (who, t)), A.min, A.max)
-        ts(R("l" + who), R(o, s - 1, 256 * s, s), MAGIC, MAGIC - MID, A.add, A.subtract)
+    def hmask(t, who, half):
+        for i in range(1, 2 + t):
+            _, k, cols = step(t, who, half, i)
+            act(R("h%s%d" % (who, t), *cols), R("jc", 128 * half, 128 * half + 128), F.Identity, scale=R("sc%s%d" % (who, t)),
+                bias=R("b%s%d" % (who, t), k, k + 1))
 
-    def gather_y(q, wid):
-        act(R("yv", 1024 * q, 1024 * q + 1024), X(R("bk", 0, wid), R("ly", 64 * q, 64 * q + 64)), F.Copy)
+    def places(t, who, half):
+        m = 2 + t
+        a, b = 128 * m * half, 128 * m * (half + 1)
+        scan(R("so" + who, a, b), R("h%s%d" % (who, t), a, b), R("u%s%d" % (who, t), a, b), A.min, A.max)
+        ts(R("l" + who, 128 * half, 128 * half + 128), R("so" + who, a + m - 1, b, m), MAGIC, MAGIC - MID, A.add, A.subtract)
+
+    def quarter(name, q):
+        return R(name, 1024 * q, 1024 * q + 1024)
+
+    def col(who, q, wid):
+        return X(R("bk", 0, wid), R("l" + who, 64 * q, 64 * q + 64))
 
     def first(q, wid):
-        tt(R("fv", 1024 * q, 1024 * q + 1024), X(R("bk", 0, wid), R("lx", 64 * q, 64 * q + 64)), R("yv", 1024 * q, 1024 * q + 1024),
-           (A.min, A.max, None, A.add)[q])
+        tt(quarter("fv", q), col("y", q, wid), quarter("sv", q), (A.min, A.max)[q])
 
-    def third(q, wid):
-        tt(R("cand", 1024 * q, 1024 * q + 1024), X(R("bk", 0, wid), R("lz", 64 * q, 64 * q + 64)), R("fv", 1024 * q, 1024 * q + 1024), A.min)
+    def third(q, wid, a=0, b=64):
+        c, d = 1024 * q + 16 * a, 1024 * q + 16 * b
+        tt(R("cand", c, d), X(R("bk", 0, wid), R("lz", 64 * q + a, 64 * q + b)), R("fv", c, d), A.min)
 
-    def sums(q):
-        o = ((0, 64 * q), (0, 128 + 64 * q)) if q < 2 else ((1, 64 * q - 128), (6, 64 * q))
-        for w, (k, c) in zip(("onx", "kwx"), o):
-            for x in range(16):
-                mm(P(k, c, c + 64), R(w, 128 * x, 128 * x + 128), R("cand", 1024 * q + x, 1024 * q + 1024, 16), x == 0, x == 15)
+    def sums(q, k):
+        mm(P(k, 0, 128), R("idp"), R("cb"), True, False)
+        for x in range(16):
+            c = 64 * (x // 8)
+            mm(P(k, c, c + 64), R("mx", 8 - x % 8, 136 - x % 8), R("cand", 1024 * q + x, 1024 * q + 1024, 16), False, x == 15)
 
     owners = [(rank + 1 + i) % N for i in range(N)]
+    low64 = slice(0, 64)
 
-    def classify(k, c, n, cs, k2, ck):
-        act(R("ab", c, c + n), P(k, cs, cs + n), F.Abs, bias=R("nmid"))
-        act(R("dead", c, c + n), R("ab", c, c + n), F.Relu, scale=R("qd"), bias=R("nhl"))
-        tt(R("zt", c, c + n), R("dead", c, c + n), P(k2, ck, ck + n), A.add)
-        ts(R("z2", c, c + n), R("zt", c, c + n), 2 ** 31 - DEAD + 3, None, A.bitwise_and)
-        cp(R("zb", c, c + n), R("z2", c, c + n))
+    def judge(k):
+        ts(R("cl"), P(k, 0, 128), R("lo"), R("hi"), A.max, A.min)
+        tt(R("dd"), P(k, 0, 128), R("cl"), A.subtract)
+        mm(P(4, 0, 64), R("wc", 8, 136), R("dd", 0, 64), True, False)
+        mm(P(4, 0, 64), R("wc", 0, 128), R("dd", 64, 128), False, True)
+
+    def count_cols(q):
+        for o in range(N):
+            for s in (2 * q, 2 * q + 1):
+                mm(P(5, 8 * (o % 2) + s, 128, 16, slice(32 * (o // 2), 32 * (o // 2) + 32)), R("ind", 256 * o + 32 * s, 256 * o + 32 * s + 32),
+                   R("blk", 0, 128, 16), True, True)
+
+    def prefix(q, w, last):
+        for o in (2 * w, 2 * w + 1):
+            for s in (2 * q, 2 * q + 1):
+                mm(P(6 + w, 8 * (o % 2) + s, 512, 16), R("trin"), R("ind", 256 * o + 32 * s, 256 * o + 32 * s + 32), False, last and o % 2 == 1 and s % 2 == 1)
+
+    def mark(q):
         for i, p in enumerate(owners):
-            ts(R("ind", 256 * i + c, 256 * i + c + n), R("zb", c, c + n), float(p), None, A.is_equal)
+            ts(R("ind", 256 * i + 64 * q, 256 * i + 64 * q + 64), P(4, 0, 64), p / 4 - 0.375, None, A.is_equal)
 
-    def build(t, wid, later, last):
-        for q in (0, 1, 2):
-            gather_y(q, wid)
-        act(R("xv"), X(R("bk", 0, wid), R("lx", 128, 192)), F.Copy)
+    def counts(q):
+        count_cols(q)
+        for w in range(2):
+            prefix(q, w, False)
+
+    def add(o, i, sem):
+        prepare("g", o[1], o[1] + i[1])
+        g.dma_start(o[0], i[0], accum_op=A.add).then_inc(T.sem[sem], 16)
+        record("g", o[1], i[1], sem, 16)
+
+    def build(t, wid, gap0, gap1, gap2):
+        act(quarter("sv", 1), col("x", 1, B), F.Copy)
         first(0, wid)
-        gather_y(3, wid)
+        act(quarter("fv", 3), col("y", 3, B), F.Copy)
+        gap0()
         third(0, wid)
-        sums(0)
+        sums(0, 0)
+        for w in range(2):
+            mm(P(6 + w, 0, 512), R("idp"), R("ctab"), True, False)
+        act(R("xa"), col("x", 3, wid), F.Copy)
+        add(quarter("fv", 3), R("xa"), "d_add%d" % t)
+        act(quarter("sv", 2), col("y", 2, B), F.Copy)
+        for h in range(2):
+            act(R("xv", 512 * h, 512 * h + 512), X(R("bk", 0, wid), R("lx", 128 + 32 * h, 160 + 32 * h)), F.Copy)
+        first(1, wid)
+        gap1()
+        judge(0)
+        third(1, wid)
+        sums(1, 1)
+        mark(0)
+        counts(0)
+        gap2()
+        judge(1)
+        third(3, wid)
         for h in range(2):
             mm(P(2 + h, 0, 512), R("idp"), R("xv", 512 * h, 512 * h + 512), True, False)
-            mm(P(2 + h, 0, 512), R("idm"), R("yv", 2048 + 512 * h, 2560 + 512 * h), False, True)
+            mm(P(2 + h, 0, 512), R("idm"), R("sv", 2048 + 512 * h, 2560 + 512 * h), False, True)
             act(R("fv", 2048 + 512 * h, 2560 + 512 * h), P(2 + h, 0, 512), F.Abs)
-        later()
-        first(1, wid)
-        third(1, wid)
-        sums(1)
-        first(3, wid)
-        third(2, wid)
-        sums(2)
-        third(3, wid)
-        last()
-        sums(3)
-        classify(0, 0, 128, 0, 0, 128)
-        classify(1, 128, 128, 0, 6, 128)
+        sums(3, 0)
+        mark(1)
+        third(2, wid, 0, 32)
+        counts(1)
+        judge(0)
+        third(2, wid, 32, 64)
+        sums(2, 1)
+        mark(3)
+        count_cols(3)
+        prefix(3, 0, False)
+        judge(1)
+        prefix(3, 1, False)
+        mark(2)
+        count_cols(2)
+        mm(P(2, 0, 68), R("idp"), R("btab"), True, False)
+        prefix(2, 0, True)
+        prefix(2, 1, True)
 
-    def send(t, gap1, gap2, gap3):
-        win, wib, arr, snd = "win%d" % t, "wib%d" % t, "arr%d" % t, "snd%d" % t
-        listify(P(4, 0, 64), "onx", "ind", 1024, True, True)
-        gap1()
-        cp(R("clb"), P(4, 0, 64))
-        scan(R("csb"), R("rst"), R("clb"), A.mult, A.add)
-        ts(R("e0"), R("clb"), 0.0, None, A.is_equal)
-        mm(P(5, 0, 64), R("blk"), R("p6"), True, False)
-        mm(P(5, 0, 64), R("neg"), R("clb"), False, False)
-        mm(P(5, 0, 64), R("blk"), R("csb"), False, False)
-        mm(P(5, 0, 64), R("idn"), R("e0"), False, True)
-        tt(R("iv"), P(5, 0, 64), R("cap"), A.is_ge)
-        ts(P(7, 128, 192), P(5, 0, 64), 191.0, None, A.min)
-        tt(R("t1"), R("iv"), P(7, 64, 128), A.mult)
-        tt(R("t3"), R("t1"), P(7, 128, 192), A.max)
-        cp(R("off"), R("t3"))
-        for h in range(2):
-            mm(P(2 + h, 0, 512), R("tri"), R("ind", 512 * h, 512 * h + 512), True, True)
-        scatter(R(win), R("off", 0, 32), R("vd"))
-        act(X(R(wib), R("off", 32, 64)), R("vdb"), F.Silu)
-        for i in range(4):
-            act(R("pref", PAIR * i + 1, PAIR * i + 257), P(2 + i // 2, 256 * (i % 2), 256 * (i % 2) + 256), F.Copy)
-        for i, w in enumerate((win, wib)):
-            ts(R("ns", 192 * i, 192 * i + 192), R(w, 0, 192), 0.0, None, A.is_equal)
-            scan(R("c1", 192 * i, 192 * i + 192), R("ns", 192 * i, 192 * i + 192), R(w, 0, 192), A.mult, A.add)
-        mm(P(5, 64, 88), R("blk"), R("p272"), True, False)
-        listify(P(5, 64, 88), "onx", "c1", 384, False, True)
-        scan(R("cnt"), R("ns"), R("one"), A.mult, A.add)
-        gap2()
-        ts(R("po"), P(5, 64, 88), 1.0 / (16 * UNIT), None, A.mult)
-        mm(P(6, 0, 24), R("blk"), R("mone"), True, False)
-        listify(P(6, 0, 24), "onx", "c1", 384, False, False)
-        tt(R("ll"), X(R("pref"), R("po")), R("cnt"), A.is_lt)
-        gap3()
-        listify(P(6, 0, 24), "lwx", "ll", 384, False, True)
-        ts(R("jl"), P(6, 0, 24), 1.0 / UNIT, float(J), A.mult, A.min)
-        cp(R(snd, 0, 192), X(R("cand"), R("jl", 0, 12)))
-        act(R(snd, 192, 288), X(R("cand"), R("jl", 12, 18)), F.Copy)
+    def send(t, gap1, gap2):
+        arr, snd = "arr%d" % t, "snd%d" % t
+        scan(R("t2", rows=low64), R("rst", rows=low64), P(5, 0, 128, rows=low64), A.mult, A.add)
+        cp(R("t1", rows=low64), P(5, 0, 128, rows=low64))
+        ts(R("t3", rows=low64), P(5, 0, 128, rows=low64), 0.0, None, A.is_equal)
+        for i in (2, 1, 3):
+            mm(P(2, 0, 68), R("t%d" % i, rows=low64), R("r%d" % i, rows=low64), False, i == 3)
+        for w in range(2):
+            act(R("vin%d" % w, 0, 512), P(6 + w, 0, 512), F.Identity, bias=R("vb"))
+        tt(R("of"), P(2, 0, 68), R("trs"), A.min)
+        cp(R("off"), R("of"))
+        scatter(R("win0"), R("off", 0, 33), R("vin0"))
+        act(X(R("win1"), R("off", 34, 67)), R("vin1"), F.Silu)
+
+        def slots(a, b, k):
+            for o in range(a, b):
+                scan(R("sx", CAP * o, CAP * o + CAP), R("stp"), R("win%d" % (o // 2), OWN * (o % 2), OWN * (o % 2) + CAP), A.add, A.max)
+            ts(R("fr", CAP * a, CAP * b), R("sx", CAP * a, CAP * b), MAGIC, MAGIC + LIFT, A.add, A.subtract)
+            mm(P(k, CAP * a, CAP * b), R("blk"), R("fr", CAP * a, CAP * b), True, True)
+
+        def pick(a, b, k):
+            scan(R("sj", CAP * a, CAP * b), R("selm", CAP * a, CAP * b), P(k, CAP * a, CAP * b), A.max, A.min)
+            ts(R("jl", 6 * a, 6 * b), R("sj", CAP * a + 15, CAP * b, 16), float(J), None, A.min)
+
+        slots(0, 2, 3)
+        slots(2, 3, 2)
+        pick(0, 2, 3)
+        act(R(snd, 0, 192), X(R("cand"), R("jl", 0, 12)), F.Copy)
+        pick(2, 3, 2)
+        cp(R(snd, 192, 288), X(R("cand"), R("jl", 12, 18)))
         mine = plan(core, cores, topo)
         src = [R(snd, CAP * i, CAP * i + CAP) for i in range(N - 1)]
         prepare("g", [], [x for s in src for x in s[1]])
@@ -393,6 +458,10 @@ def rank_program(g, core, T, topo):
             tr.append(RemoteDMATransfer(dst_ids=[DstId(rid=rid, pnc=pid)], dma_engine_mask=sum(1 << e for e in mine[d]),
                                         remote_sem=T.sem["arrv%d" % t], src=src[i][0], dst=T[arr][:, CAP * rank:CAP * rank + CAP]))
         g.remote_dma_fused(tr, local_sem=T.sem["snt%d" % t])
+        slots(3, 4, 3)
+        gap1()
+        pick(3, 4, 3)
+        gap2()
         act(R(arr, CAP * rank, CAP * rank + CAP), X(R("cand"), R("jl", 18, 24)), F.Copy)
         total = sum(len(plan(c, cores, topo)[core]) for c in cores if c != core)
         order[0] += 1
@@ -429,16 +498,16 @@ def rank_program(g, core, T, topo):
         scan(R("ks"), R("one", 0, 24), R("kp"), A.mult, A.add)
         ts(R("nk"), P(1, 0, 24), 0.0, None, A.is_gt)
         if t == 0:
-            mm(P(5, 100, 101), R("blk"), R("ks", 23, 24), True, True)
+            mm(P(5, 200, 201), R("blk"), R("ks", 23, 24), True, True)
         mm(P(4, 64, 88), R("neg"), R("kp"), True, False)
         mm(P(4, 64, 88), R("blk"), R("ks"), False, True)
         if t == 0:
-            ts(R("wx"), P(5, 100, 101), R("nq", 0, 1), HALF, A.mult, A.add)
-            cp(R("n4"), P(5, 100, 101))
+            ts(R("wx"), P(5, 200, 201), R("nq", 0, 1), HALF, A.mult, A.add)
+            cp(R("n4"), P(5, 200, 201))
             ts(R("w0"), R("wx"), MAGIC, MAGIC, A.add, A.subtract)
             ts(R("n4q"), R("n4"), 1.0 / 4096, None, A.mult)
-            ts(R("scy1"), R("w0"), -8192.0, R("k1"), A.mult, A.subtract)
             ts(R("scx1"), R("w0"), 8192.0, R("k1"), A.mult, A.add)
+            ts(R("scy1"), R("w0"), -8192.0, R("k1"), A.mult, A.subtract)
         tt(R("tn"), R("nk"), R("tk"), A.mult)
         tt(R("om"), R("tn"), P(4, 64, 88), A.max)
         if base is None:
@@ -449,89 +518,107 @@ def rank_program(g, core, T, topo):
     def append(t):
         scatter(R("bk", B, B + 4 * M), R("mo"), R("arr%d" % t))
 
-    for i in range(1, 4):
-        hmask(0, "y", i, 4)
-    for i in range(1, 4):
-        hmask(0, "x", i, 4)
-    cp(R("laf", 0, 256), R("la", 0, 256))
-    for k in range(4):
-        affine(0, "x", k, 4)
-    for k in range(4):
-        ts(R("uy0", 3 - k, 1024, 4), R("lb", 0, 256), R("nq", k, k + 1), R("ub", k, k + 1), A.mult, A.add)
-    places(0, "y", 4)
-    places(0, "x", 4)
+    for who, half in (("x", 0), ("y", 0), ("y", 1), ("x", 1)):
+        hmask(0, who, half)
+    for i in range(2):
+        affine(0, "x", 0, i, "v")
+    places(0, "x", 0)
+    act(quarter("sv", 0), col("x", 0, B), F.Copy)
+    for who, half in (("y", 0), ("y", 1)):
+        for i in range(2):
+            affine(0, who, half, i, "v")
+        places(0, who, half)
     ts(R("zf"), R("lc", 0, 256), B / 4096.0, BIAS, A.mult, A.add)
     ts(R("lz"), R("zf"), MAGIC, MAGIC - MID, A.add, A.subtract)
-    iota(R("mob"), [[0, 128]], -1)
-    iota(R("kib"), [[0, 128]], 1024)
+    for i in range(2):
+        affine(0, "x", 1, i, "v")
+    places(0, "x", 1)
     sel(R("idp"), R("ob"), [[-1, 128]], A.is_equal, 0, 1)
+    iota(R("ci"), [[1, 144]], 0)
+    iota(R("ctab"), [[1, 32], [0, 2], [32, 8]], 0)
+    iota(R("mob"), [[0, 128]], -1)
+    sel(R("tri"), R("blk"), [[1, 128]], A.is_ge, 0, -1)
     sel(R("idm"), R("mob"), [[-1, 128]], A.is_equal, 0, 1)
+    iota(R("trs0"), [[0, 2], [16, 34]], TRASH)
+    iota(R("se0"), [[0, 24], [1, 16]], 0)
+    cp(R("mx", 8, 136, 16), R("blk", 0, 128, 16))
+    ts(R("mx", 16, 144, 16), R("blk", 0, 128, 16), R("w4"), None, A.mult)
+    ts(R("cb"), R("ob"), R("krow"), -0.375, A.mult, A.mult)
+
+    def gap0():
+        ts(R("lh", 0, 1), R("sc", 4, 5), R("sc", 5, 6), -5000.0, A.is_gt, A.mult)
+        ts(R("lo"), R("sc", 4, 5), R("srow"), R("krow"), A.mult, A.subtract)
+        ts(R("wc"), R("ci"), R("cv"), None, A.is_equal)
+        ts(R("lh", 1, 2), R("lh", 0, 1), R("sc", 5, 6), R("srow"), A.add, A.mult)
+        ts(R("trin"), R("tri"), -STEP, None, A.mult)
+        ts(R("hi"), R("krow"), 10000.0, R("lh", 1, 2), A.mult, A.add)
+        blocks = [[32, 2], [0, 34]]
+        iota(R("n68"), [[0, 68]], int(BIG))
+        sel(R("ra0"), R("ob", 0, 68), blocks, A.is_ge, 31, -1)
+        sel(R("r2"), R("ra0"), [[-32, 2], [0, 34]], A.is_ge, 0, 1)
+        sel(R("rb0"), R("mob", 0, 68), blocks, A.is_ge, 31, -1)
+        sel(R("r1"), R("rb0"), [[-32, 2], [-1, 34]], A.is_ge, 0, 1)
+        sel(R("i68"), R("n68"), blocks, A.is_ge, 31, -1)
+        sel(R("r3"), R("i68"), [[-32, 2], [-1, 34]], A.is_equal, 0, 1)
+        iota(R("rst"), [[0, 128]], 1)
+        iota(R("rst", 0, 128, 8), [[0, 16]], 0)
+        for o in (0, 1):
+            iota(clear(o), [[0, CAP]], 0)
+        for w in range(2):
+            iota(R("vin%d" % w, 512, 528), [[0, 16]], 300)
+        iota(R("cand", J, J + 16), [[0, 16]], -1)
+
+    def gap1():
+        ts(R("bse"), R("krow"), float(OWN), None, A.mult)
+        ts(R("bmk", 0, 1), R("rf", 3, 4), 7.0, BIG, A.not_equal, A.mult)
+        fill(R("vb"), LIFT + 0.5 + STEP / 2)
+
+    def gap2():
+        ts(R("btab"), R("ob", 0, 68), R("bse"), None, A.mult)
+        ts(R("trs"), R("trs0"), row, None, A.add)
+        ts(R("btab", 32, 68, 34), R("ob", 0, 2), R("bmk", 0, 1), R("bse"), A.mult, A.add)
+        fill(R("stp"), STEP)
+        ts(R("selm"), R("se0"), row, 32768.0, A.is_le, A.mult)
+
+    build(0, B, gap0, gap1, gap2)
+
+    def gap0a():
+        cp(R("onx", 16, 144, 16), R("blk", 0, 128, 16))
+        ts(R("kwx", 16, 144, 16), R("blk", 0, 128, 16), R("wk"), None, A.mult)
+        ts(R("kblk"), R("blk"), R("wk"), None, A.mult)
+
+    sent0, got0 = send(0, gap0a, lambda: None)
+
+    iota(R("z16"), [[0, 16]], 0)
+    iota(R("tk0"), [[16, 24]], 2 * M)
+    sel(R("stri"), R("blk"), [[1, 128]], A.is_ge, -1, -1)
     sel(R("nb"), R("mob"), [[-16, 8], [0, 16]], A.is_ge, 0, 1)
     sel(R("nblk"), R("nb"), [[16, 8], [0, 16]], A.is_ge, 15, -1)
     sel(R("neg"), R("nblk"), [[-1, 128]], A.is_ge, 0, 1)
-    sel(R("tri"), R("blk"), [[1, 128]], A.is_ge, 0, -1)
-    sel(R("idn"), R("kib"), [[-1, 128]], A.is_equal, 0, 1)
-    iota(R("cand", J, J + 16), [[0, 16]], -1)
-    iota(R("trx0"), [[0, 2], [16, 32]], 192)
-    iota(R("rst"), [[0, 64]], 1)
-    iota(R("cap"), [[0, 2], [CAP, 2], [0, 16]], CAP)
-    iota(R("p6"), [[0, 2], [6, 2], [0, 16]], 0)
-    iota(R("rst", 0, 64, 16), [[0, 4]], 0)
-    for w in ("win0", "wib0"):
-        iota(R(w, 0, 192), [[0, 192]], 0)
-    iota(R("vdb"), [[0, 2], [UNIT, 256]], UNIT)
-    iota(R("vd"), [[0, 2], [UNIT, 256]], UNIT)
-    for w in ("win0", "wib0"):
-        iota(R(w, 0, 192, CAP), [[0, 2]], -UNIT)
-    iota(R("pref"), [[0, 4 * PAIR]], 0)
-    iota(R("p272"), [[UNIT * PAIR, 4], [0, 6]], 0)
     iota(R("one"), [[0, 384]], 1)
-    iota(R("mone"), [[0, 24]], -UNIT)
-    iota(R("tk0"), [[16, 24]], 2 * M)
-    iota(R("tb0"), [[16, 24]], J + 16)
-    sel(R("stri"), R("blk"), [[1, 128]], A.is_ge, -1, -1)
-    iota(R("z16"), [[0, 16]], 0)
-    iota(R("tx"), [[0, 2048]], 0)
-
-    def limits():
-        ts(R("nmid"), R("sc", 4, 5), R("sc", 5, 6), -0.5, A.add, A.mult)
-        ts(R("nhl"), R("sc", 5, 6), R("sc", 4, 5), -0.5 * DEAD, A.subtract, A.mult)
-        fill(R("qd"), float(DEAD))
-
-    build(0, B, lambda: act(R("lwx"), R("onx"), F.Silu, scale=R("wl")), limits)
-
-    def gap0a():
-        ts(P(7, 64, 128), R("trx0"), R("rf"), None, A.add)
-        ts(R("tk"), R("tk0"), R("rf"), None, A.add)
-        ts(R("kblk"), R("blk"), R("wk"), None, A.mult)
-        cp(R("lbf", 256, 512), R("lb", 256, 512))
-
-    def gap0b():
-        fill(R("tbl", J, J + 16), 1)
-        for k in range(4):
-            affine(1, "y", k, 5)
-
-    def gap0c():
-        cp(R("laf", 256, 512), R("la", 256, 512))
-        cp(R("lcf", 256, 512), R("lc", 256, 512))
-
-    sent0, got0 = send(0, gap0a, gap0b, gap0c)
-
-    for h in ("hy1", "hx1"):
-        iota(R(h, 0, 1280, 5), [[0, 256]], -4096)
     iota(R("bk", B, B + 4 * M), [[0, 4 * M]], 0)
-    for k in range(4):
-        affine(1, "x", k, 5)
+    for h in ("hx1", "hy1"):
+        iota(R(h, 0, 768, 3), [[0, 256]], -4096)
+    iota(R("tb0"), [[16, 24]], J + 16)
+    for o in range(N):
+        iota(clear(o), [[0, CAP]], 0)
+    fill(R("tx"), 0.0)
+    cp(R("laf", 256, 512), R("la", 256, 512))
+    cp(R("lbf", 256, 512), R("lb", 256, 512))
+    fill(R("tbl", J, J + 16), 1)
     fill(R("q1"), 1.0 / 4096)
     fill(R("b75"), B / 4096.0)
     fill(R("bia"), BIAS)
     fill(R("b4"), B + BIAS)
     pairs(2, ((1, 3), (2, 2)))
+    cp(R("lcf", 256, 512), R("lc", 256, 512))
     ts(R("w", 2, 4), R("wq", 2, 4), MAGIC, MAGIC, A.add, A.subtract)
+    ts(R("tk"), R("tk0"), row, None, A.add)
     spread("tx", "stri")
-    for i in range(2):
-        for w in ("win1", "wib1"):
-            iota(R(w, 0, 192, CAP if i else 1), [[0, 2 if i else 192]], -UNIT * i)
+    for who, half in (("x", 0), ("y", 1), ("y", 0), ("x", 1)):
+        for i in range(3):
+            if step(1, who, half, i)[0] < 4:
+                affine(1, who, half, i)
     ts(R("wb"), R("w", 2, 3), 2.0, R("w", 3, 4), A.mult, A.add)
     ts(R("by1", 1, 2), R("w", 3, 4), -8388608.0, -2048.0, A.mult, A.add)
     ts(R("by1", 2, 3), R("w", 3, 4), 8388608.0, -2048.0, A.mult, A.add)
@@ -542,31 +629,34 @@ def rank_program(g, core, T, topo):
 
     keep(0, None)
 
-    for i in range(1, 5):
-        hmask(1, "y", i, 5)
-    act(R("uy1", 0, 1280, 5), R("lbf", 256, 512), F.Identity, scale=R("n4q"), bias=R("b4"))
-    act(R("ux1", 0, 1280, 5), R("laf", 256, 512), F.Identity, scale=R("n4q"), bias=R("b4"))
-    for i in range(1, 5):
-        hmask(1, "x", i, 5)
+    hmask(1, "x", 0)
+    affine(1, "y", 0, 0)
+    hmask(1, "y", 0)
     act(R("tq"), R("n4"), F.Identity, scale=R("q1"), bias=R("b75"))
+    places(1, "x", 0)
+    act(quarter("sv", 0), col("x", 0, B), F.Copy)
+    hmask(1, "y", 1)
     act(R("zf"), R("lcf", 256, 512), F.Identity, scale=R("tq"), bias=R("bia"))
+    affine(1, "x", 1, 0)
+    hmask(1, "x", 1)
     append(0)
-    places(1, "y", 5)
-    places(1, "x", 5)
+    places(1, "y", 0)
+    places(1, "y", 1)
     ts(R("lz"), R("zf"), MAGIC, MAGIC - MID, A.add, A.subtract)
-    build(1, B + M, lambda: None, lambda: None)
+    places(1, "x", 1)
+    build(1, B + M, lambda: None, lambda: None, lambda: None)
 
     def gap1a():
         cp(R("ud"), R("one"))
-        ts(R("tb"), R("tb0"), R("rf"), None, A.add)
+        ts(R("tb"), R("tb0"), row, None, A.add)
+        ts(R("bm"), R("kb2"), float(J), None, A.min)
 
     def gap1b():
-        ts(R("bm"), R("kb2"), float(J), None, A.min)
         tt(R("tn2"), R("nk"), R("tb"), A.mult)
         tt(R("om2"), R("tn2"), R("bm"), A.max)
         cp(R("mo2"), R("om2"))
 
-    sent1, got1 = send(1, gap1a, gap1b, lambda: None)
+    sent1, got1 = send(1, gap1a, gap1b)
     scatter(R("tbl"), R("mo2"), R("ud"))
 
     keep(1, R("n4"))

@@ -9,6 +9,8 @@ HALF = -2047.5 / 4096
 MID = 1728
 BIAS = HALF - MID
 INV = 1048576
+NONE = 576
+SPARE = J + 16
 OWN = 4128
 TRASH = 2 * OWN
 WIN = TRASH + 544
@@ -19,32 +21,31 @@ STEP = 1.0 / 32
 SCRATCH = {}
 ALIAS, COLS, SIZE = {}, {}, {F32: 0, BF: 0, I32: 0}
 for _n, _c, _d in [
-    ("nl", 8, I32), ("nf", 8, F32), ("sc", 8, F32), ("nq", 8, F32), ("cs4", 8, F32), ("ub", 8, F32), ("pr", 4, F32), ("wq", 4, F32), ("w", 4, F32),
-    ("one8", 128, F32), ("b8a", 128, F32), ("b8", 128, F32), ("on4", 8, F32),
-    ("pid", 1, I32), ("ri", 4, I32), ("rf", 4, F32), ("pf1", 1, F32), ("wk", 1, F32), ("w4", 1, F32), ("srow", 1, F32), ("krow", 1, F32), ("gp", 1, F32),
-    ("cv", 1, F32), ("b3", 1, F32), ("pm", 1, F32), ("lh", 8, F32), ("lo", 1, F32), ("hi", 1, F32), ("vb", 1, F32), ("bse", 1, F32), ("bmk", 2, F32),
-    ("jc0", 256, F32), ("jc", 256, F32), ("tk0", 24, F32), ("tk", 24, F32), ("tb0", 24, F32), ("tb", 24, F32),
-    ("i8", 8, F32), ("i68", 68, F32), ("n68", 68, F32), ("trs0", 68, F32), ("trs", 68, F32), ("ci", 144, F32), ("se0", M, F32), ("se1", M, BF),
-    ("ob", 128, BF), ("ba", 128, BF), ("blk", 128, BF), ("nb", 128, BF), ("nblk", 128, BF), ("trin", 128, BF), ("tri", 128, BF), ("neg", 128, BF), ("stri", 128, BF),
-    ("kblk", 128, BF), ("mob", 128, BF), ("idp", 128, BF), ("idm", 128, BF), ("z16", 16, BF), ("blk8", 8, BF), ("cb", 128, BF),
-    ("mx", 144, BF), ("wc", 144, BF), ("onx", 144, BF), ("kwx", 144, BF), ("tx", 2048, BF),
-    ("r1", 68, BF), ("r2", 68, BF), ("r3", 68, BF), ("ra0", 68, BF), ("rb0", 68, BF), ("btab", 68, BF), ("rst", 128, BF), ("ctab", 512, BF), ("selm", M, BF), ("stp", CAP, F32),
-    ("one", 384, BF), ("ud", 384, I32),
-    ("q1", 1, F32), ("b75", 1, F32), ("bia", 1, F32), ("b4", 1, F32),
+    ("nl", 8, I32), ("nf", 10, F32), ("sc", 10, F32), ("ub", 8, F32), ("wi", 2, I32), ("wf", 2, F32), ("wq", 2, F32), ("wm", 2, F32), ("w", 2, F32),
+    ("one8", 128, F32), ("b8a", 128, F32), ("b8", 128, F32), ("blkf", 128, F32),
+    ("pid", 1, I32), ("ri", 2, I32), ("rf", 2, F32), ("wk", 1, F32), ("w4", 1, F32), ("srow", 1, F32), ("krow", 1, F32), ("kneg", 1, F32),
+    ("lh", 8, F32), ("lo", 1, F32), ("hi", 1, F32), ("bse", 1, F32), ("bmk", 2, F32), ("sb", 1, F32), ("mb", 1, F32),
+    ("jc0", 256, F32), ("jc", 256, F32), ("tk0", 24, F32), ("tk", 24, F32),
+    ("i68", 68, F32), ("n68", 68, F32), ("trs0", 68, F32), ("trs", 68, F32), ("se0", M, F32),
+    ("ob", 128, BF), ("ba", 128, BF), ("blk", 128, BF), ("nb", 128, BF), ("nst", 128, BF), ("tra", 128, BF), ("trin", 128, BF), ("neg", 128, BF),
+    ("kblk", 128, BF), ("mob", 128, BF), ("idp", 128, BF), ("idm", 128, BF), ("idn", 128, BF), ("z16", 16, BF), ("cb", 128, BF),
+    ("wts", 4 * 144, BF), ("wca", 144, BF), ("wc", 144, BF),
+    ("r1", 68, BF), ("r2", 68, BF), ("r3", 68, BF), ("ra0", 68, BF), ("rb0", 68, BF), ("btab", 68, BF), ("rst", 128, BF), ("ctab", 512, BF),
+    ("selm", M, BF), ("mle", M, BF), ("stp", CAP, F32), ("one", 24, BF), ("ud", M, F32), ("ui", 256, I32), ("uf", 256, F32),
     ("bx0", 4, F32), ("by0", 4, F32), ("bx1", 4, F32), ("by1", 4, F32), ("wb", 1, F32), ("k1", 1, F32),
     ("scx0", 1, F32), ("scy0", 1, F32), ("scx1", 1, F32), ("scy1", 1, F32),
-    ("n4", 1, F32), ("n4q", 1, F32), ("tq", 1, F32), ("wx", 1, F32), ("w0", 1, F32),
+    ("n4", 1, F32), ("n4q", 1, F32), ("tq", 1, F32), ("w0", 1, I32), ("ksum", 1, F32),
     ("la", 512, I32), ("lb", 512, I32), ("lc", 512, I32), ("laf", 512, F32), ("lbf", 512, F32), ("lcf", 512, F32),
     ("ux0", 512, F32), ("uy0", 512, F32), ("ux1", 768, F32), ("uy1", 768, F32),
     ("hx0", 512, BF), ("hy0", 512, BF), ("hx1", 768, BF), ("hy1", 768, BF), ("sox", 768, F32), ("soy", 768, F32),
     ("zf", 256, F32), ("lx", 256, U16), ("ly", 256, U16), ("lz", 256, U16),
-    ("bk", B + 4 * M, BF), ("sv", 3072, BF), ("xv", 1024, BF), ("xa", 1024, BF), ("fv", J, BF), ("cand", J + 16, BF),
-    ("cl", 128, I32), ("dd", 128, BF), ("ind", 1024, BF), ("t1", 128, BF), ("t2", 128, BF), ("t3", 128, BF), ("of", 68, F32), ("off", 68, U16),
+    ("bk", B + SPARE + 2 * M, BF), ("sv", 3072, BF), ("xv", 1024, BF), ("xa", 1024, BF), ("fv", J, BF), ("cand", J + 16, BF),
+    ("cl", 128, I32), ("dd", 128, BF), ("ind", 1024, BF), ("ab", 256, BF), ("t1", 128, BF), ("t2", 128, BF), ("t3", 128, BF), ("of", 68, F32), ("off", 68, U16),
     ("vin0", 528, F32), ("vin1", 528, F32), ("win0", WIN, F32), ("win1", WIN, F32), ("sx", M, F32), ("fr", M, BF), ("sj", M, F32),
     ("jl", 24, U16), ("snd0", 288, BF), ("snd1", 288, BF), ("arr0", M, BF), ("arr1", M, BF),
-    ("ki", 24, I32), ("kb", 24, I32), ("kf", 24, F32), ("kb2", 24, I32), ("bm", 24, F32), ("bo", 24, U16), ("r32", M, I32), ("r33", M, I32), ("r16", M, U16),
-    ("tbl", J + 16 + M, I32), ("us", M, BF), ("eq", 24 * M, BF), ("dm", M, BF),
-    ("nk", 24, BF), ("kp", 24, BF), ("ks", 24, BF), ("tn", 24, F32), ("om", 24, F32), ("mo", 24, U16), ("tn2", 24, F32), ("om2", 24, F32), ("mo2", 24, U16),
+    ("ki", 24, I32), ("kb", 24, I32), ("kf", 24, F32), ("kb2", 24, I32), ("bm", 24, F32), ("bo", 24, U16), ("fl", M, BF), ("r16", M, U16),
+    ("tbl", SPARE + M, F32), ("us", M, BF), ("dm", M, BF),
+    ("nk", 24, BF), ("kp", 24, BF), ("ks", 24, BF), ("tn", 24, F32), ("om", 24, F32), ("mo", 24, U16), ("om2", 24, F32), ("mo2", 24, U16),
 ]:
     COLS[_n] = _c
     if _c <= 128 and _d != U16 and _n != "nl":
@@ -55,10 +56,11 @@ for _n, _c, _d in [
 SCRATCH["pf"] = ("sbuf", [128, SIZE[F32]], F32)
 SCRATCH["pb"] = ("sbuf", [128, SIZE[BF]], BF)
 SCRATCH["pi"] = ("sbuf", [128, SIZE[I32]], I32)
+SCRATCH["eq"] = ("sbuf", [128, 24, M], BF)
 for _n in range(8):
     SCRATCH["ps%d" % _n] = ("psum", [128, 512], F32)
 
-DMAS = ["d_ncl", "d_lim", "d_la0", "d_lb0", "d_lc0", "d_la1", "d_lb1", "d_lc1", "d_bk", "d_used", "d_y", "d_add0", "d_add1"]
+DMAS = ["d_ncl", "d_lim", "d_la0", "d_lb0", "d_lc0", "d_la1", "d_lb1", "d_lc1", "d_bk", "d_ui", "d_used", "d_y", "d_add0", "d_add1"]
 SEMAPHORES = ["cv", "cs", "ct", "cg", "arrv0", "arrv1", "snt0", "snt1"] + DMAS
 
 
@@ -125,7 +127,7 @@ def rank_program(g, core, T, topo):
                 if ps and t["q"] != q or (overlap(r, r2) and not (ps and q == "t")):
                     toks.append(t)
             for r2, t in read.get(n, []):
-                if t["q"] != q and (ps or overlap(r, r2)):
+                if (ps and t["q"] != q) or overlap(r, r2):
                     toks.append(t)
         need(q, toks)
 
@@ -182,19 +184,24 @@ def rank_program(g, core, T, topo):
     def scatter(w, o, i):
         emit("v", w[1], i[1] + o[1], lambda e: e.tensor_copy(w[0].indirect(o[0]), i[0]))
 
-    def scan(o, a, b, op0, op1):
-        emit("v", o[1], a[1] + b[1], lambda e: e.tensor_tensor_scan(o[0], a[0], b[0], 0.0, op0, op1))
+    def scan(o, a, b, op0, op1, first=0.0):
+        emit("v", o[1], a[1] + b[1], lambda e: e.tensor_tensor_scan(o[0], a[0], b[0], first, op0, op1))
 
     def fill(o, c):
         emit("v", o[1], [], lambda e: e.memset(o[0], c))
 
-    def act(o, i, func, scale=None, bias=None):
-        kw, more = {}, []
+    def act(o, i, func, scale=None, bias=None, total=None):
+        kw, more, outs = {}, [], o[1]
         for k, x in (("scale", scale), ("bias", bias)):
             if x is not None:
-                kw[k] = x[0]
-                more = more + x[1]
-        emit("s", o[1], i[1] + more, lambda e: e.activation(o[0], i[0], func, **kw))
+                kw[k], r = scal(x)
+                more = more + r
+        if total is not None:
+            kw["accum_out"], outs = total[0], outs + total[1]
+        emit("s", outs, i[1] + more, lambda e: e.activation(o[0], i[0], func, **kw))
+
+    def lin(o, i, scale=None, bias=None):
+        act(o, i, F.Identity, scale, bias)
 
     def mm(o, l, r, start, stop):
         emit("t", o[1], l[1] + r[1], lambda e: e.matmul(o[0], l[0], r[0], start, stop))
@@ -202,8 +209,8 @@ def rank_program(g, core, T, topo):
     def iota(o, pattern, base, cm=0):
         emit("g", o[1], [], lambda e: e.iota(o[0], pattern, base, cm, allow_small_or_imprecise_dtypes=True))
 
-    def sel(o, i, pattern, op, base, cm):
-        emit("g", o[1], i[1], lambda e: e.affine_select(o[0], i[0], pattern, op, 0.0, base, cm))
+    def sel(o, i, pattern, op, base, cm, other=0.0):
+        emit("g", o[1], i[1], lambda e: e.affine_select(o[0], i[0], pattern, op, other, base, cm))
 
     def dma(q, sem, o, i, total=16):
         if total == 16:
@@ -214,17 +221,16 @@ def rank_program(g, core, T, topo):
     def ext(ap):
         return (ap, [])
 
-    def listify(o, wname, src, ncols, start, stop, st=16):
+    def W(name, a, b, st=1):
+        o = 144 * ("mx", "onx", "kwx", "zero").index(name)
+        return R("wts", o + a, o + b, st)
+
+    def listify(o, wname, src):
         for x in range(16):
-            w = R(wname, 128 * x, 128 * x + 128) if wname == "tx" else R(wname, 16 - x, 144 - x)
-            mm(o, w, R(src, x, ncols, st), start and x == 0, stop and x == 15)
+            mm(o, W(wname, 16 - x, 144 - x), R(src, x, M, 16), x == 0, x == 15)
 
     def P(k, a, b, st=1, rows=None):
         return R("ps%d" % k, a, b, st, rows)
-
-    def spread(name, src, xs=range(16)):
-        for x in xs:
-            act(R(name, 129 * x, 128 * x + 128, 16), R(src, x, 128, 16), F.Copy)
 
     first8 = slice(0, 8)
     dma("y", "d_ncl", R("nl", 0, 4, rows=first8), ext(T.ncl[:, :]))
@@ -236,62 +242,61 @@ def rank_program(g, core, T, topo):
     dma("y", "d_lb1", R("lb", 256, 512), ext(T.rb[:, 256:512]))
     dma("y", "d_la1", R("la", 256, 512), ext(T.ra[:, 256:512]))
     dma("y", "d_lc1", R("lc", 256, 512), ext(T.rc[:, 256:512]))
-    for r in range(16):
-        dma("y", "d_used", R("tbl", 0, J, rows=slice(r, 128, 16)), ext(T.used[:, :]), 256)
+    dma("y", "d_ui", R("ui"), ext(T.used[:, :]))
 
     def clear(o):
         return R("win%d" % (o // 2), OWN * (o % 2), OWN * (o % 2) + CAP)
 
     fill(R("one8"), 1.0)
-    fill(R("q1"), 0.0)
     fill(R("ob"), 1.0)
     for o in (2, 3):
-        act(clear(o), R("one8", 0, CAP), F.Silu, scale=R("q1"))
+        act(clear(o), R("one8", 0, CAP), F.Silu, scale=0.0)
     iota(R("pid"), [[0, 1]], 0, 1)
     sel(R("b8a", rows=first8), R("one8", rows=first8), [[1, 128]], A.is_ge, 0, -16)
     sel(R("b8", rows=first8), R("b8a", rows=first8), [[-1, 128]], A.is_ge, 15, 16)
     iota(R("jc0"), [[16, 256]], -2048)
     sel(R("ba"), R("ob"), [[-16, 8], [0, 16]], A.is_ge, 0, 1)
     sel(R("blk"), R("ba"), [[16, 8], [0, 16]], A.is_ge, 15, -1)
-    for i, bits in enumerate((15, 1, 8, 7)):
+    for i, bits in enumerate((15, 7)):
         ts(R("ri", i, i + 1), R("pid"), bits, None, A.bitwise_and)
+    fill(R("wts"), 0.0)
+    cp(R("rf"), R("ri"))
+    row = R("rf", 0, 1)
     for h in ("hx0", "hy0"):
         fill(R(h, 0, 512, 2), -4096.0)
-    cp(R("rf"), R("ri"))
-    cp(R("pf1"), R("pid"))
-    row = R("rf", 0, 1)
-    for w in ("mx", "onx", "kwx"):
-        fill(R(w), 0.0)
-    ts(R("wk"), row, 14.0, 9.0, A.mult, A.add)
-    ts(R("w4"), R("rf", 1, 2), 0.5, 0.25, A.mult, A.add)
-    ts(R("srow"), R("rf", 2, 3), 0.0, None, A.is_equal)
-    ts(R("krow"), R("rf", 2, 3), 0.0, None, A.not_equal)
-    ts(R("cv"), R("pf1"), R("rf", 2, 3), 8.0, A.subtract, A.add)
-    fill(R("on4"), 1.0)
-    fill(R("by0", 1, 2), -2048.0)
     fill(R("ub", 0, 1), BIAS)
+    fill(R("nst"), -STEP)
+    ts(R("srow"), row, 8.0, None, A.is_lt)
+    ts(R("krow"), row, 8.0, None, A.is_ge)
+    ts(R("w4"), row, 3.5, 2.25, A.mult, A.add)
+    ts(R("bmk", 0, 1), R("rf", 1, 2), 7.0, BIG, A.not_equal, A.mult)
+    fill(R("stp"), STEP)
+    ts(R("bse"), R("krow"), float(OWN), None, A.mult)
+    ts(R("cb"), R("ob"), R("krow"), -0.375, A.mult, A.mult)
+    ts(R("btab"), R("ob", 0, 68), R("bse"), None, A.mult)
+    ts(R("jc"), R("jc0"), row, None, A.add)
+    lin(R("wk"), row, 14.0, 9.0)
+    lin(R("sb"), row, 32768.0, 32768.0)
+    lin(R("mb"), row, -1.0, 1.0)
+    lin(R("btab", 32, 68, 34), R("ob", 0, 2), R("bmk", 0, 1), R("bse"))
 
     cp(R("nf", 0, 6, rows=first8), R("nl", 0, 6, rows=first8))
-    mm(P(7, 0, 6), R("b8", rows=first8), R("nf", 0, 6, rows=first8), True, True)
-    ts(R("jc"), R("jc0"), row, None, A.add)
-    cp(R("sc", 0, 6), P(7, 0, 6))
-
-    def pairs(k, ab):
-        for i, (a, b) in enumerate(ab):
-            tt(R("pr", k + i, k + i + 1), R("sc", a, a + 1), R("sc", b, b + 1), A.mult)
-        ts(R("wq", k, k + 2), R("pr", k, k + 2), 1.0 / 4096, HALF, A.mult, A.add)
-
-    pairs(0, ((0, 3), (1, 2)))
-    ts(R("nq", 0, 4), R("sc", 0, 4), 1.0 / 4096, None, A.mult)
-    scan(R("cs4", 0, 4), R("on4", 0, 4), R("sc", 0, 4), A.mult, A.add)
-    ts(R("w", 0, 2), R("wq", 0, 2), MAGIC, MAGIC, A.add, A.subtract)
-    ts(R("ub", 1, 4), R("cs4", 0, 3), BIAS, None, A.add)
-    ts(R("bx0", 0, 1), R("w", 1, 2), 16777216.0, 2048.0, A.mult, A.add)
-    ts(R("scx0"), R("w", 0, 1), R("w", 1, 2), 8192.0, A.add, A.mult)
-    ts(R("by0", 2, 3), R("w", 1, 2), 16777216.0, -2048.0, A.mult, A.add)
-    ts(R("scy0"), R("w", 0, 1), R("w", 1, 2), -8192.0, A.add, A.mult)
-    ts(R("by0", 0, 1), R("w", 1, 2), -16777216.0, -2048.0, A.mult, A.add)
-    ts(R("bx0", 2, 3), R("w", 1, 2), -16777216.0, 2048.0, A.mult, A.add)
+    ts(R("nf", 6, 10, rows=first8), R("nl", 0, 4, rows=first8), 1.0 / 4096, None, A.mult)
+    mm(P(7, 0, 10), R("b8", rows=first8), R("nf", rows=first8), True, True)
+    act(W("mx", 8, 136, 16), R("blk", 0, 128, 16), F.Copy)
+    act(W("mx", 16, 144, 16), R("blk", 0, 128, 16), F.Copy, scale=R("w4"))
+    cp(R("lbf", 0, 256), R("lb", 0, 256))
+    for i, (a, b) in enumerate(((0, 3), (1, 2))):
+        ts(R("wi", i, i + 1), P(7, a, a + 1), P(7, 6 + b, 7 + b), HALF, A.mult, A.add)
+    cp(R("sc"), P(7, 0, 10))
+    ts(R("wf"), R("wi"), 8192.0, None, A.mult)
+    scan(R("ub", 1, 5), R("one8", 0, 4), P(7, 0, 4), A.mult, A.add, BIAS)
+    ts(R("bx0", 0, 1), R("wi", 1, 2), 16777216.0, 2048.0, A.mult, A.add)
+    tt(R("scx0"), R("wf", 0, 1), R("wf", 1, 2), A.add)
+    lin(R("by0", 0, 1), R("wf", 1, 2), -2048.0, -2048.0)
+    lin(R("by0", 2, 3), R("wf", 1, 2), 2048.0, -2048.0)
+    lin(R("bx0", 2, 3), R("wf", 1, 2), -2048.0, 2048.0)
+    lin(R("scy0"), R("scx0"), -1.0)
 
     def step(t, who, half, i):
         m = 2 + t
@@ -300,18 +305,21 @@ def rank_program(g, core, T, topo):
 
     def affine(t, who, half, i, q="s"):
         k, _, cols = step(t, who, half, i)
-        sc_, bi = (R("nq", k, k + 1), R("ub", k, k + 1)) if k < 4 else (R("n4q"), R("b4"))
+        sc_, bi = R("sc", 6 + k, 7 + k) if k < 4 else R("n4q"), R("ub", k, k + 1)
         name, a = "l" + ("a" if who == "x" else "b"), 256 * t + 128 * half
         if q == "s":
-            act(R("u%s%d" % (who, t), *cols), R(name + "f", a, a + 128), F.Identity, scale=sc_, bias=bi)
+            lin(R("u%s%d" % (who, t), *cols), R(name + "f", a, a + 128), sc_, bi)
         else:
             ts(R("u%s%d" % (who, t), *cols), R(name, a, a + 128), sc_, bi, A.mult, A.add)
 
-    def hmask(t, who, half):
+    def hmask(t, who, half, q="s"):
         for i in range(1, 2 + t):
             _, k, cols = step(t, who, half, i)
-            act(R("h%s%d" % (who, t), *cols), R("jc", 128 * half, 128 * half + 128), F.Identity, scale=R("sc%s%d" % (who, t)),
-                bias=R("b%s%d" % (who, t), k, k + 1))
+            x = R("h%s%d" % (who, t), *cols), R("jc", 128 * half, 128 * half + 128), R("sc%s%d" % (who, t)), R("b%s%d" % (who, t), k, k + 1)
+            if q == "s":
+                lin(*x)
+            else:
+                ts(*x, A.mult, A.add)
 
     def places(t, who, half):
         m = 2 + t
@@ -336,7 +344,7 @@ def rank_program(g, core, T, topo):
         mm(P(k, 0, 128), R("idp"), R("cb"), True, False)
         for x in range(16):
             c = 64 * (x // 8)
-            mm(P(k, c, c + 64), R("mx", 8 - x % 8, 136 - x % 8), R("cand", 1024 * q + x, 1024 * q + 1024, 16), False, x == 15)
+            mm(P(k, c, c + 64), W("mx", 8 - x % 8, 136 - x % 8), R("cand", 1024 * q + x, 1024 * q + 1024, 16), False, x == 15)
 
     owners = [(rank + 1 + i) % N for i in range(N)]
     low64 = slice(0, 64)
@@ -350,17 +358,25 @@ def rank_program(g, core, T, topo):
     def count_cols(q):
         for o in range(N):
             for s in (2 * q, 2 * q + 1):
-                mm(P(5, 8 * (o % 2) + s, 128, 16, slice(32 * (o // 2), 32 * (o // 2) + 32)), R("ind", 256 * o + 32 * s, 256 * o + 32 * s + 32),
-                   R("blk", 0, 128, 16), True, True)
+                mm(P(5, 8 * (o % 2) + s, 128, 16, slice(32 * (o // 2), 32 * (o // 2) + 32)), seg(o, s), R("blk", 0, 128, 16), True, True)
 
     def prefix(q, w, last):
         for o in (2 * w, 2 * w + 1):
             for s in (2 * q, 2 * q + 1):
-                mm(P(6 + w, 8 * (o % 2) + s, 512, 16), R("trin"), R("ind", 256 * o + 32 * s, 256 * o + 32 * s + 32), False, last and o % 2 == 1 and s % 2 == 1)
+                mm(P(6 + w, 8 * (o % 2) + s, 512, 16), R("trin"), seg(o, s), False, last and o % 2 == 1 and s % 2 == 1)
 
-    def mark(q):
+    def mark(q, who="v"):
         for i, p in enumerate(owners):
-            ts(R("ind", 256 * i + 64 * q, 256 * i + 64 * q + 64), P(4, 0, 64), p / 4 - 0.375, None, A.is_equal)
+            if who == "v":
+                ts(R("ind", 256 * q + 64 * i, 256 * q + 64 * i + 64), P(4, 0, 64), p / 4 - 0.375, None, A.is_equal)
+            else:
+                act(R("ab", 64 * i, 64 * i + 64), P(4, 0, 64), F.Abs, None, 0.375 - p / 4)
+        if who == "s":
+            act(R("ind", 256 * q, 256 * q + 256), R("ab"), F.Relu, -4.0, 1.0)
+
+    def seg(o, s):
+        a = 256 * (s // 2) + 64 * o + 32 * (s % 2)
+        return R("ind", a, a + 32)
 
     def counts(q):
         count_cols(q)
@@ -372,11 +388,14 @@ def rank_program(g, core, T, topo):
         g.dma_start(o[0], i[0], accum_op=A.add).then_inc(T.sem[sem], 16)
         record("g", o[1], i[1], sem, 16)
 
-    def build(t, wid, gap0, gap1, gap2):
+    def build(t, wid, gap0, gap1, gap2, gap3):
         act(quarter("sv", 1), col("x", 1, B), F.Copy)
+        places(t, "y", 1)
         first(0, wid)
         act(quarter("fv", 3), col("y", 3, B), F.Copy)
+        ts(R("lz"), R("zf"), MAGIC, MAGIC - MID, A.add, A.subtract)
         gap0()
+        places(t, "x", 1)
         third(0, wid)
         sums(0, 0)
         for w in range(2):
@@ -384,27 +403,36 @@ def rank_program(g, core, T, topo):
         act(R("xa"), col("x", 3, wid), F.Copy)
         add(quarter("fv", 3), R("xa"), "d_add%d" % t)
         act(quarter("sv", 2), col("y", 2, B), F.Copy)
-        for h in range(2):
+
+        def gather_x2(h):
             act(R("xv", 512 * h, 512 * h + 512), X(R("bk", 0, wid), R("lx", 128 + 32 * h, 160 + 32 * h)), F.Copy)
+
+        def differ(h):
+            mm(P(2 + h, 0, 512), R("idp"), R("xv", 512 * h, 512 * h + 512), True, False)
+            mm(P(2 + h, 0, 512), R("idm"), R("sv", 2048 + 512 * h, 2560 + 512 * h), False, True)
+
         first(1, wid)
         gap1()
         judge(0)
+        gather_x2(0)
+        differ(0)
+        mark(0, "s")
+        gather_x2(1)
         third(1, wid)
-        sums(1, 1)
-        mark(0)
         counts(0)
-        gap2()
-        judge(1)
-        third(3, wid)
+        sums(1, 1)
+        differ(1)
         for h in range(2):
-            mm(P(2 + h, 0, 512), R("idp"), R("xv", 512 * h, 512 * h + 512), True, False)
-            mm(P(2 + h, 0, 512), R("idm"), R("sv", 2048 + 512 * h, 2560 + 512 * h), False, True)
             act(R("fv", 2048 + 512 * h, 2560 + 512 * h), P(2 + h, 0, 512), F.Abs)
+        gap2()
+        third(3, wid)
         sums(3, 0)
-        mark(1)
+        judge(1)
+        mark(1, "s")
         third(2, wid, 0, 32)
-        counts(1)
         judge(0)
+        counts(1)
+        gap3()
         third(2, wid, 32, 64)
         sums(2, 1)
         mark(3)
@@ -426,7 +454,7 @@ def rank_program(g, core, T, topo):
         for i in (2, 1, 3):
             mm(P(2, 0, 68), R("t%d" % i, rows=low64), R("r%d" % i, rows=low64), False, i == 3)
         for w in range(2):
-            act(R("vin%d" % w, 0, 512), P(6 + w, 0, 512), F.Identity, bias=R("vb"))
+            lin(R("vin%d" % w, 0, 512), P(6 + w, 0, 512), None, LIFT + 0.5 + STEP / 2)
         tt(R("of"), P(2, 0, 68), R("trs"), A.min)
         cp(R("off"), R("of"))
         scatter(R("win0"), R("off", 0, 33), R("vin0"))
@@ -471,44 +499,45 @@ def rank_program(g, core, T, topo):
                 wrote.setdefault(arr, []).append((range(CAP * q, CAP * q + CAP), tok))
         return sum(len(e) for e in mine.values()), total
 
-    def keep(t, base):
+    def keep(t, meanwhile):
         arr = "arr%d" % t
         mm(P(2, 0, M), R("kblk"), R(arr), True, True)
-        listify(P(3, 0, 24), "kwx", arr, M, True, True)
-        cp(R("r32"), P(2, 0, M))
-        ts(R("r33"), R("r32"), INV + 16383, None, A.bitwise_and)
+        mm(P(6, 0, M), R("kblk"), R(arr), True, False)
+        listify(P(3, 0, 24), "kwx", arr)
+        lin(R("fl"), P(2, 0, M), 1.0 / 16384, 128.5 + 1.0 / 32768)
+        mm(P(6, 0, M), R("idn"), R("fl"), False, True)
         cp(R("ki"), P(3, 0, 24))
-        cp(R("r16"), R("r33"))
         ts(R("kb"), R("ki"), INV + 16383, None, A.bitwise_and)
         cp(R("kf"), R("kb"))
-        mm(P(0, 0, 16), R("blk"), R("z16"), True, True)
+        ts(R("kb2"), R("kb"), 2, None, A.arith_shift_right)
+        ts(R("r16"), P(6, 0, M), 129.0 * 16384, None, A.add)
+        ts(R("bo"), R("kb2"), J, None, A.min)
+        act(R("us"), X(R("tbl", 0, J + 16), R("bo")), F.Copy)
+        meanwhile()
+        mm(P(0, 0, M), W("zero", 0, 128), R("mle"), True, False)
         for q in range(24):
-            ts(R("eq", 400 * q, M * q + M), R("r16", 16 * q, M), R("kf", q, q + 1), None, A.is_equal)
-            if q == 0:
-                ts(R("kb2"), R("kb"), 2, None, A.arith_shift_right)
-            if q == 1:
-                ts(R("bo"), R("kb2"), J, None, A.min)
+            n = M - 16 * q
+            ts((T.eq[:, q, 0:n], [("eq", range(M * q, M * q + n))]), R("r16", 16 * q, M), R("kf", q, q + 1), None, A.is_equal)
             if q < 23:
-                mm(P(0, 16 * q + 16, M), R("blk"), R("eq", 400 * q + 16, M * q + M), q == 0, q == 22)
-        listify(P(1, 0, 24), "tx", "eq", 24 * M, True, False, 400)
-        cp(R("us"), X(R("tbl", 0, J + 16), R("bo")))
-        tt(R("dm"), R("us"), P(0, 0, M), A.add)
-        listify(P(1, 0, 24), "onx", "dm", M, False, True)
-        ts(R("kp"), P(1, 0, 24), 0.0, None, A.is_equal)
-        scan(R("ks"), R("one", 0, 24), R("kp"), A.mult, A.add)
-        ts(R("nk"), P(1, 0, 24), 0.0, None, A.is_gt)
+                mm(P(0, 16 * q + 16, M), R("blk"), (T.eq[:, q, 16:n], [("eq", range(M * q, M * q + n))]), False, False)
+            if q == 8:
+                mm(P(0, 0, M), R("idp"), R("us"), False, False)
+        mm(P(0, 0, M), R("idp"), (T.eq[:, :, 0:16], [("eq", range(0, 24 * M))]), False, True)
+        tt(R("dm"), P(0, 0, M), R("mle"), A.mult)
+        listify(P(1, 0, 24), "onx", "dm")
+        act(R("kp"), P(1, 0, 24), F.Relu, -1.0, 2.0, R("ksum"))
         if t == 0:
-            mm(P(5, 200, 201), R("blk"), R("ks", 23, 24), True, True)
+            mm(P(5, 200, 201), R("blkf"), R("ksum"), True, True)
+        scan(R("ks"), R("one"), R("kp"), A.mult, A.add)
+        ts(R("nk"), R("kp"), 0.0, None, A.is_equal)
         mm(P(4, 64, 88), R("neg"), R("kp"), True, False)
         mm(P(4, 64, 88), R("blk"), R("ks"), False, True)
         if t == 0:
-            ts(R("wx"), P(5, 200, 201), R("nq", 0, 1), HALF, A.mult, A.add)
-            cp(R("n4"), P(5, 200, 201))
-            ts(R("w0"), R("wx"), MAGIC, MAGIC, A.add, A.subtract)
-            ts(R("n4q"), R("n4"), 1.0 / 4096, None, A.mult)
-            ts(R("scx1"), R("w0"), 8192.0, R("k1"), A.mult, A.add)
-            ts(R("scy1"), R("w0"), -8192.0, R("k1"), A.mult, A.subtract)
+            ts(R("w0"), P(5, 200, 201), R("sc", 6, 7), HALF, A.mult, A.add)
+
         tt(R("tn"), R("nk"), R("tk"), A.mult)
+
+    def rooms(base):
         tt(R("om"), R("tn"), P(4, 64, 88), A.max)
         if base is None:
             cp(R("mo"), R("om"))
@@ -516,42 +545,44 @@ def rank_program(g, core, T, topo):
             ts(R("mo"), R("om"), base, None, A.add)
 
     def append(t):
-        scatter(R("bk", B, B + 4 * M), R("mo"), R("arr%d" % t))
+        scatter(R("bk", B), R("mo"), R("arr%d" % t))
 
-    for who, half in (("x", 0), ("y", 0), ("y", 1), ("x", 1)):
-        hmask(0, who, half)
+    def nothing():
+        pass
+
     for i in range(2):
         affine(0, "x", 0, i, "v")
+    hmask(0, "x", 0, "v")
+    for half in range(2):
+        hmask(0, "y", half)
+        for i in range(2):
+            affine(0, "y", half, i)
+    hmask(0, "x", 1)
     places(0, "x", 0)
     act(quarter("sv", 0), col("x", 0, B), F.Copy)
-    for who, half in (("y", 0), ("y", 1)):
-        for i in range(2):
-            affine(0, who, half, i, "v")
-        places(0, who, half)
     ts(R("zf"), R("lc", 0, 256), B / 4096.0, BIAS, A.mult, A.add)
-    ts(R("lz"), R("zf"), MAGIC, MAGIC - MID, A.add, A.subtract)
+    places(0, "y", 0)
     for i in range(2):
         affine(0, "x", 1, i, "v")
-    places(0, "x", 1)
+    ts(R("lh", 0, 1), R("sc", 4, 5), R("sc", 5, 6), -5000.0, A.is_gt, A.mult)
+    ts(R("lo"), R("sc", 4, 5), R("srow"), R("krow"), A.mult, A.subtract)
     sel(R("idp"), R("ob"), [[-1, 128]], A.is_equal, 0, 1)
-    iota(R("ci"), [[1, 144]], 0)
     iota(R("ctab"), [[1, 32], [0, 2], [32, 8]], 0)
+    sel(R("wca"), W("zero", 0, 144), [[-16, 9], [256, 2], [-1, 8]], A.not_equal, -256, 1, 1.0)
+    sel(R("wc"), R("wca"), [[-16, 9], [256, 2], [-1, 8]], A.not_equal, -264, 1, 1.0)
+    sel(R("tra"), R("nst"), [[1, 128]], A.is_ge, 0, -1)
+    sel(R("trin"), R("tra"), [[-16, 8], [0, 16]], A.is_ge, 0, 1)
     iota(R("mob"), [[0, 128]], -1)
-    sel(R("tri"), R("blk"), [[1, 128]], A.is_ge, 0, -1)
     sel(R("idm"), R("mob"), [[-1, 128]], A.is_equal, 0, 1)
     iota(R("trs0"), [[0, 2], [16, 34]], TRASH)
     iota(R("se0"), [[0, 24], [1, 16]], 0)
-    cp(R("mx", 8, 136, 16), R("blk", 0, 128, 16))
-    ts(R("mx", 16, 144, 16), R("blk", 0, 128, 16), R("w4"), None, A.mult)
-    ts(R("cb"), R("ob"), R("krow"), -0.375, A.mult, A.mult)
+    iota(R("tk0"), [[16, 24]], SPARE)
 
     def gap0():
-        ts(R("lh", 0, 1), R("sc", 4, 5), R("sc", 5, 6), -5000.0, A.is_gt, A.mult)
-        ts(R("lo"), R("sc", 4, 5), R("srow"), R("krow"), A.mult, A.subtract)
-        ts(R("wc"), R("ci"), R("cv"), None, A.is_equal)
         ts(R("lh", 1, 2), R("lh", 0, 1), R("sc", 5, 6), R("srow"), A.add, A.mult)
-        ts(R("trin"), R("tri"), -STEP, None, A.mult)
-        ts(R("hi"), R("krow"), 10000.0, R("lh", 1, 2), A.mult, A.add)
+        ts(R("hi"), R("krow"), 1000000.0, R("lh", 1, 2), A.mult, A.add)
+
+    def gap1():
         blocks = [[32, 2], [0, 34]]
         iota(R("n68"), [[0, 68]], int(BIG))
         sel(R("ra0"), R("ob", 0, 68), blocks, A.is_ge, 31, -1)
@@ -566,100 +597,89 @@ def rank_program(g, core, T, topo):
             iota(clear(o), [[0, CAP]], 0)
         for w in range(2):
             iota(R("vin%d" % w, 512, 528), [[0, 16]], 300)
-        iota(R("cand", J, J + 16), [[0, 16]], -1)
-
-    def gap1():
-        ts(R("bse"), R("krow"), float(OWN), None, A.mult)
-        ts(R("bmk", 0, 1), R("rf", 3, 4), 7.0, BIG, A.not_equal, A.mult)
-        fill(R("vb"), LIFT + 0.5 + STEP / 2)
+        iota(R("cand", J, J + 16), [[0, 16]], NONE)
+        iota(R("tbl", J, J + 16), [[0, 16]], 2)
+        iota(R("one"), [[0, 24]], 1)
+        sel(R("nb"), R("mob"), [[-1, 128]], A.is_ge, 0, 1)
+        sel(R("neg"), R("nb"), [[16, 8], [0, 16]], A.is_ge, 15, -1)
+        iota(R("bk", B, B + 2 * M), [[0, 2 * M]], 0)
+        for h in ("hx1", "hy1"):
+            iota(R(h, 0, 768, 3), [[0, 256]], -4096)
 
     def gap2():
-        ts(R("btab"), R("ob", 0, 68), R("bse"), None, A.mult)
-        ts(R("trs"), R("trs0"), row, None, A.add)
-        ts(R("btab", 32, 68, 34), R("ob", 0, 2), R("bmk", 0, 1), R("bse"), A.mult, A.add)
-        fill(R("stp"), STEP)
-        ts(R("selm"), R("se0"), row, 32768.0, A.is_le, A.mult)
+        cp(R("uf"), R("ui"))
+        prepare("y", [], R("uf")[1])
+        for r in range(16):
+            dma("y", "d_used", R("tbl", 0, J, rows=slice(r, 128, 16)), R("uf"), 256)
 
-    build(0, B, gap0, gap1, gap2)
+    def gap3():
+        lin(R("trs"), R("trs0"), None, row)
+        act(R("selm"), R("se0"), F.Relu, -32768.0, R("sb"))
+        act(W("onx", 16, 144, 16), R("blk", 0, 128, 16), F.Copy)
+        act(W("kwx", 16, 144, 16), R("blk", 0, 128, 16), F.Copy, scale=R("wk"))
+        act(R("kblk"), R("blk"), F.Copy, scale=R("wk"))
+        act(R("idn"), R("idp"), F.Copy, scale=-16384.0)
+        act(R("blkf"), R("blk"), F.Copy)
+        lin(R("tk"), R("tk0"), None, row)
+        act(R("mle"), R("se0"), F.Relu, None, R("mb"))
+        for i, (a, b) in enumerate(((1, 3), (2, 2))):
+            lin(R("wq", i, i + 1), R("sc", a, a + 1), R("sc", 6 + b, 7 + b), HALF)
+        lin(R("wm"), R("wq"), None, MAGIC)
+        lin(R("w"), R("wm"), None, -MAGIC)
+        lin(R("wb"), R("w", 0, 1), 2.0, R("w", 1, 2))
+        lin(R("by1", 1, 2), R("w", 1, 2), -8388608.0, -2048.0)
+        lin(R("by1", 2, 3), R("w", 1, 2), 8388608.0, -2048.0)
+        lin(R("k1"), R("wb"), 4096.0)
+        lin(R("by1", 0, 1), R("wb"), -8388608.0, -2048.0)
+        lin(R("by1", 3, 4), R("wb"), 8388608.0, -2048.0)
+        lin(R("bx1"), R("by1"), -1.0)
 
-    def gap0a():
-        cp(R("onx", 16, 144, 16), R("blk", 0, 128, 16))
-        ts(R("kwx", 16, 144, 16), R("blk", 0, 128, 16), R("wk"), None, A.mult)
-        ts(R("kblk"), R("blk"), R("wk"), None, A.mult)
+    build(0, B, gap0, gap1, gap2, gap3)
+    sent0, got0 = send(0, nothing, nothing)
 
-    sent0, got0 = send(0, gap0a, lambda: None)
-
-    iota(R("z16"), [[0, 16]], 0)
-    iota(R("tk0"), [[16, 24]], 2 * M)
-    sel(R("stri"), R("blk"), [[1, 128]], A.is_ge, -1, -1)
-    sel(R("nb"), R("mob"), [[-16, 8], [0, 16]], A.is_ge, 0, 1)
-    sel(R("nblk"), R("nb"), [[16, 8], [0, 16]], A.is_ge, 15, -1)
-    sel(R("neg"), R("nblk"), [[-1, 128]], A.is_ge, 0, 1)
-    iota(R("one"), [[0, 384]], 1)
-    iota(R("bk", B, B + 4 * M), [[0, 4 * M]], 0)
-    for h in ("hx1", "hy1"):
-        iota(R(h, 0, 768, 3), [[0, 256]], -4096)
-    iota(R("tb0"), [[16, 24]], J + 16)
     for o in range(N):
         iota(clear(o), [[0, CAP]], 0)
-    fill(R("tx"), 0.0)
-    cp(R("laf", 256, 512), R("la", 256, 512))
-    cp(R("lbf", 256, 512), R("lb", 256, 512))
-    fill(R("tbl", J, J + 16), 1)
-    fill(R("q1"), 1.0 / 4096)
-    fill(R("b75"), B / 4096.0)
-    fill(R("bia"), BIAS)
-    fill(R("b4"), B + BIAS)
-    pairs(2, ((1, 3), (2, 2)))
-    cp(R("lcf", 256, 512), R("lc", 256, 512))
-    ts(R("w", 2, 4), R("wq", 2, 4), MAGIC, MAGIC, A.add, A.subtract)
-    ts(R("tk"), R("tk0"), row, None, A.add)
-    spread("tx", "stri")
-    for who, half in (("x", 0), ("y", 1), ("y", 0), ("x", 1)):
-        for i in range(3):
-            if step(1, who, half, i)[0] < 4:
-                affine(1, who, half, i)
-    ts(R("wb"), R("w", 2, 3), 2.0, R("w", 3, 4), A.mult, A.add)
-    ts(R("by1", 1, 2), R("w", 3, 4), -8388608.0, -2048.0, A.mult, A.add)
-    ts(R("by1", 2, 3), R("w", 3, 4), 8388608.0, -2048.0, A.mult, A.add)
-    ts(R("k1"), R("wb"), 4096.0, None, A.mult)
-    ts(R("by1", 0, 1), R("wb"), -8388608.0, -2048.0, A.mult, A.add)
-    ts(R("by1", 3, 4), R("wb"), 8388608.0, -2048.0, A.mult, A.add)
-    ts(R("bx1"), R("by1"), -1.0, None, A.mult)
+    iota(R("ud"), [[0, M]], LIFT)
+    for name in ("la", "lb", "lc"):
+        cp(R(name + "f", 256, 512), R(name, 256, 512))
 
-    keep(0, None)
+    def old_classes():
+        for who, half in (("x", 0), ("y", 0), ("y", 1), ("x", 1)):
+            for i in range(3):
+                if step(1, who, half, i)[0] < 4:
+                    affine(1, who, half, i)
 
+    keep(0, old_classes)
+
+    act(R("n4"), P(5, 200, 201), F.Copy)
+    ts(R("scx1"), R("w0"), 8192.0, R("k1"), A.mult, A.add)
     hmask(1, "x", 0)
+    lin(R("n4q"), R("n4"), 1.0 / 4096)
+    lin(R("scy1"), R("scx1"), -1.0)
     affine(1, "y", 0, 0)
     hmask(1, "y", 0)
-    act(R("tq"), R("n4"), F.Identity, scale=R("q1"), bias=R("b75"))
+    hmask(1, "y", 1)
+    rooms(None)
     places(1, "x", 0)
     act(quarter("sv", 0), col("x", 0, B), F.Copy)
-    hmask(1, "y", 1)
-    act(R("zf"), R("lcf", 256, 512), F.Identity, scale=R("tq"), bias=R("bia"))
+    lin(R("tq"), R("n4"), 1.0 / 4096, B / 4096.0)
+    lin(R("zf"), R("lcf", 256, 512), R("tq"), BIAS)
     affine(1, "x", 1, 0)
     hmask(1, "x", 1)
     append(0)
     places(1, "y", 0)
-    places(1, "y", 1)
-    ts(R("lz"), R("zf"), MAGIC, MAGIC - MID, A.add, A.subtract)
-    places(1, "x", 1)
-    build(1, B + M, lambda: None, lambda: None, lambda: None)
 
-    def gap1a():
-        cp(R("ud"), R("one"))
-        ts(R("tb"), R("tb0"), row, None, A.add)
+    def taken():
         ts(R("bm"), R("kb2"), float(J), None, A.min)
-
-    def gap1b():
-        tt(R("tn2"), R("nk"), R("tb"), A.mult)
-        tt(R("om2"), R("tn2"), R("bm"), A.max)
+        tt(R("om2"), R("tn"), R("bm"), A.max)
         cp(R("mo2"), R("om2"))
 
-    sent1, got1 = send(1, gap1a, gap1b)
-    scatter(R("tbl"), R("mo2"), R("ud"))
+    build(1, B + M, nothing, nothing, nothing, nothing)
+    sent1, got1 = send(1, taken, nothing)
+    act(X(R("tbl"), R("mo2")), R("ud"), F.Silu)
 
-    keep(1, R("n4"))
+    keep(1, nothing)
+    rooms(R("n4"))
     append(1)
     dma("y", "d_y", ext(T.y[:, :]), R("bk", B, B + 2 * M))
 

@@ -1,7 +1,7 @@
 from concourse.bass import DstId, RemoteDMATransfer
 from concourse.mybir import AluOpType as A, ActivationFunctionType as F
 
-F32, BF, I32, U16 = "float32", "bfloat16", "int32", "uint16"
+F32, BF, F16, I32, U16 = "float32", "bfloat16", "float16", "int32", "uint16"
 B, J, CAP, N = 3072, 4096, 96, 4
 M = N * CAP
 MAGIC = 12582912.0
@@ -15,7 +15,8 @@ OWN = 4128
 TRASH = 2 * OWN
 WIN = TRASH + 544
 BIG = 16384.0
-LIFT = 32
+LIFT = 1024
+OWN_ROWS = 16
 STEP = 1.0 / 32
 
 SCRATCH = {}
@@ -23,32 +24,33 @@ ALIAS, COLS, SIZE = {}, {}, {F32: 0, BF: 0, I32: 0}
 for _n, _c, _d in [
     ("nl", 8, I32), ("nf", 10, F32), ("sc", 10, F32), ("ub", 8, F32), ("wi", 2, I32), ("wf", 2, F32), ("wq", 2, F32), ("wm", 2, F32), ("w", 2, F32),
     ("one8", 128, F32), ("b8a", 128, F32), ("b8", 128, F32), ("blkf", 128, F32),
-    ("pid", 1, I32), ("ri", 2, I32), ("rf", 2, F32), ("wk", 1, F32), ("w4", 1, F32), ("srow", 1, F32), ("krow", 1, F32), ("kneg", 1, F32),
-    ("lh", 8, F32), ("lo", 1, F32), ("hi", 1, F32), ("bse", 1, F32), ("bmk", 2, F32), ("sb", 1, F32), ("mb", 1, F32),
+    ("pid", 1, I32), ("ri", 3, I32), ("rf", 3, F32), ("wk", 1, F32), ("w4", 1, F32), ("wz", 1, F32), ("srow", 1, F32), ("krow", 1, F32), ("hk", 1, F32),
+    ("lh", 8, F32), ("lo", 1, F32), ("hi", 1, F32), ("bse", 1, F32), ("bmk", 2, F32), ("mb", 1, F32), ("c0", 1, F32), ("nkf", 24, F32),
     ("jc0", 256, F32), ("jc", 256, F32), ("tk0", 24, F32), ("tk", 24, F32),
     ("i68", 68, F32), ("n68", 68, F32), ("trs0", 68, F32), ("trs", 68, F32), ("se0", M, F32),
     ("ob", 128, BF), ("ba", 128, BF), ("blk", 128, BF), ("nb", 128, BF), ("nst", 128, BF), ("tra", 128, BF), ("trin", 128, BF), ("neg", 128, BF),
-    ("kblk", 128, BF), ("mob", 128, BF), ("idp", 128, BF), ("idm", 128, BF), ("idn", 128, BF), ("z16", 16, BF), ("cb", 128, BF),
-    ("wts", 4 * 144, BF), ("wca", 144, BF), ("wc", 144, BF),
+    ("kblk", 128, BF), ("mob", 128, BF), ("idp", 128, BF), ("idm", 128, BF), ("idn", 128, BF), ("cb0", 128, BF), ("cb1", 128, BF),
+    ("wts", 5 * 144, BF), ("wca", 144, BF), ("wc", 144, BF),
     ("r1", 68, BF), ("r2", 68, BF), ("r3", 68, BF), ("ra0", 68, BF), ("rb0", 68, BF), ("btab", 68, BF), ("rst", 128, BF), ("ctab", 512, BF),
-    ("selm", M, BF), ("mle", M, BF), ("stp", CAP, F32), ("one", 24, BF), ("ud", M, F32), ("ui", 256, I32), ("uf", 256, F32),
+    ("mle", M, BF), ("stp", CAP, F32), ("one", 24, BF), ("ud", M, BF), ("ui", 256, I32), ("uf", 256, BF),
     ("bx0", 4, F32), ("by0", 4, F32), ("bx1", 4, F32), ("by1", 4, F32), ("wb", 1, F32), ("k1", 1, F32),
     ("scx0", 1, F32), ("scy0", 1, F32), ("scx1", 1, F32), ("scy1", 1, F32),
     ("n4", 1, F32), ("n4q", 1, F32), ("tq", 1, F32), ("w0", 1, I32), ("ksum", 1, F32),
     ("la", 512, I32), ("lb", 512, I32), ("lc", 512, I32), ("laf", 512, F32), ("lbf", 512, F32), ("lcf", 512, F32),
-    ("ux0", 512, F32), ("uy0", 512, F32), ("ux1", 768, F32), ("uy1", 768, F32),
-    ("hx0", 512, BF), ("hy0", 512, BF), ("hx1", 768, BF), ("hy1", 768, BF), ("sox", 768, F32), ("soy", 768, F32),
+    ("ux0", 512, F32), ("uy0", 512, F32), ("ux1", 768, F16), ("uy1", 768, F16), ("rawx", 768, F32), ("rawy", 768, F32),
+    ("hx0", 512, BF), ("hy0", 512, BF), ("hx1", 768, BF), ("hy1", 768, BF),
+    ("sox0", 512, F32), ("soy0", 512, F32), ("sox1", 768, F16), ("soy1", 768, F16),
     ("zf", 256, F32), ("lx", 256, U16), ("ly", 256, U16), ("lz", 256, U16),
     ("bk", B + SPARE + 2 * M, BF), ("sv", 3072, BF), ("xv", 1024, BF), ("xa", 1024, BF), ("fv", J, BF), ("cand", J + 16, BF),
-    ("cl", 128, I32), ("dd", 128, BF), ("ind", 1024, BF), ("ab", 256, BF), ("t1", 128, BF), ("t2", 128, BF), ("t3", 128, BF), ("of", 68, F32), ("off", 68, U16),
-    ("vin0", 528, F32), ("vin1", 528, F32), ("win0", WIN, F32), ("win1", WIN, F32), ("sx", M, F32), ("fr", M, BF), ("sj", M, F32),
+    ("cl", 128, F16), ("ind", 1024, BF), ("ab", 256, BF), ("t1", 128, BF), ("t2", 128, BF), ("t3", 128, BF), ("of", 68, F32), ("off", 68, U16),
+    ("vin0", 528, F32), ("vin1", 528, F32), ("win0", WIN, F32), ("win1", WIN, F32), ("fr", M, F16),
     ("jl", 24, U16), ("snd0", 288, BF), ("snd1", 288, BF), ("arr0", M, BF), ("arr1", M, BF),
     ("ki", 24, I32), ("kb", 24, I32), ("kf", 24, F32), ("kb2", 24, I32), ("bm", 24, F32), ("bo", 24, U16), ("fl", M, BF), ("r16", M, U16),
-    ("tbl", SPARE + M, F32), ("us", M, BF), ("dm", M, BF),
+    ("tbl", SPARE + M, BF), ("us", M, BF), ("dm", M, BF),
     ("nk", 24, BF), ("kp", 24, BF), ("ks", 24, BF), ("tn", 24, F32), ("om", 24, F32), ("mo", 24, U16), ("om2", 24, F32), ("mo2", 24, U16),
 ]:
     COLS[_n] = _c
-    if _c <= 128 and _d != U16 and _n != "nl":
+    if _c <= 128 and _d in SIZE and _n != "nl":
         ALIAS[_n] = ({F32: "pf", BF: "pb", I32: "pi"}[_d], SIZE[_d])
         SIZE[_d] += -(-_c // 8) * 8
     else:
@@ -57,6 +59,7 @@ SCRATCH["pf"] = ("sbuf", [128, SIZE[F32]], F32)
 SCRATCH["pb"] = ("sbuf", [128, SIZE[BF]], BF)
 SCRATCH["pi"] = ("sbuf", [128, SIZE[I32]], I32)
 SCRATCH["eq"] = ("sbuf", [128, 24, M], BF)
+SCRATCH["far"] = ("sbuf", [128, 24 - OWN_ROWS, M - 16 * OWN_ROWS], BF)
 for _n in range(8):
     SCRATCH["ps%d" % _n] = ("psum", [128, 512], F32)
 
@@ -222,12 +225,12 @@ def rank_program(g, core, T, topo):
         return (ap, [])
 
     def W(name, a, b, st=1):
-        o = 144 * ("mx", "onx", "kwx", "zero").index(name)
+        o = 144 * ("mx", "zx", "onx", "kwx", "zero").index(name)
         return R("wts", o + a, o + b, st)
 
-    def listify(o, wname, src):
+    def listify(o, wname, src, a=0, b=M):
         for x in range(16):
-            mm(o, W(wname, 16 - x, 144 - x), R(src, x, M, 16), x == 0, x == 15)
+            mm(o, W(wname, 16 - x, 144 - x), R(src, a + x, b, 16), x == 0, x == 15)
 
     def P(k, a, b, st=1, rows=None):
         return R("ps%d" % k, a, b, st, rows)
@@ -257,7 +260,7 @@ def rank_program(g, core, T, topo):
     iota(R("jc0"), [[16, 256]], -2048)
     sel(R("ba"), R("ob"), [[-16, 8], [0, 16]], A.is_ge, 0, 1)
     sel(R("blk"), R("ba"), [[16, 8], [0, 16]], A.is_ge, 15, -1)
-    for i, bits in enumerate((15, 7)):
+    for i, bits in enumerate((15, 7, 1)):
         ts(R("ri", i, i + 1), R("pid"), bits, None, A.bitwise_and)
     fill(R("wts"), 0.0)
     cp(R("rf"), R("ri"))
@@ -268,16 +271,17 @@ def rank_program(g, core, T, topo):
     fill(R("nst"), -STEP)
     ts(R("srow"), row, 8.0, None, A.is_lt)
     ts(R("krow"), row, 8.0, None, A.is_ge)
-    ts(R("w4"), row, 3.5, 2.25, A.mult, A.add)
+    ts(R("w4"), R("rf", 2, 3), -0.5, 0.25, A.mult, A.add)
     ts(R("bmk", 0, 1), R("rf", 1, 2), 7.0, BIG, A.not_equal, A.mult)
     fill(R("stp"), STEP)
     ts(R("bse"), R("krow"), float(OWN), None, A.mult)
-    ts(R("cb"), R("ob"), R("krow"), -0.375, A.mult, A.mult)
+    ts(R("cb1"), R("ob"), R("krow"), -0.375, A.mult, A.mult)
     ts(R("btab"), R("ob", 0, 68), R("bse"), None, A.mult)
-    ts(R("jc"), R("jc0"), row, None, A.add)
-    lin(R("wk"), row, 14.0, 9.0)
-    lin(R("sb"), row, 32768.0, 32768.0)
-    lin(R("mb"), row, -1.0, 1.0)
+    lin(R("jc"), R("jc0"), None, row)
+    ts(R("wz"), R("w4"), 1.0, None, A.add)
+    ts(R("c0"), R("krow"), 3576.0, -2040.0, A.mult, A.add)
+    lin(R("hk"), R("krow"), 6040.0, -2040.0)
+    act(R("cb0"), R("ob"), F.Copy, scale=R("c0"))
     lin(R("btab", 32, 68, 34), R("ob", 0, 2), R("bmk", 0, 1), R("bse"))
 
     cp(R("nf", 0, 6, rows=first8), R("nl", 0, 6, rows=first8))
@@ -285,6 +289,7 @@ def rank_program(g, core, T, topo):
     mm(P(7, 0, 10), R("b8", rows=first8), R("nf", rows=first8), True, True)
     act(W("mx", 8, 136, 16), R("blk", 0, 128, 16), F.Copy)
     act(W("mx", 16, 144, 16), R("blk", 0, 128, 16), F.Copy, scale=R("w4"))
+    act(W("zx", 16, 144, 16), R("blk", 0, 128, 16), F.Copy, scale=R("wz"))
     cp(R("lbf", 0, 256), R("lb", 0, 256))
     for i, (a, b) in enumerate(((0, 3), (1, 2))):
         ts(R("wi", i, i + 1), P(7, a, a + 1), P(7, 6 + b, 7 + b), HALF, A.mult, A.add)
@@ -308,7 +313,7 @@ def rank_program(g, core, T, topo):
         sc_, bi = R("sc", 6 + k, 7 + k) if k < 4 else R("n4q"), R("ub", k, k + 1)
         name, a = "l" + ("a" if who == "x" else "b"), 256 * t + 128 * half
         if q == "s":
-            lin(R("u%s%d" % (who, t), *cols), R(name + "f", a, a + 128), sc_, bi)
+            lin(R("raw" + who if t and k < 4 else "u%s%d" % (who, t), *cols), R(name + "f", a, a + 128), sc_, bi)
         else:
             ts(R("u%s%d" % (who, t), *cols), R(name, a, a + 128), sc_, bi, A.mult, A.add)
 
@@ -321,11 +326,19 @@ def rank_program(g, core, T, topo):
             else:
                 ts(*x, A.mult, A.add)
 
-    def places(t, who, half):
+    def places(t, *lists, between=None):
         m = 2 + t
-        a, b = 128 * m * half, 128 * m * (half + 1)
-        scan(R("so" + who, a, b), R("h%s%d" % (who, t), a, b), R("u%s%d" % (who, t), a, b), A.min, A.max)
-        ts(R("l" + who, 128 * half, 128 * half + 128), R("so" + who, a + m - 1, b, m), MAGIC, MAGIC - MID, A.add, A.subtract)
+        for who, half in lists:
+            a, b = 128 * m * half, 128 * m * (half + 1)
+            scan(R("so%s%d" % (who, t), a, b), R("h%s%d" % (who, t), a, b), R("u%s%d" % (who, t), a, b), A.min, A.max)
+        if between:
+            between()
+        for who, half in lists:
+            a, b = 128 * m * half, 128 * m * (half + 1)
+            ts(R("l" + who, 128 * half, 128 * half + 128), R("so%s%d" % (who, t), a + m - 1, b, m), MAGIC, MAGIC - MID, A.add, A.subtract)
+
+    def place_z():
+        ts(R("lz"), R("zf"), MAGIC, MAGIC - MID, A.add, A.subtract)
 
     def quarter(name, q):
         return R(name, 1024 * q, 1024 * q + 1024)
@@ -340,20 +353,28 @@ def rank_program(g, core, T, topo):
         c, d = 1024 * q + 16 * a, 1024 * q + 16 * b
         tt(R("cand", c, d), X(R("bk", 0, wid), R("lz", 64 * q + a, 64 * q + b)), R("fv", c, d), A.min)
 
-    def sums(q, k):
-        mm(P(k, 0, 128), R("idp"), R("cb"), True, False)
+    def centre():
+        for i in range(2):
+            mm(P(0, 0, 128), R("idp"), R("cb%d" % i), i == 0, False)
+
+    def apart(q):
         for x in range(16):
             c = 64 * (x // 8)
-            mm(P(k, c, c + 64), W("mx", 8 - x % 8, 136 - x % 8), R("cand", 1024 * q + x, 1024 * q + 1024, 16), False, x == 15)
+            mm(P(0, c, c + 64), W("mx", 8 - x % 8, 136 - x % 8), R("cand", 1024 * q + x, 1024 * q + 1024, 16), False, x == 15)
+
+    def joined(q, k):
+        for x in range(16):
+            mm(P(k, 0, 64), W("zx", 16 - x, 144 - x), R("cand", 1024 * q + x, 1024 * q + 1024, 16), x == 0, False)
 
     owners = [(rank + 1 + i) % N for i in range(N)]
     low64 = slice(0, 64)
 
-    def judge(k):
-        ts(R("cl"), P(k, 0, 128), R("lo"), R("hi"), A.max, A.min)
-        tt(R("dd"), P(k, 0, 128), R("cl"), A.subtract)
-        mm(P(4, 0, 64), R("wc", 8, 136), R("dd", 0, 64), True, False)
-        mm(P(4, 0, 64), R("wc", 0, 128), R("dd", 64, 128), False, True)
+    def judge(k, more=True):
+        ts(R("cl"), P(0, 0, 128), R("lo"), R("hi"), A.max, A.min)
+        mm(P(k, 0, 64), R("wc", 8, 136), R("cl", 0, 64), False, False)
+        mm(P(k, 0, 64), R("wc", 0, 128), R("cl", 64, 128), False, True)
+        if more:
+            centre()
 
     def count_cols(q):
         for o in range(N):
@@ -365,12 +386,12 @@ def rank_program(g, core, T, topo):
             for s in (2 * q, 2 * q + 1):
                 mm(P(6 + w, 8 * (o % 2) + s, 512, 16), R("trin"), seg(o, s), False, last and o % 2 == 1 and s % 2 == 1)
 
-    def mark(q, who="v"):
+    def mark(q, k, who="v"):
         for i, p in enumerate(owners):
             if who == "v":
-                ts(R("ind", 256 * q + 64 * i, 256 * q + 64 * i + 64), P(4, 0, 64), p / 4 - 0.375, None, A.is_equal)
+                ts(R("ind", 256 * q + 64 * i, 256 * q + 64 * i + 64), P(k, 0, 64), 504 + p / 4, None, A.is_equal)
             else:
-                act(R("ab", 64 * i, 64 * i + 64), P(4, 0, 64), F.Abs, None, 0.375 - p / 4)
+                act(R("ab", 64 * i, 64 * i + 64), P(k, 0, 64), F.Abs, None, -504 - p / 4)
         if who == "s":
             act(R("ind", 256 * q, 256 * q + 256), R("ab"), F.Relu, -4.0, 1.0)
 
@@ -390,16 +411,15 @@ def rank_program(g, core, T, topo):
 
     def build(t, wid, gap0, gap1, gap2, gap3):
         act(quarter("sv", 1), col("x", 1, B), F.Copy)
-        places(t, "y", 1)
         first(0, wid)
         act(quarter("fv", 3), col("y", 3, B), F.Copy)
-        ts(R("lz"), R("zf"), MAGIC, MAGIC - MID, A.add, A.subtract)
         gap0()
-        places(t, "x", 1)
         third(0, wid)
-        sums(0, 0)
+        centre()
         for w in range(2):
             mm(P(6 + w, 0, 512), R("idp"), R("ctab"), True, False)
+        apart(0)
+        joined(0, 4)
         act(R("xa"), col("x", 3, wid), F.Copy)
         add(quarter("fv", 3), R("xa"), "d_add%d" % t)
         act(quarter("sv", 2), col("y", 2, B), F.Copy)
@@ -413,36 +433,38 @@ def rank_program(g, core, T, topo):
 
         first(1, wid)
         gap1()
-        judge(0)
+        judge(4)
         gather_x2(0)
-        differ(0)
-        mark(0, "s")
         gather_x2(1)
         third(1, wid)
-        counts(0)
-        sums(1, 1)
+        differ(0)
+        apart(1)
         differ(1)
         for h in range(2):
             act(R("fv", 2048 + 512 * h, 2560 + 512 * h), P(2 + h, 0, 512), F.Abs)
-        gap2()
-        third(3, wid)
-        sums(3, 0)
+        joined(1, 1)
+        mark(0, 4)
+        third(3, wid, 0, 32)
         judge(1)
-        mark(1, "s")
+        counts(0)
+        mark(1, 1, "s")
+        third(3, wid, 32, 64)
+        apart(3)
+        joined(3, 4)
         third(2, wid, 0, 32)
-        judge(0)
+        judge(4)
         counts(1)
+        mm(P(2, 0, 68), R("idp"), R("btab"), True, False)
         gap3()
         third(2, wid, 32, 64)
-        sums(2, 1)
-        mark(3)
-        count_cols(3)
-        prefix(3, 0, False)
-        judge(1)
-        prefix(3, 1, False)
-        mark(2)
+        apart(2)
+        joined(2, 1)
+        mark(3, 4)
+        judge(1, False)
+        gap2()
+        counts(3)
+        mark(2, 1)
         count_cols(2)
-        mm(P(2, 0, 68), R("idp"), R("btab"), True, False)
         prefix(2, 0, True)
         prefix(2, 1, True)
 
@@ -462,20 +484,17 @@ def rank_program(g, core, T, topo):
 
         def slots(a, b, k):
             for o in range(a, b):
-                scan(R("sx", CAP * o, CAP * o + CAP), R("stp"), R("win%d" % (o // 2), OWN * (o % 2), OWN * (o % 2) + CAP), A.add, A.max)
-            ts(R("fr", CAP * a, CAP * b), R("sx", CAP * a, CAP * b), MAGIC, MAGIC + LIFT, A.add, A.subtract)
-            mm(P(k, CAP * a, CAP * b), R("blk"), R("fr", CAP * a, CAP * b), True, True)
+                scan(R("fr", CAP * o, CAP * o + CAP), R("stp"), clear(o), A.add, A.max)
+            listify(P(k, 6 * a, 6 * b), "onx", "fr", CAP * a, CAP * b)
 
         def pick(a, b, k):
-            scan(R("sj", CAP * a, CAP * b), R("selm", CAP * a, CAP * b), P(k, CAP * a, CAP * b), A.max, A.min)
-            ts(R("jl", 6 * a, 6 * b), R("sj", CAP * a + 15, CAP * b, 16), float(J), None, A.min)
+            ts(R("jl", 6 * a, 6 * b), P(k, 6 * a, 6 * b), -16.0 * LIFT, float(J), A.add, A.min)
 
-        slots(0, 2, 3)
-        slots(2, 3, 2)
-        pick(0, 2, 3)
-        act(R(snd, 0, 192), X(R("cand"), R("jl", 0, 12)), F.Copy)
-        pick(2, 3, 2)
-        cp(R(snd, 192, 288), X(R("cand"), R("jl", 12, 18)))
+        slots(0, 3, 3)
+        slots(3, 4, 2)
+        pick(0, 3, 3)
+        cp(R(snd, 0, 160), X(R("cand"), R("jl", 0, 10)))
+        act(R(snd, 160, 288), X(R("cand"), R("jl", 10, 18)), F.Copy)
         mine = plan(core, cores, topo)
         src = [R(snd, CAP * i, CAP * i + CAP) for i in range(N - 1)]
         prepare("g", [], [x for s in src for x in s[1]])
@@ -486,9 +505,8 @@ def rank_program(g, core, T, topo):
             tr.append(RemoteDMATransfer(dst_ids=[DstId(rid=rid, pnc=pid)], dma_engine_mask=sum(1 << e for e in mine[d]),
                                         remote_sem=T.sem["arrv%d" % t], src=src[i][0], dst=T[arr][:, CAP * rank:CAP * rank + CAP]))
         g.remote_dma_fused(tr, local_sem=T.sem["snt%d" % t])
-        slots(3, 4, 3)
+        pick(3, 4, 2)
         gap1()
-        pick(3, 4, 3)
         gap2()
         act(R(arr, CAP * rank, CAP * rank + CAP), X(R("cand"), R("jl", 18, 24)), F.Copy)
         total = sum(len(plan(c, cores, topo)[core]) for c in cores if c != core)
@@ -499,11 +517,11 @@ def rank_program(g, core, T, topo):
                 wrote.setdefault(arr, []).append((range(CAP * q, CAP * q + CAP), tok))
         return sum(len(e) for e in mine.values()), total
 
-    def keep(t, meanwhile):
+    def keep(t):
         arr = "arr%d" % t
         mm(P(2, 0, M), R("kblk"), R(arr), True, True)
-        mm(P(6, 0, M), R("kblk"), R(arr), True, False)
         listify(P(3, 0, 24), "kwx", arr)
+        mm(P(6, 0, M), R("kblk"), R(arr), True, False)
         lin(R("fl"), P(2, 0, M), 1.0 / 16384, 128.5 + 1.0 / 32768)
         mm(P(6, 0, M), R("idn"), R("fl"), False, True)
         cp(R("ki"), P(3, 0, 24))
@@ -512,16 +530,29 @@ def rank_program(g, core, T, topo):
         ts(R("kb2"), R("kb"), 2, None, A.arith_shift_right)
         ts(R("r16"), P(6, 0, M), 129.0 * 16384, None, A.add)
         ts(R("bo"), R("kb2"), J, None, A.min)
+        lin(R("nkf"), R("kf"), -1.0, 129.0 * 16384)
+
+        def rows(name, a, b, c, d):
+            return (T[name][:, a, c:d] if b == a + 1 else T[name][:, a:b, c:d], [(name, range(M * a, M * b))])
+
+        for q in range(OWN_ROWS, 24):
+            act(rows("far", q - OWN_ROWS, q - OWN_ROWS + 1, 0, M - 16 * q), P(6, 16 * q, M), F.Abs, None, R("nkf", q, q + 1))
+        for a in range(OWN_ROWS, 24, 4):
+            act(rows("eq", a, a + 4, 0, M - 16 * a), rows("far", a - OWN_ROWS, a - OWN_ROWS + 4, 0, M - 16 * a), F.Relu, -1.0, 1.0)
         act(R("us"), X(R("tbl", 0, J + 16), R("bo")), F.Copy)
-        meanwhile()
         mm(P(0, 0, M), W("zero", 0, 128), R("mle"), True, False)
-        for q in range(24):
-            n = M - 16 * q
-            ts((T.eq[:, q, 0:n], [("eq", range(M * q, M * q + n))]), R("r16", 16 * q, M), R("kf", q, q + 1), None, A.is_equal)
-            if q < 23:
-                mm(P(0, 16 * q + 16, M), R("blk"), (T.eq[:, q, 16:n], [("eq", range(M * q, M * q + n))]), False, False)
-            if q == 8:
+
+        def earlier(q):
+            mm(P(0, 16 * q + 16, M), R("blk"), rows("eq", q, q + 1, 16, M - 16 * q), False, False)
+
+        for q in range(OWN_ROWS):
+            ts(rows("eq", q, q + 1, 0, M - 16 * q), R("r16", 16 * q, M), R("kf", q, q + 1), None, A.is_equal)
+            if q == OWN_ROWS - 4:
+                for p in range(OWN_ROWS, 23):
+                    earlier(p)
+            if q == OWN_ROWS - 1:
                 mm(P(0, 0, M), R("idp"), R("us"), False, False)
+            earlier(q)
         mm(P(0, 0, M), R("idp"), (T.eq[:, :, 0:16], [("eq", range(0, 24 * M))]), False, True)
         tt(R("dm"), P(0, 0, M), R("mle"), A.mult)
         listify(P(1, 0, 24), "onx", "dm")
@@ -557,19 +588,18 @@ def rank_program(g, core, T, topo):
         hmask(0, "y", half)
         for i in range(2):
             affine(0, "y", half, i)
-    hmask(0, "x", 1)
-    places(0, "x", 0)
+    places(0, ("x", 0), between=lambda: affine(0, "x", 1, 0, "v"))
     act(quarter("sv", 0), col("x", 0, B), F.Copy)
+    affine(0, "x", 1, 1, "v")
+    hmask(0, "x", 1, "v")
+    places(0, ("y", 0), ("y", 1), ("x", 1))
     ts(R("zf"), R("lc", 0, 256), B / 4096.0, BIAS, A.mult, A.add)
-    places(0, "y", 0)
-    for i in range(2):
-        affine(0, "x", 1, i, "v")
     ts(R("lh", 0, 1), R("sc", 4, 5), R("sc", 5, 6), -5000.0, A.is_gt, A.mult)
-    ts(R("lo"), R("sc", 4, 5), R("srow"), R("krow"), A.mult, A.subtract)
+    ts(R("lo"), R("sc", 4, 5), -2040.0, R("srow"), A.add, A.mult)
     sel(R("idp"), R("ob"), [[-1, 128]], A.is_equal, 0, 1)
     iota(R("ctab"), [[1, 32], [0, 2], [32, 8]], 0)
-    sel(R("wca"), W("zero", 0, 144), [[-16, 9], [256, 2], [-1, 8]], A.not_equal, -256, 1, 1.0)
-    sel(R("wc"), R("wca"), [[-16, 9], [256, 2], [-1, 8]], A.not_equal, -264, 1, 1.0)
+    sel(R("wca"), W("zero", 0, 144), [[-16, 9], [256, 2], [-1, 8]], A.not_equal, -256, 1, -1.0)
+    sel(R("wc"), R("wca"), [[-16, 9], [256, 2], [-1, 8]], A.not_equal, -264, 1, -1.0)
     sel(R("tra"), R("nst"), [[1, 128]], A.is_ge, 0, -1)
     sel(R("trin"), R("tra"), [[-16, 8], [0, 16]], A.is_ge, 0, 1)
     iota(R("mob"), [[0, 128]], -1)
@@ -580,7 +610,8 @@ def rank_program(g, core, T, topo):
 
     def gap0():
         ts(R("lh", 1, 2), R("lh", 0, 1), R("sc", 5, 6), R("srow"), A.add, A.mult)
-        ts(R("hi"), R("krow"), 1000000.0, R("lh", 1, 2), A.mult, A.add)
+        place_z()
+        ts(R("hi"), R("lh", 1, 2), R("hk"), None, A.add)
 
     def gap1():
         blocks = [[32, 2], [0, 34]]
@@ -596,7 +627,7 @@ def rank_program(g, core, T, topo):
         for o in (0, 1):
             iota(clear(o), [[0, CAP]], 0)
         for w in range(2):
-            iota(R("vin%d" % w, 512, 528), [[0, 16]], 300)
+            iota(R("vin%d" % w, 512, 528), [[0, 16]], LIFT + 300)
         iota(R("cand", J, J + 16), [[0, 16]], NONE)
         iota(R("tbl", J, J + 16), [[0, 16]], 2)
         iota(R("one"), [[0, 24]], 1)
@@ -605,6 +636,10 @@ def rank_program(g, core, T, topo):
         iota(R("bk", B, B + 2 * M), [[0, 2 * M]], 0)
         for h in ("hx1", "hy1"):
             iota(R(h, 0, 768, 3), [[0, 256]], -4096)
+        iota(R("rawx", 384, 768, 3), [[0, 128]], 0)
+        iota(R("rawy", 0, 384, 3), [[0, 128]], 0)
+        for q in range(24 - OWN_ROWS):
+            iota((T.far[:, q, :], [("far", range(M * q, M * q + M))]), [[0, M - 16 * OWN_ROWS]], 1)
 
     def gap2():
         cp(R("uf"), R("ui"))
@@ -613,8 +648,9 @@ def rank_program(g, core, T, topo):
             dma("y", "d_used", R("tbl", 0, J, rows=slice(r, 128, 16)), R("uf"), 256)
 
     def gap3():
+        lin(R("wk"), row, 14.0, 9.0)
+        lin(R("mb"), row, -1.0, 1.0)
         lin(R("trs"), R("trs0"), None, row)
-        act(R("selm"), R("se0"), F.Relu, -32768.0, R("sb"))
         act(W("onx", 16, 144, 16), R("blk", 0, 128, 16), F.Copy)
         act(W("kwx", 16, 144, 16), R("blk", 0, 128, 16), F.Copy, scale=R("wk"))
         act(R("kblk"), R("blk"), F.Copy, scale=R("wk"))
@@ -639,46 +675,50 @@ def rank_program(g, core, T, topo):
 
     for o in range(N):
         iota(clear(o), [[0, CAP]], 0)
-    iota(R("ud"), [[0, M]], LIFT)
-    for name in ("la", "lb", "lc"):
+    iota(R("ud"), [[0, M]], 1)
+    for name in ("la", "lb"):
         cp(R(name + "f", 256, 512), R(name, 256, 512))
 
-    def old_classes():
-        for who, half in (("x", 0), ("y", 0), ("y", 1), ("x", 1)):
+    for who in "xy":
+        for half in range(2):
             for i in range(3):
                 if step(1, who, half, i)[0] < 4:
                     affine(1, who, half, i)
+        ts(R("u%s1" % who), R("raw" + who), MAGIC, MAGIC, A.add, A.subtract)
 
-    keep(0, old_classes)
+    keep(0)
 
     act(R("n4"), P(5, 200, 201), F.Copy)
     ts(R("scx1"), R("w0"), 8192.0, R("k1"), A.mult, A.add)
-    hmask(1, "x", 0)
+    hmask(1, "x", 0, "v")
     lin(R("n4q"), R("n4"), 1.0 / 4096)
     lin(R("scy1"), R("scx1"), -1.0)
     affine(1, "y", 0, 0)
     hmask(1, "y", 0)
     hmask(1, "y", 1)
-    rooms(None)
-    places(1, "x", 0)
+    tt(R("om"), R("tn"), P(4, 64, 88), A.max)
+    places(1, ("x", 0), between=lambda: cp(R("mo"), R("om")))
     act(quarter("sv", 0), col("x", 0, B), F.Copy)
     lin(R("tq"), R("n4"), 1.0 / 4096, B / 4096.0)
-    lin(R("zf"), R("lcf", 256, 512), R("tq"), BIAS)
     affine(1, "x", 1, 0)
     hmask(1, "x", 1)
     append(0)
-    places(1, "y", 0)
+    places(1, ("y", 0), ("y", 1))
+
+    def others():
+        ts(R("zf"), R("lc", 256, 512), R("tq"), BIAS, A.mult, A.add)
+        places(1, ("x", 1), between=place_z)
 
     def taken():
         ts(R("bm"), R("kb2"), float(J), None, A.min)
         tt(R("om2"), R("tn"), R("bm"), A.max)
         cp(R("mo2"), R("om2"))
 
-    build(1, B + M, nothing, nothing, nothing, nothing)
+    build(1, B + M, others, nothing, nothing, nothing)
     sent1, got1 = send(1, taken, nothing)
-    act(X(R("tbl"), R("mo2")), R("ud"), F.Silu)
+    scatter(R("tbl"), R("mo2"), R("ud"))
 
-    keep(1, nothing)
+    keep(1)
     rooms(R("n4"))
     append(1)
     dma("y", "d_y", ext(T.y[:, :]), R("bk", B, B + 2 * M))

@@ -10,29 +10,32 @@ MID = 1728
 BIAS = HALF - MID
 INV = 1048576
 NONE = 576
-SPARE = J + 16
+SPARE = 2 * M
 OWN = 4128
 TRASH = 2 * OWN
-WIN = TRASH + 544
-BIG = 16384.0
+WIN = TRASH + 704
+BIG = 32768.0
 LIFT = 1024
 OWN_ROWS = 16
 STEP = 1.0 / 32
+DROP = -2048.0
 
 SCRATCH = {}
 ALIAS, COLS, SIZE = {}, {}, {F32: 0, BF: 0, I32: 0}
 for _n, _c, _d in [
     ("nl", 8, I32), ("nf", 10, F32), ("sc", 10, F32), ("ub", 8, F32), ("wi", 2, I32), ("wf", 2, F32), ("wq", 2, F32), ("wm", 2, F32), ("w", 2, F32),
     ("one8", 128, F32), ("b8a", 128, F32), ("b8", 128, F32), ("blkf", 128, F32),
-    ("pid", 1, I32), ("ri", 3, I32), ("rf", 3, F32), ("wk", 1, F32), ("w4", 1, F32), ("wz", 1, F32), ("srow", 1, F32), ("krow", 1, F32), ("hk", 1, F32),
+    ("pid", 1, I32), ("ri", 4, I32), ("rf", 4, F32), ("bs4", 2, F32), ("wk", 1, F32), ("w4", 1, F32), ("wz", 1, F32), ("srow", 1, F32), ("krow", 1, F32), ("hk", 1, F32),
     ("lh", 8, F32), ("lo", 1, F32), ("hi", 1, F32), ("bse", 1, F32), ("bmk", 2, F32), ("mb", 1, F32), ("c0", 1, F32), ("nkf", 24, F32),
-    ("jc0", 256, F32), ("jc", 256, F32), ("tk0", 24, F32), ("tk", 24, F32),
-    ("i68", 68, F32), ("n68", 68, F32), ("trs0", 68, F32), ("trs", 68, F32), ("se0", M, F32),
+    ("jc0", 256, F32), ("jc", 256, F32), ("tk0", 24, F32), ("tk", 24, F16),
+    ("i36", 36, F32), ("n36", 36, F32), ("trs0", 33, F32), ("trs1", 36, F32), ("se0", M, F32),
     ("ob", 128, BF), ("ba", 128, BF), ("blk", 128, BF), ("nb", 128, BF), ("nst", 128, BF), ("tra", 128, BF), ("trin", 128, BF), ("neg", 128, BF),
-    ("kblk", 128, BF), ("mob", 128, BF), ("idp", 128, BF), ("idm", 128, BF), ("idn", 128, BF), ("cb0", 128, BF), ("cb1", 128, BF),
-    ("wts", 5 * 144, BF), ("wca", 144, BF), ("wc", 144, BF),
-    ("r1", 68, BF), ("r2", 68, BF), ("r3", 68, BF), ("ra0", 68, BF), ("rb0", 68, BF), ("btab", 68, BF), ("rst", 128, BF), ("ctab", 512, BF),
-    ("mle", M, BF), ("stp", CAP, F32), ("one", 24, BF), ("ud", M, BF), ("ui", 256, I32), ("uf", 256, BF),
+    ("kblk", 128, BF), ("mob", 36, BF), ("idp", 128, BF), ("idn", 128, BF), ("cb0", 128, BF), ("cb1", 128, BF), ("cen", 128, BF),
+    ("bdrop", 128, BF), ("idrop", 128, BF), ("before", 2048, BF), ("under", 16, F32), ("w8", 1, F32), ("s8", 1, F32),
+    ("wts", 6 * 144, BF), ("wca", 144, BF), ("wc", 144, BF),
+    ("r1", 36, BF), ("r2", 36, BF), ("r3", 36, BF), ("ra0", 36, BF), ("rb0", 36, BF), ("e1", 33, BF), ("e3", 33, BF), ("pick0", 128, BF), ("pick1", 128, BF),
+    ("bt0", 33, F32), ("btab0", 33, F16), ("btab1", 36, BF), ("rst0", 128, BF), ("rst1", 128, BF), ("ctab0", 512, BF), ("ctab1", 512, BF), ("half", 18, F16),
+    ("trow", M, F16), ("hold", M, BF), ("i16", 16, F32), ("stp", CAP, F32), ("ud", M, BF), ("ui", 256, I32), ("uf", 256, BF),
     ("bx0", 4, F32), ("by0", 4, F32), ("bx1", 4, F32), ("by1", 4, F32), ("wb", 1, F32), ("k1", 1, F32),
     ("scx0", 1, F32), ("scy0", 1, F32), ("scx1", 1, F32), ("scy1", 1, F32),
     ("n4", 1, F32), ("n4q", 1, F32), ("tq", 1, F32), ("w0", 1, I32), ("ksum", 1, F32),
@@ -41,13 +44,12 @@ for _n, _c, _d in [
     ("hx0", 512, BF), ("hy0", 512, BF), ("hx1", 768, BF), ("hy1", 768, BF),
     ("sox0", 512, F32), ("soy0", 512, F32), ("sox1", 768, F16), ("soy1", 768, F16),
     ("zf", 256, F32), ("lx", 256, U16), ("ly", 256, U16), ("lz", 256, U16),
-    ("bk", B + SPARE + 2 * M, BF), ("sv", 3072, BF), ("xv", 1024, BF), ("xa", 1024, BF), ("fv", J, BF), ("cand", J + 16, BF),
-    ("cl", 128, F16), ("ind", 1024, BF), ("ab", 256, BF), ("t1", 128, BF), ("t2", 128, BF), ("t3", 128, BF), ("of", 68, F32), ("off", 68, U16),
-    ("vin0", 528, F32), ("vin1", 528, F32), ("win0", WIN, F32), ("win1", WIN, F32), ("fr", M, F16),
+    ("bk", B + SPARE + 3 * M, BF), ("sv", 3072, BF), ("xv", 1024, BF), ("xa", 1024, BF), ("fv", J, BF), ("cand", J + 16, BF),
+    ("cl", 128, F16), ("ind", 1024, BF), ("ab", 256, BF), ("t1", 128, BF), ("t2", 128, BF), ("t3", 128, BF), ("of", 36, F32), ("off0", 33, U16), ("off1", 36, U16),
+    ("vin", 512, F32), ("vin0", 272, F32), ("vin1", 272, F32), ("win", 2 * WIN, F32), ("fr", M, F16),
     ("jl", 24, U16), ("snd0", 288, BF), ("snd1", 288, BF), ("arr0", M, BF), ("arr1", M, BF),
     ("ki", 24, I32), ("kb", 24, I32), ("kf", 24, F32), ("kb2", 24, I32), ("bm", 24, F32), ("bo", 24, U16), ("fl", M, BF), ("r16", M, U16),
-    ("tbl", SPARE + M, BF), ("us", M, BF), ("dm", M, BF),
-    ("nk", 24, BF), ("kp", 24, BF), ("ks", 24, BF), ("tn", 24, F32), ("om", 24, F32), ("mo", 24, U16), ("om2", 24, F32), ("mo2", 24, U16),
+    ("tbl", 11 * 3 * M, BF), ("us", M, BF), ("kr", M, F16), ("ks", M, F16), ("om", 24, F32), ("mo", 24, U16), ("om2", 24, F32), ("mo2", 24, U16),
 ]:
     COLS[_n] = _c
     if _c <= 128 and _d in SIZE and _n != "nl":
@@ -63,7 +65,7 @@ SCRATCH["far"] = ("sbuf", [128, 24 - OWN_ROWS, M - 16 * OWN_ROWS], BF)
 for _n in range(8):
     SCRATCH["ps%d" % _n] = ("psum", [128, 512], F32)
 
-DMAS = ["d_ncl", "d_lim", "d_la0", "d_lb0", "d_lc0", "d_la1", "d_lb1", "d_lc1", "d_bk", "d_ui", "d_used", "d_y", "d_add0", "d_add1"]
+DMAS = ["d_ncl", "d_lim", "d_la0", "d_lb0", "d_lc0", "d_la1", "d_lb1", "d_lc1", "d_bk", "d_ui", "d_used", "d_y", "d_add00", "d_add01", "d_add10", "d_add11"]
 SEMAPHORES = ["cv", "cs", "ct", "cg", "arrv0", "arrv1", "snt0", "snt1"] + DMAS
 
 
@@ -225,7 +227,7 @@ def rank_program(g, core, T, topo):
         return (ap, [])
 
     def W(name, a, b, st=1):
-        o = 144 * ("mx", "zx", "onx", "kwx", "zero").index(name)
+        o = 144 * ("mx", "zx", "onx", "kwx", "sgn", "zero").index(name)
         return R("wts", o + a, o + b, st)
 
     def listify(o, wname, src, a=0, b=M):
@@ -240,15 +242,15 @@ def rank_program(g, core, T, topo):
     dma("s", "d_lim", R("nl", 4, 6, rows=first8), ext(T.lim[:, :]))
     dma("y", "d_la0", R("la", 0, 256), ext(T.ra[:, 0:256]))
     dma("s", "d_lb0", R("lb", 0, 256), ext(T.rb[:, 0:256]))
-    dma("y", "d_lc0", R("lc", 0, 256), ext(T.rc[:, 0:256]))
     dma("y", "d_bk", R("bk", 0, B), ext(T.bank[:, :]))
+    dma("y", "d_lc0", R("lc", 0, 256), ext(T.rc[:, 0:256]))
     dma("y", "d_lb1", R("lb", 256, 512), ext(T.rb[:, 256:512]))
     dma("y", "d_la1", R("la", 256, 512), ext(T.ra[:, 256:512]))
     dma("y", "d_lc1", R("lc", 256, 512), ext(T.rc[:, 256:512]))
-    dma("y", "d_ui", R("ui"), ext(T.used[:, :]))
 
     def clear(o):
-        return R("win%d" % (o // 2), OWN * (o % 2), OWN * (o % 2) + CAP)
+        a = WIN * (o // 2) + OWN * (o % 2)
+        return R("win", a, a + CAP)
 
     fill(R("one8"), 1.0)
     fill(R("ob"), 1.0)
@@ -256,40 +258,40 @@ def rank_program(g, core, T, topo):
         act(clear(o), R("one8", 0, CAP), F.Silu, scale=0.0)
     iota(R("pid"), [[0, 1]], 0, 1)
     sel(R("b8a", rows=first8), R("one8", rows=first8), [[1, 128]], A.is_ge, 0, -16)
-    sel(R("b8", rows=first8), R("b8a", rows=first8), [[-1, 128]], A.is_ge, 15, 16)
-    iota(R("jc0"), [[16, 256]], -2048)
     sel(R("ba"), R("ob"), [[-16, 8], [0, 16]], A.is_ge, 0, 1)
+    sel(R("b8", rows=first8), R("b8a", rows=first8), [[-1, 128]], A.is_ge, 15, 16)
     sel(R("blk"), R("ba"), [[16, 8], [0, 16]], A.is_ge, 15, -1)
-    for i, bits in enumerate((15, 7, 1)):
+    iota(R("jc0"), [[16, 256]], -2048)
+    for i, bits in enumerate((15, 7, 1, 4)):
         ts(R("ri", i, i + 1), R("pid"), bits, None, A.bitwise_and)
     fill(R("wts"), 0.0)
     cp(R("rf"), R("ri"))
     row = R("rf", 0, 1)
     for h in ("hx0", "hy0"):
         fill(R(h, 0, 512, 2), -4096.0)
-    fill(R("ub", 0, 1), BIAS)
-    fill(R("nst"), -STEP)
-    ts(R("srow"), row, 8.0, None, A.is_lt)
     ts(R("krow"), row, 8.0, None, A.is_ge)
     ts(R("w4"), R("rf", 2, 3), -0.5, 0.25, A.mult, A.add)
+    ts(R("srow"), row, 8.0, None, A.is_lt)
     ts(R("bmk", 0, 1), R("rf", 1, 2), 7.0, BIG, A.not_equal, A.mult)
-    fill(R("stp"), STEP)
-    ts(R("bse"), R("krow"), float(OWN), None, A.mult)
-    ts(R("cb1"), R("ob"), R("krow"), -0.375, A.mult, A.mult)
-    ts(R("btab"), R("ob", 0, 68), R("bse"), None, A.mult)
+    fill(R("ub", 0, 1), BIAS)
+    fill(R("nst"), -STEP)
+    lin(R("bs4", 0, 1), R("rf", 3, 4), OWN / 4.0)
+    lin(R("wz"), R("w4"), None, 1.0)
+    lin(R("bse"), R("krow"), float(OWN))
+    lin(R("bs4", 1, 2), R("krow"), float(WIN), R("bs4", 0, 1))
+    act(W("mx", 8, 136, 16), R("blk", 0, 128, 16), F.Copy)
+    act(W("mx", 16, 144, 16), R("blk", 0, 128, 16), F.Copy, scale=R("w4"))
+    act(W("zx", 16, 144, 16), R("blk", 0, 128, 16), F.Copy, scale=R("wz"))
+    act(R("btab1"), R("ob", 0, 36), F.Copy, scale=R("bse"))
+    act(R("bt0"), R("ob", 0, 33), F.Copy, scale=R("bs4", 1, 2))
     lin(R("jc"), R("jc0"), None, row)
-    ts(R("wz"), R("w4"), 1.0, None, A.add)
-    ts(R("c0"), R("krow"), 3576.0, -2040.0, A.mult, A.add)
     lin(R("hk"), R("krow"), 6040.0, -2040.0)
-    act(R("cb0"), R("ob"), F.Copy, scale=R("c0"))
-    lin(R("btab", 32, 68, 34), R("ob", 0, 2), R("bmk", 0, 1), R("bse"))
+    lin(R("btab1", 16, 36, 18), R("ob", 0, 2), R("bmk", 0, 1), R("bse"))
 
     cp(R("nf", 0, 6, rows=first8), R("nl", 0, 6, rows=first8))
     ts(R("nf", 6, 10, rows=first8), R("nl", 0, 4, rows=first8), 1.0 / 4096, None, A.mult)
     mm(P(7, 0, 10), R("b8", rows=first8), R("nf", rows=first8), True, True)
-    act(W("mx", 8, 136, 16), R("blk", 0, 128, 16), F.Copy)
-    act(W("mx", 16, 144, 16), R("blk", 0, 128, 16), F.Copy, scale=R("w4"))
-    act(W("zx", 16, 144, 16), R("blk", 0, 128, 16), F.Copy, scale=R("wz"))
+    fill(R("stp"), STEP)
     cp(R("lbf", 0, 256), R("lb", 0, 256))
     for i, (a, b) in enumerate(((0, 3), (1, 2))):
         ts(R("wi", i, i + 1), P(7, a, a + 1), P(7, 6 + b, 7 + b), HALF, A.mult, A.add)
@@ -354,16 +356,15 @@ def rank_program(g, core, T, topo):
         tt(R("cand", c, d), X(R("bk", 0, wid), R("lz", 64 * q + a, 64 * q + b)), R("fv", c, d), A.min)
 
     def centre():
-        for i in range(2):
-            mm(P(0, 0, 128), R("idp"), R("cb%d" % i), i == 0, False)
+        mm(P(0, 0, 128), R("cen"), R("ob"), True, False)
 
     def apart(q):
         for x in range(16):
             c = 64 * (x // 8)
             mm(P(0, c, c + 64), W("mx", 8 - x % 8, 136 - x % 8), R("cand", 1024 * q + x, 1024 * q + 1024, 16), False, x == 15)
 
-    def joined(q, k):
-        for x in range(16):
+    def joined(q, k, xs=range(16)):
+        for x in xs:
             mm(P(k, 0, 64), W("zx", 16 - x, 144 - x), R("cand", 1024 * q + x, 1024 * q + 1024, 16), x == 0, False)
 
     owners = [(rank + 1 + i) % N for i in range(N)]
@@ -376,15 +377,22 @@ def rank_program(g, core, T, topo):
         if more:
             centre()
 
-    def count_cols(q):
+    def entries(q):
+        wide = 32 if q < 2 else 16
         for o in range(N):
-            for s in (2 * q, 2 * q + 1):
-                mm(P(5, 8 * (o % 2) + s, 128, 16, slice(32 * (o // 2), 32 * (o // 2) + 32)), seg(o, s), R("blk", 0, 128, 16), True, True)
+            for a in range(0, 64, wide):
+                s = (64 * (q % 2) + a) // wide
+                yield o, (4 * o + s if q < 2 else 8 * (o % 2) + s), o // 2, R("ind", 256 * q + 64 * o + a, 256 * q + 64 * o + a + wide)
 
-    def prefix(q, w, last):
-        for o in (2 * w, 2 * w + 1):
-            for s in (2 * q, 2 * q + 1):
-                mm(P(6 + w, 8 * (o % 2) + s, 512, 16), R("trin"), seg(o, s), False, last and o % 2 == 1 and s % 2 == 1)
+    def count_cols(q):
+        for o, i, w, x in entries(q):
+            out = P(5, i, 128, 16, slice(0, 32)) if q < 2 else P(5, 128 + i, 256, 16, slice(32 * w, 32 * w + 16))
+            mm(out, x, R("blk", 0, 128, 16), True, True)
+
+    def prefix(q, last=False):
+        todo = list(entries(q))
+        for n, (o, i, w, x) in enumerate(todo):
+            mm(P(6, i, 512, 16) if q < 2 else P(7, 256 * w + i, 256 * w + 256, 16), R("trin"), x, False, last and n == len(todo) - 1)
 
     def mark(q, k, who="v"):
         for i, p in enumerate(owners):
@@ -395,14 +403,9 @@ def rank_program(g, core, T, topo):
         if who == "s":
             act(R("ind", 256 * q, 256 * q + 256), R("ab"), F.Relu, -4.0, 1.0)
 
-    def seg(o, s):
-        a = 256 * (s // 2) + 64 * o + 32 * (s % 2)
-        return R("ind", a, a + 32)
-
-    def counts(q):
+    def counts(q, last=False):
         count_cols(q)
-        for w in range(2):
-            prefix(q, w, False)
+        prefix(q, last)
 
     def add(o, i, sem):
         prepare("g", o[1], o[1] + i[1])
@@ -410,26 +413,31 @@ def rank_program(g, core, T, topo):
         record("g", o[1], i[1], sem, 16)
 
     def build(t, wid, gap0, gap1, gap2, gap3):
+        def plus(h):
+            act(R("xa", 512 * h, 512 * h + 512), X(R("bk", 0, wid), R("lx", 192 + 32 * h, 224 + 32 * h)), F.Copy)
+            add(R("fv", 3072 + 512 * h, 3584 + 512 * h), R("xa", 512 * h, 512 * h + 512), "d_add%d%d" % (t, h))
+
         act(quarter("sv", 1), col("x", 1, B), F.Copy)
         first(0, wid)
         act(quarter("fv", 3), col("y", 3, B), F.Copy)
         gap0()
+        plus(0)
+        plus(1)
         third(0, wid)
         centre()
-        for w in range(2):
-            mm(P(6 + w, 0, 512), R("idp"), R("ctab"), True, False)
+        mm(P(6, 0, 512), R("idp"), R("ctab0"), True, False)
+        mm(P(5, 128, 256, rows=low64), W("zero", 0, 64), R("ob"), True, True)
         apart(0)
         joined(0, 4)
-        act(R("xa"), col("x", 3, wid), F.Copy)
-        add(quarter("fv", 3), R("xa"), "d_add%d" % t)
-        act(quarter("sv", 2), col("y", 2, B), F.Copy)
+        mm(P(7, 0, 512), R("idp"), R("ctab1"), True, False)
+        act(quarter("sv", 2), col("y", 2, B), F.Copy, -1.0)
 
         def gather_x2(h):
             act(R("xv", 512 * h, 512 * h + 512), X(R("bk", 0, wid), R("lx", 128 + 32 * h, 160 + 32 * h)), F.Copy)
 
         def differ(h):
             mm(P(2 + h, 0, 512), R("idp"), R("xv", 512 * h, 512 * h + 512), True, False)
-            mm(P(2 + h, 0, 512), R("idm"), R("sv", 2048 + 512 * h, 2560 + 512 * h), False, True)
+            mm(P(2 + h, 0, 512), R("idp"), R("sv", 2048 + 512 * h, 2560 + 512 * h), False, True)
 
         first(1, wid)
         gap1()
@@ -439,48 +447,63 @@ def rank_program(g, core, T, topo):
         third(1, wid)
         differ(0)
         apart(1)
+        mark(0, 4)
         differ(1)
+        joined(1, 1)
+        counts(0)
         for h in range(2):
             act(R("fv", 2048 + 512 * h, 2560 + 512 * h), P(2 + h, 0, 512), F.Abs)
-        joined(1, 1)
-        mark(0, 4)
         third(3, wid, 0, 32)
         judge(1)
-        counts(0)
         mark(1, 1, "s")
         third(3, wid, 32, 64)
         apart(3)
         joined(3, 4)
         third(2, wid, 0, 32)
         judge(4)
-        counts(1)
-        mm(P(2, 0, 68), R("idp"), R("btab"), True, False)
+        counts(1, True)
+        mm(P(2, 0, 33), R("idp"), R("btab0"), True, False)
+        mm(P(3, 0, 36), R("idp"), R("btab1"), True, False)
+        low32 = slice(0, 32)
+        act(R("t1", rows=low32), P(5, 0, 128, rows=low32), F.Copy)
+        act(R("t3", rows=low32), P(5, 0, 128, rows=low32), F.Relu, -1.0, 1.0)
+        lin(R("vin"), P(6, 0, 512), None, LIFT + 0.5 + STEP / 2)
         gap3()
         third(2, wid, 32, 64)
         apart(2)
-        joined(2, 1)
         mark(3, 4)
+        scan(R("t2", rows=low32), R("rst0", rows=low32), P(5, 0, 128, rows=low32), A.mult, A.add)
+        joined(2, 1, range(4))
+        for i, r in ((1, R("e1", rows=low32)), (3, R("e3", rows=low32)), (2, R("ob", 0, 33, rows=low32))):
+            mm(P(2, 0, 33), R("t%d" % i, rows=low32), r, False, i == 2)
+        joined(2, 1, range(4, 16))
         judge(1, False)
-        gap2()
+        tt(R("of", 0, 33), P(2, 0, 33), R("trs0"), A.min)
+        ts(R("half"), R("ob", 0, 18), P(2, 32, 33), None, A.mult)
+        cp(R("off0"), R("of", 0, 33))
+        act(X(R("win"), R("off0", 0, 32)), R("vin"), F.Silu)
         counts(3)
         mark(2, 1)
         count_cols(2)
-        prefix(2, 0, True)
-        prefix(2, 1, True)
-
-    def send(t, gap1, gap2):
-        arr, snd = "arr%d" % t, "snd%d" % t
-        scan(R("t2", rows=low64), R("rst", rows=low64), P(5, 0, 128, rows=low64), A.mult, A.add)
-        cp(R("t1", rows=low64), P(5, 0, 128, rows=low64))
-        ts(R("t3", rows=low64), P(5, 0, 128, rows=low64), 0.0, None, A.is_equal)
-        for i in (2, 1, 3):
-            mm(P(2, 0, 68), R("t%d" % i, rows=low64), R("r%d" % i, rows=low64), False, i == 3)
         for w in range(2):
-            lin(R("vin%d" % w, 0, 512), P(6 + w, 0, 512), None, LIFT + 0.5 + STEP / 2)
-        tt(R("of"), P(2, 0, 68), R("trs"), A.min)
-        cp(R("off"), R("of"))
-        scatter(R("win0"), R("off", 0, 33), R("vin0"))
-        act(X(R("win1"), R("off", 34, 67)), R("vin1"), F.Silu)
+            mm(P(3, 18 * w, 18 * w + 18), R("pick%d" % w), R("half"), False, False)
+        prefix(2, True)
+        gap2()
+
+    def send(t, gap0, gap1, gap2):
+        arr, snd = "arr%d" % t, "snd%d" % t
+        scan(R("t2", rows=low64), R("rst1", rows=low64), P(5, 128, 256, rows=low64), A.mult, A.add)
+        cp(R("t1", rows=low64), P(5, 128, 256, rows=low64))
+        ts(R("t3", rows=low64), P(5, 128, 256, rows=low64), 0.0, None, A.is_equal)
+        for i in (2, 1, 3):
+            mm(P(3, 0, 36), R("t%d" % i, rows=low64), R("r%d" % i, rows=low64), False, i == 3)
+        ts(R("vin0", 0, 256), P(7, 0, 256), LIFT + 0.5 + STEP / 2, None, A.add)
+        lin(R("vin1", 0, 256), P(7, 256, 512), None, LIFT + 0.5 + STEP / 2)
+        tt(R("of"), P(3, 0, 36), R("trs1"), A.min)
+        cp(R("off1"), R("of"))
+        scatter(R("win", 0, WIN), R("off1", 0, 17), R("vin0"))
+        act(X(R("win", WIN), R("off1", 18, 35)), R("vin1"), F.Silu)
+        gap0()
 
         def slots(a, b, k):
             for o in range(a, b):
@@ -517,7 +540,7 @@ def rank_program(g, core, T, topo):
                 wrote.setdefault(arr, []).append((range(CAP * q, CAP * q + CAP), tok))
         return sum(len(e) for e in mine.values()), total
 
-    def keep(t):
+    def keep(t, meanwhile):
         arr = "arr%d" % t
         mm(P(2, 0, M), R("kblk"), R(arr), True, True)
         listify(P(3, 0, 24), "kwx", arr)
@@ -525,55 +548,43 @@ def rank_program(g, core, T, topo):
         lin(R("fl"), P(2, 0, M), 1.0 / 16384, 128.5 + 1.0 / 32768)
         mm(P(6, 0, M), R("idn"), R("fl"), False, True)
         cp(R("ki"), P(3, 0, 24))
-        ts(R("kb"), R("ki"), INV + 16383, None, A.bitwise_and)
+        ts(R("kb"), R("ki"), INV + 16380, None, A.bitwise_and)
         cp(R("kf"), R("kb"))
-        ts(R("kb2"), R("kb"), 2, None, A.arith_shift_right)
-        ts(R("r16"), P(6, 0, M), 129.0 * 16384, None, A.add)
-        ts(R("bo"), R("kb2"), J, None, A.min)
-        lin(R("nkf"), R("kf"), -1.0, 129.0 * 16384)
+        ts(R("r16"), P(6, 0, M), 129.0 * 16384 - rank, None, A.add)
+        ts(R("bo"), R("kf"), 0.25, float(J), A.mult, A.min)
+        lin(R("nkf"), R("kf"), -1.0, 129.0 * 16384 - rank)
 
         def rows(name, a, b, c, d):
             return (T[name][:, a, c:d] if b == a + 1 else T[name][:, a:b, c:d], [(name, range(M * a, M * b))])
 
-        for q in range(OWN_ROWS, 24):
+        for q in range(23, OWN_ROWS - 1, -1):
             act(rows("far", q - OWN_ROWS, q - OWN_ROWS + 1, 0, M - 16 * q), P(6, 16 * q, M), F.Abs, None, R("nkf", q, q + 1))
-        for a in range(OWN_ROWS, 24, 4):
+            if q == 20:
+                act(R("us"), X(R("tbl", 0, J + 16), R("bo")), F.Copy)
+        for a in (20, OWN_ROWS):
             act(rows("eq", a, a + 4, 0, M - 16 * a), rows("far", a - OWN_ROWS, a - OWN_ROWS + 4, 0, M - 16 * a), F.Relu, -1.0, 1.0)
-        act(R("us"), X(R("tbl", 0, J + 16), R("bo")), F.Copy)
-        mm(P(0, 0, M), W("zero", 0, 128), R("mle"), True, False)
+        meanwhile()
+        mm(P(0, 0, M), R("idp"), R("trow"), True, False)
+        mm(P(4, 64, 88), R("idp"), R("tk"), True, False)
 
         def earlier(q):
-            mm(P(0, 16 * q + 16, M), R("blk"), rows("eq", q, q + 1, 16, M - 16 * q), False, False)
+            mm(P(0, 16 * q + 16, M), R("bdrop"), rows("eq", q, q + 1, 16, M - 16 * q), False, False)
 
         for q in range(OWN_ROWS):
             ts(rows("eq", q, q + 1, 0, M - 16 * q), R("r16", 16 * q, M), R("kf", q, q + 1), None, A.is_equal)
-            if q == OWN_ROWS - 4:
-                for p in range(OWN_ROWS, 23):
-                    earlier(p)
-            if q == OWN_ROWS - 1:
-                mm(P(0, 0, M), R("idp"), R("us"), False, False)
             earlier(q)
-        mm(P(0, 0, M), R("idp"), (T.eq[:, :, 0:16], [("eq", range(0, 24 * M))]), False, True)
-        tt(R("dm"), P(0, 0, M), R("mle"), A.mult)
-        listify(P(1, 0, 24), "onx", "dm")
-        act(R("kp"), P(1, 0, 24), F.Relu, -1.0, 2.0, R("ksum"))
+            if q == 4:
+                mm(P(0, 0, M), R("idrop"), R("us"), False, False)
+            for p in {10: range(20, 23), 13: range(OWN_ROWS, 20)}.get(q, ()):
+                earlier(p)
+        for x in range(1, 16):
+            mm(P(0, x, M, 16), R("before", 128 * x, 128 * x + 128), (T.eq[:, :, x], [("eq", range(0, 24 * M))]), False, x == 15)
+        act(R("kr"), P(0, 0, M), F.Relu, total=R("ksum"))
         if t == 0:
             mm(P(5, 200, 201), R("blkf"), R("ksum"), True, True)
-        scan(R("ks"), R("one"), R("kp"), A.mult, A.add)
-        ts(R("nk"), R("kp"), 0.0, None, A.is_equal)
-        mm(P(4, 64, 88), R("neg"), R("kp"), True, False)
-        mm(P(4, 64, 88), R("blk"), R("ks"), False, True)
-        if t == 0:
-            ts(R("w0"), P(5, 200, 201), R("sc", 6, 7), HALF, A.mult, A.add)
-
-        tt(R("tn"), R("nk"), R("tk"), A.mult)
-
-    def rooms(base):
-        tt(R("om"), R("tn"), P(4, 64, 88), A.max)
-        if base is None:
-            cp(R("mo"), R("om"))
-        else:
-            ts(R("mo"), R("om"), base, None, A.add)
+        scan(R("ks"), R("hold"), R("kr"), A.mult, A.add)
+        for x in range(16):
+            mm(P(4, 64, 88), W("sgn", 16 - x, 144 - x), R("ks", x, M, 16), False, x == 15)
 
     def append(t):
         scatter(R("bk", B), R("mo"), R("arr%d" % t))
@@ -597,16 +608,17 @@ def rank_program(g, core, T, topo):
     ts(R("lh", 0, 1), R("sc", 4, 5), R("sc", 5, 6), -5000.0, A.is_gt, A.mult)
     ts(R("lo"), R("sc", 4, 5), -2040.0, R("srow"), A.add, A.mult)
     sel(R("idp"), R("ob"), [[-1, 128]], A.is_equal, 0, 1)
-    iota(R("ctab"), [[1, 32], [0, 2], [32, 8]], 0)
+    dma("g", "d_ui", R("ui"), ext(T.used[:, :]))
+    iota(R("cb0"), [[0, 8], [3576, 2], [0, 8]], -2040)
+    iota(R("ctab0"), [[1, 32], [0, 4], [32, 4]], 0)
+    sel(R("cb1"), R("cb0"), [[-1, 128]], A.is_equal, 0, 1)
     sel(R("wca"), W("zero", 0, 144), [[-16, 9], [256, 2], [-1, 8]], A.not_equal, -256, 1, -1.0)
-    sel(R("wc"), R("wca"), [[-16, 9], [256, 2], [-1, 8]], A.not_equal, -264, 1, -1.0)
+    sel(R("cen"), R("cb1"), [[-16, 8], [256, 2], [-1, 8]], A.not_equal, -256, 1, -0.375)
     sel(R("tra"), R("nst"), [[1, 128]], A.is_ge, 0, -1)
+    sel(R("wc"), R("wca"), [[-16, 9], [256, 2], [-1, 8]], A.not_equal, -264, 1, -1.0)
     sel(R("trin"), R("tra"), [[-16, 8], [0, 16]], A.is_ge, 0, 1)
-    iota(R("mob"), [[0, 128]], -1)
-    sel(R("idm"), R("mob"), [[-1, 128]], A.is_equal, 0, 1)
-    iota(R("trs0"), [[0, 2], [16, 34]], TRASH)
-    iota(R("se0"), [[0, 24], [1, 16]], 0)
-    iota(R("tk0"), [[16, 24]], SPARE)
+    for w in range(2):
+        iota(R("ctab1", 256 * w, 256 * w + 256), [[1, 16], [0, 2], [16, 8]], 128)
 
     def gap0():
         ts(R("lh", 1, 2), R("lh", 0, 1), R("sc", 5, 6), R("srow"), A.add, A.mult)
@@ -614,32 +626,35 @@ def rank_program(g, core, T, topo):
         ts(R("hi"), R("lh", 1, 2), R("hk"), None, A.add)
 
     def gap1():
-        blocks = [[32, 2], [0, 34]]
-        iota(R("n68"), [[0, 68]], int(BIG))
-        sel(R("ra0"), R("ob", 0, 68), blocks, A.is_ge, 31, -1)
-        sel(R("r2"), R("ra0"), [[-32, 2], [0, 34]], A.is_ge, 0, 1)
-        sel(R("rb0"), R("mob", 0, 68), blocks, A.is_ge, 31, -1)
-        sel(R("r1"), R("rb0"), [[-32, 2], [-1, 34]], A.is_ge, 0, 1)
-        sel(R("i68"), R("n68"), blocks, A.is_ge, 31, -1)
-        sel(R("r3"), R("i68"), [[-32, 2], [-1, 34]], A.is_equal, 0, 1)
-        iota(R("rst"), [[0, 128]], 1)
-        iota(R("rst", 0, 128, 8), [[0, 16]], 0)
+        blocks = [[32, 2], [0, 18]]
+        sel(R("btab0"), R("bt0"), [[-1, 33]], A.is_gt, 32, 0)
+        iota(R("n36"), [[0, 36]], int(BIG))
+        iota(R("mob"), [[0, 36]], -1)
+        sel(R("rst0"), R("ob"), [[0, 32], [1, 4]], A.is_gt, 0, 0)
+        sel(R("e3"), R("n36", 0, 33), [[-1, 33]], A.is_equal, 0, 1)
+        sel(R("e1"), R("mob", 0, 33), [[-1, 33]], A.is_ge, 0, 1)
+        iota(R("trs0"), [[16, 33]], WIN + TRASH, 1)
         for o in (0, 1):
             iota(clear(o), [[0, CAP]], 0)
         for w in range(2):
-            iota(R("vin%d" % w, 512, 528), [[0, 16]], LIFT + 300)
+            sel(R("pick%d" % w), R("ob"), [[-16, 8], [-4, 2], [0, 8]], A.is_equal, -8 * w - 3, 1)
+        sel(R("ra0"), R("ob", 0, 36), blocks, A.is_ge, 15, -1)
+        sel(R("rb0"), R("mob", 0, 36), blocks, A.is_ge, 15, -1)
+        sel(R("i36"), R("n36"), blocks, A.is_ge, 15, -1)
+        sel(R("r2"), R("ra0"), [[-32, 2], [0, 18]], A.is_ge, 0, 1)
+        sel(R("r1"), R("rb0"), [[-32, 2], [-1, 18]], A.is_ge, 0, 1)
+        sel(R("r3"), R("i36"), [[-32, 2], [-1, 18]], A.is_equal, 0, 1)
+        sel(R("rst1"), R("ob"), [[0, 16], [1, 8]], A.is_gt, 0, 0)
+        iota(R("trs1"), [[0, 2], [16, 18]], TRASH, 1)
+        for w in range(2):
+            iota(R("vin%d" % w, 256, 272), [[0, 16]], LIFT + 300)
         iota(R("cand", J, J + 16), [[0, 16]], NONE)
-        iota(R("tbl", J, J + 16), [[0, 16]], 2)
-        iota(R("one"), [[0, 24]], 1)
-        sel(R("nb"), R("mob"), [[-1, 128]], A.is_ge, 0, 1)
-        sel(R("neg"), R("nb"), [[16, 8], [0, 16]], A.is_ge, 15, -1)
-        iota(R("bk", B, B + 2 * M), [[0, 2 * M]], 0)
-        for h in ("hx1", "hy1"):
-            iota(R(h, 0, 768, 3), [[0, 256]], -4096)
+        iota(R("tk0"), [[16, 24]], SPARE)
+        iota(R("se0"), [[1, M]], SPARE + 1)
+        iota(R("i16"), [[1, 16]], 0)
+        iota(R("tbl", J, J + 16), [[0, 16]], 1)
         iota(R("rawx", 384, 768, 3), [[0, 128]], 0)
         iota(R("rawy", 0, 384, 3), [[0, 128]], 0)
-        for q in range(24 - OWN_ROWS):
-            iota((T.far[:, q, :], [("far", range(M * q, M * q + M))]), [[0, M - 16 * OWN_ROWS]], 1)
 
     def gap2():
         cp(R("uf"), R("ui"))
@@ -648,20 +663,24 @@ def rank_program(g, core, T, topo):
             dma("y", "d_used", R("tbl", 0, J, rows=slice(r, 128, 16)), R("uf"), 256)
 
     def gap3():
+        act(R("bdrop"), R("blk"), F.Copy, scale=DROP)
         lin(R("wk"), row, 14.0, 9.0)
-        lin(R("mb"), row, -1.0, 1.0)
-        lin(R("trs"), R("trs0"), None, row)
         act(W("onx", 16, 144, 16), R("blk", 0, 128, 16), F.Copy)
         act(W("kwx", 16, 144, 16), R("blk", 0, 128, 16), F.Copy, scale=R("wk"))
         act(R("kblk"), R("blk"), F.Copy, scale=R("wk"))
-        act(R("idn"), R("idp"), F.Copy, scale=-16384.0)
-        act(R("blkf"), R("blk"), F.Copy)
-        lin(R("tk"), R("tk0"), None, row)
-        act(R("mle"), R("se0"), F.Relu, None, R("mb"))
+
+    def gap4():
         for i, (a, b) in enumerate(((1, 3), (2, 2))):
             lin(R("wq", i, i + 1), R("sc", a, a + 1), R("sc", 6 + b, 7 + b), HALF)
+        act(R("idn"), R("idp"), F.Copy, scale=-16384.0)
         lin(R("wm"), R("wq"), None, MAGIC)
+        act(R("idrop"), R("idp"), F.Copy, scale=DROP)
         lin(R("w"), R("wm"), None, -MAGIC)
+        lin(R("w8"), R("srow"), 0.25, -0.125)
+        lin(R("s8"), R("srow"), 0.125)
+        lin(R("tk"), R("tk0"), None, row)
+
+    def thresholds():
         lin(R("wb"), R("w", 0, 1), 2.0, R("w", 1, 2))
         lin(R("by1", 1, 2), R("w", 1, 2), -8388608.0, -2048.0)
         lin(R("by1", 2, 3), R("w", 1, 2), 8388608.0, -2048.0)
@@ -670,36 +689,54 @@ def rank_program(g, core, T, topo):
         lin(R("by1", 3, 4), R("wb"), 8388608.0, -2048.0)
         lin(R("bx1"), R("by1"), -1.0)
 
-    build(0, B, gap0, gap1, gap2, gap3)
-    sent0, got0 = send(0, nothing, nothing)
+    def rows_before(xs):
+        for x in xs:
+            sel(R("before", 128 * x, 128 * x + 128), R("bdrop"), [[16, 8], [0, 16]], A.is_gt, x, -1)
 
+    build(0, B, gap0, gap1, gap2, gap3)
+    sent0, got0 = send(0, gap4, nothing, nothing)
+
+    for q in range(24 - OWN_ROWS):
+        if q % 4:
+            a = M - 16 * (OWN_ROWS + q)
+            iota((T.far[:, q, a:a + 16 * (q % 4)], [("far", range(M * q, M * q + M))]), [[0, 16 * (q % 4)]], 1)
+    rows_before(range(1, 10))
+    for h in ("hx1", "hy1"):
+        iota(R(h, 0, 768, 3), [[0, 256]], -4096)
+    iota(R("bk", B, B + 2 * M), [[0, 2 * M]], 0)
     for o in range(N):
         iota(clear(o), [[0, CAP]], 0)
     iota(R("ud"), [[0, M]], 1)
     for name in ("la", "lb"):
         cp(R(name + "f", 256, 512), R(name, 256, 512))
+    ts(R("under"), R("i16"), row, DROP, A.is_gt, A.mult)
 
-    for who in "xy":
+    for n, who in enumerate("xy"):
         for half in range(2):
             for i in range(3):
                 if step(1, who, half, i)[0] < 4:
                     affine(1, who, half, i)
+        for x in range(10 + 3 * n, 13 + 3 * n):
+            ts(R("before", 128 * x, 128 * x + 128), R("blk"), R("under", x, x + 1), None, A.mult)
         ts(R("u%s1" % who), R("raw" + who), MAGIC, MAGIC, A.add, A.subtract)
+    lin(R("trow"), R("se0"), R("krow"), R("srow"))
+    lin(R("hold"), R("se0"), 0.0, R("srow"))
+    act(W("sgn", 16, 144, 16), R("blk", 0, 128, 16), F.Copy, scale=R("w8"))
+    act(R("blkf"), R("blk"), F.Copy, scale=R("s8"))
 
-    keep(0)
+    keep(0, thresholds)
 
-    act(R("n4"), P(5, 200, 201), F.Copy)
+    ts(R("w0"), P(5, 200, 201), R("sc", 6, 7), HALF, A.mult, A.add)
+    lin(R("n4q"), P(5, 200, 201), 1.0 / 4096)
     ts(R("scx1"), R("w0"), 8192.0, R("k1"), A.mult, A.add)
-    hmask(1, "x", 0, "v")
-    lin(R("n4q"), R("n4"), 1.0 / 4096)
     lin(R("scy1"), R("scx1"), -1.0)
     affine(1, "y", 0, 0)
+    hmask(1, "x", 0, "v")
     hmask(1, "y", 0)
     hmask(1, "y", 1)
-    tt(R("om"), R("tn"), P(4, 64, 88), A.max)
-    places(1, ("x", 0), between=lambda: cp(R("mo"), R("om")))
+    places(1, ("x", 0), between=lambda: cp(R("mo"), P(4, 64, 88)))
     act(quarter("sv", 0), col("x", 0, B), F.Copy)
-    lin(R("tq"), R("n4"), 1.0 / 4096, B / 4096.0)
+    lin(R("tq"), R("n4q"), None, B / 4096.0)
     affine(1, "x", 1, 0)
     hmask(1, "x", 1)
     append(0)
@@ -710,16 +747,18 @@ def rank_program(g, core, T, topo):
         places(1, ("x", 1), between=place_z)
 
     def taken():
-        ts(R("bm"), R("kb2"), float(J), None, A.min)
-        tt(R("om2"), R("tn"), R("bm"), A.max)
+        ts(R("om"), R("mo"), -float(M), 11.0, A.add, A.mult)
+        ts(R("bm"), R("kf"), 0.25, float(J), A.mult, A.min)
+        ts(R("n4"), R("n4q"), 4096.0, None, A.mult)
+        tt(R("om2"), R("om"), R("bm"), A.max)
         cp(R("mo2"), R("om2"))
 
     build(1, B + M, others, nothing, nothing, nothing)
-    sent1, got1 = send(1, taken, nothing)
+    sent1, got1 = send(1, nothing, taken, nothing)
     scatter(R("tbl"), R("mo2"), R("ud"))
 
-    keep(1)
-    rooms(R("n4"))
+    keep(1, nothing)
+    ts(R("mo"), P(4, 64, 88), R("n4"), None, A.add)
     append(1)
     dma("y", "d_y", ext(T.y[:, :]), R("bk", B, B + 2 * M))
 

from concourse.bass import DstId, RemoteDMATransfer
from concourse.mybir import AluOpType as A, ActivationFunctionType as F

F32, BF, F16, I32, U16 = "float32", "bfloat16", "float16", "int32", "uint16"
B, J, CAP, N = 3072, 4096, 96, 4
M = N * CAP
MAGIC = 12582912.0
HALF = -2047.5 / 4096
MID = 1728
BIAS = HALF - MID
INV = 1048576
NONE = 576
SPARE = 2 * M
OWN = 4128
TRASH = 2 * OWN
WIN = TRASH + 704
BIG = 32768.0
LIFT = 1024
OWN_ROWS = 16
STEP = 1.0 / 32
DROP = -2048.0

SCRATCH = {}
ALIAS, COLS, SIZE = {}, {}, {F32: 0, BF: 0, I32: 0}
for _n, _c, _d in [
    ("nl", 8, I32), ("nf", 10, F32), ("sc", 10, F32), ("ub", 8, F32), ("wi", 2, I32), ("wf", 2, F32), ("wq", 2, F32), ("wm", 2, F32), ("w", 2, F32),
    ("one8", 128, F32), ("b8a", 128, F32), ("b8", 128, F32), ("blkf", 128, F32),
    ("pid", 1, I32), ("ri", 4, I32), ("rf", 4, F32), ("bs4", 2, F32), ("wk", 1, F32), ("w4", 1, F32), ("wz", 1, F32), ("srow", 1, F32), ("krow", 1, F32), ("hk", 1, F32),
    ("lh", 8, F32), ("lo", 1, F32), ("hi", 1, F32), ("bse", 1, F32), ("bmk", 2, F32), ("mb", 1, F32), ("c0", 1, F32), ("nkf", 24, F32),
    ("jc0", 256, F32), ("jc", 256, F32), ("tk0", 24, F32), ("tk", 24, F16),
    ("i36", 36, F32), ("n36", 36, F32), ("trs0", 33, F32), ("trs1", 36, F32), ("se0", M, F32),
    ("ob", 128, BF), ("ba", 128, BF), ("blk", 128, BF), ("nb", 128, BF), ("nst", 128, BF), ("tra", 128, BF), ("trin", 128, BF), ("neg", 128, BF),
    ("kblk", 128, BF), ("mob", 36, BF), ("idp", 128, BF), ("idn", 128, BF), ("cb0", 128, BF), ("cb1", 128, BF), ("cen", 128, BF),
    ("bdrop", 128, BF), ("idrop", 128, BF), ("before", 2048, BF), ("under", 16, F32), ("w8", 1, F32), ("s8", 1, F32),
    ("wts", 6 * 144, BF), ("wca", 144, BF), ("wc", 144, BF),
    ("r1", 36, BF), ("r2", 36, BF), ("r3", 36, BF), ("ra0", 36, BF), ("rb0", 36, BF), ("e1", 33, BF), ("e3", 33, BF), ("pick0", 128, BF), ("pick1", 128, BF),
    ("bt0", 33, F32), ("btab0", 33, F16), ("btab1", 36, BF), ("rst0", 128, BF), ("rst1", 128, BF), ("ctab0", 512, BF), ("ctab1", 512, BF), ("half", 18, F16),
    ("trow", M, F16), ("hold", M, BF), ("i16", 16, F32), ("stp", CAP, F32), ("ud", M, BF), ("ui", 256, I32), ("uf", 256, BF),
    ("bx0", 4, F32), ("by0", 4, F32), ("bx1", 4, F32), ("by1", 4, F32), ("wb", 1, F32), ("k1", 1, F32),
    ("scx0", 1, F32), ("scy0", 1, F32), ("scx1", 1, F32), ("scy1", 1, F32),
    ("n4", 1, F32), ("n4q", 1, F32), ("tq", 1, F32), ("w0", 1, I32), ("ksum", 1, F32),
    ("la", 512, I32), ("lb", 512, I32), ("lc", 512, I32), ("laf", 512, F32), ("lbf", 512, F32), ("lcf", 512, F32),
    ("ux0", 512, F32), ("uy0", 512, F32), ("ux1", 768, F16), ("uy1", 768, F16), ("rawx", 768, F32), ("rawy", 768, F32),
    ("hx0", 512, BF), ("hy0", 512, BF), ("hx1", 768, BF), ("hy1", 768, BF),
    ("sox0", 512, F32), ("soy0", 512, F32), ("sox1", 768, F16), ("soy1", 768, F16),
    ("zf", 256, F32), ("lx", 256, U16), ("ly", 256, U16), ("lz", 256, U16),
    ("bk", B + SPARE + 3 * M, BF), ("sv", 3072, BF), ("xv", 1024, BF), ("xa", 1024, BF), ("fv", J, BF), ("cand", J + 16, BF),
    ("cl", 128, F16), ("ind", 1024, BF), ("ab", 256, BF), ("t1", 128, BF), ("t2", 128, BF), ("t3", 128, BF), ("of", 36, F32), ("off0", 33, U16), ("off1", 36, U16),
    ("vin", 512, F32), ("vin0", 272, F32), ("vin1", 272, F32), ("win", 2 * WIN, F32), ("fr", M, F16),
    ("jl", 24, U16), ("snd0", 288, BF), ("snd1", 288, BF), ("arr0", M, BF), ("arr1", M, BF),
    ("ki", 24, I32), ("kb", 24, I32), ("kf", 24, F32), ("kb2", 24, I32), ("bm", 24, F32), ("bo", 24, U16), ("fl", M, BF), ("r16", M, U16),
    ("tbl", 11 * 3 * M, BF), ("us", M, BF), ("kr", M, F16), ("ks", M, F16), ("om", 24, F32), ("mo", 24, U16), ("om2", 24, F32), ("mo2", 24, U16),
]:
    COLS[_n] = _c
    if _c <= 128 and _d in SIZE and _n != "nl":
        ALIAS[_n] = ({F32: "pf", BF: "pb", I32: "pi"}[_d], SIZE[_d])
        SIZE[_d] += -(-_c // 8) * 8
    else:
        SCRATCH[_n] = ("sbuf", [128, _c], _d)
SCRATCH["pf"] = ("sbuf", [128, SIZE[F32]], F32)
SCRATCH["pb"] = ("sbuf", [128, SIZE[BF]], BF)
SCRATCH["pi"] = ("sbuf", [128, SIZE[I32]], I32)
SCRATCH["eq"] = ("sbuf", [128, 24, M], BF)
SCRATCH["far"] = ("sbuf", [128, 24 - OWN_ROWS, M - 16 * OWN_ROWS], BF)
for _n in range(8):
    SCRATCH["ps%d" % _n] = ("psum", [128, 512], F32)

DMAS = ["d_ncl", "d_lim", "d_la0", "d_lb0", "d_lc0", "d_la1", "d_lb1", "d_lc1", "d_bk", "d_ui", "d_used", "d_y", "d_add00", "d_add01", "d_add10", "d_add11"]
SEMAPHORES = ["cv", "cs", "ct", "cg", "arrv0", "arrv1", "snt0", "snt1"] + DMAS


def plan(src, cores, topo):
    own = topo.cores_of(src)
    far = [c for c in cores if c not in own]
    out = {}
    taken = []
    for i, d in enumerate(far):
        e = topo.engines(src, d)
        n = len(e) // len(far)
        out[d] = e[i * n:(i + 1) * n]
        taken += e
    for d in cores:
        if d in own and d != src:
            out[d] = [e for e in topo.engines(src, d) if e not in taken][:4]
    return out


def overlap(a, b):
    if a.start >= b.stop or b.start >= a.stop:
        return False
    if a.step == b.step and a.step > 1 and (a.start - b.start) % a.step:
        return False
    return True


def covers(a, b):
    return a.step == 1 and a.start <= b.start and b.stop <= a.stop


def rank_program(g, core, T, topo):
    rank = T.rank_of(core)
    if rank is None:
        return
    cores = list(T.cores)
    queues = {"v": g.vector, "s": g.scalar, "t": g.tensor, "g": g, "y": g.sync}
    qsem = {"v": "cv", "s": "cs", "t": "ct", "g": "cg"}
    count = {"v": 0, "s": 0, "t": 0, "g": 0}
    known = {q: {} for q in queues}
    wrote, read = {}, {}
    order = [0]

    def need(q, toks):
        for t in sorted(toks, key=lambda t: -t["n"]):
            if known[q].get(t["sem"], 0) < t["val"]:
                queues[q].wait_ge(T.sem[t["sem"]], t["val"])
                for k, v in t["snap"].items():
                    if known[q].get(k, 0) < v:
                        known[q][k] = v
                known[q][t["sem"]] = max(known[q].get(t["sem"], 0), t["val"])

    def prepare(q, outs, ins):
        toks = []
        for n, r in ins:
            for r2, t in wrote.get(n, []):
                if overlap(r, r2):
                    toks.append(t)
            if n.startswith("ps"):
                toks += [t for r2, t in wrote.get(n, []) + read.get(n, []) if t["q"] != q]
        for n, r in outs:
            ps = n.startswith("ps")
            for r2, t in wrote.get(n, []):
                if ps and t["q"] != q or (overlap(r, r2) and not (ps and q == "t")):
                    toks.append(t)
            for r2, t in read.get(n, []):
                if (ps and t["q"] != q) or overlap(r, r2):
                    toks.append(t)
        need(q, toks)

    def record(q, outs, ins, sem, val):
        order[0] += 1
        tok = {"n": order[0], "sem": sem, "val": val, "q": q, "snap": dict(known[q])}
        for n, r in outs:
            wrote[n] = [x for x in wrote.get(n, []) if not covers(r, x[0]) or n.startswith("ps")] + [(r, tok)]
            if not n.startswith("ps"):
                read[n] = [x for x in read.get(n, []) if not covers(r, x[0])]
        for n, r in ins:
            read[n] = [x for x in read.get(n, []) if not (x[1]["q"] == q and x[0] == r)] + [(r, tok)]
        for n, r in outs + ins:
            if n.startswith("ps"):
                for d in (wrote, read):
                    d[n] = list({(x[1]["q"], x[0].start, x[0].stop): x for x in d.get(n, [])}.values())

    def R(name, a=0, b=None, st=1, rows=None):
        b = COLS.get(name, 512) if b is None else b
        if name in ALIAS:
            name, o = ALIAS[name]
            a, b = a + o, b + o
        cols = slice(a, b) if st == 1 else slice(a, b, st)
        ap = T[name][:, cols] if rows is None else T[name][rows, cols]
        return (ap, [(name, range(a, b, st))])

    def X(w, o):
        return (w[0].indirect(o[0]), w[1] + o[1])

    def emit(q, outs, ins, f):
        prepare(q, outs, ins)
        inst = f(queues[q])
        count[q] += 1
        inst.then_inc(T.sem[qsem[q]], 1)
        record(q, outs, ins, qsem[q], count[q])

    def scal(x):
        return (x[0], x[1]) if isinstance(x, tuple) else (x, [])

    def ts(o, i, s1, s2, op0, op1=None):
        a, ra_ = scal(s1)
        b, rb_ = scal(s2)
        if op1 is None:
            emit("v", o[1], i[1] + ra_, lambda e: e.tensor_scalar(o[0], i[0], a, None, op0))
        else:
            emit("v", o[1], i[1] + ra_ + rb_, lambda e: e.tensor_scalar(o[0], i[0], a, b, op0, op1))

    def tt(o, a, b, op):
        emit("v", o[1], a[1] + b[1], lambda e: e.tensor_tensor(o[0], a[0], b[0], op))

    def cp(o, i):
        emit("v", o[1], i[1], lambda e: e.tensor_copy(o[0], i[0]))

    def scatter(w, o, i):
        emit("v", w[1], i[1] + o[1], lambda e: e.tensor_copy(w[0].indirect(o[0]), i[0]))

    def scan(o, a, b, op0, op1, first=0.0):
        emit("v", o[1], a[1] + b[1], lambda e: e.tensor_tensor_scan(o[0], a[0], b[0], first, op0, op1))

    def fill(o, c):
        emit("v", o[1], [], lambda e: e.memset(o[0], c))

    def act(o, i, func, scale=None, bias=None, total=None):
        kw, more, outs = {}, [], o[1]
        for k, x in (("scale", scale), ("bias", bias)):
            if x is not None:
                kw[k], r = scal(x)
                more = more + r
        if total is not None:
            kw["accum_out"], outs = total[0], outs + total[1]
        emit("s", outs, i[1] + more, lambda e: e.activation(o[0], i[0], func, **kw))

    def lin(o, i, scale=None, bias=None):
        act(o, i, F.Identity, scale, bias)

    def mm(o, l, r, start, stop):
        emit("t", o[1], l[1] + r[1], lambda e: e.matmul(o[0], l[0], r[0], start, stop))

    def iota(o, pattern, base, cm=0):
        emit("g", o[1], [], lambda e: e.iota(o[0], pattern, base, cm, allow_small_or_imprecise_dtypes=True))

    def sel(o, i, pattern, op, base, cm, other=0.0):
        emit("g", o[1], i[1], lambda e: e.affine_select(o[0], i[0], pattern, op, other, base, cm))

    def dma(q, sem, o, i, total=16):
        if total == 16:
            prepare(q, o[1], i[1])
        queues[q].dma_start(o[0], i[0]).then_inc(T.sem[sem], 16)
        record(q, o[1], i[1], sem, total)

    def ext(ap):
        return (ap, [])

    def W(name, a, b, st=1):
        o = 144 * ("mx", "zx", "onx", "kwx", "sgn", "zero").index(name)
        return R("wts", o + a, o + b, st)

    def listify(o, wname, src, a=0, b=M):
        for x in range(16):
            mm(o, W(wname, 16 - x, 144 - x), R(src, a + x, b, 16), x == 0, x == 15)

    def P(k, a, b, st=1, rows=None):
        return R("ps%d" % k, a, b, st, rows)

    first8 = slice(0, 8)
    dma("y", "d_ncl", R("nl", 0, 4, rows=first8), ext(T.ncl[:, :]))
    dma("s", "d_lim", R("nl", 4, 6, rows=first8), ext(T.lim[:, :]))
    dma("y", "d_la0", R("la", 0, 256), ext(T.ra[:, 0:256]))
    dma("s", "d_lb0", R("lb", 0, 256), ext(T.rb[:, 0:256]))
    dma("y", "d_bk", R("bk", 0, B), ext(T.bank[:, :]))
    dma("y", "d_lc0", R("lc", 0, 256), ext(T.rc[:, 0:256]))
    dma("y", "d_lb1", R("lb", 256, 512), ext(T.rb[:, 256:512]))
    dma("y", "d_la1", R("la", 256, 512), ext(T.ra[:, 256:512]))
    dma("y", "d_lc1", R("lc", 256, 512), ext(T.rc[:, 256:512]))

    def clear(o):
        a = WIN * (o // 2) + OWN * (o % 2)
        return R("win", a, a + CAP)

    fill(R("one8"), 1.0)
    fill(R("ob"), 1.0)
    for o in (2, 3):
        act(clear(o), R("one8", 0, CAP), F.Silu, scale=0.0)
    iota(R("pid"), [[0, 1]], 0, 1)
    sel(R("b8a", rows=first8), R("one8", rows=first8), [[1, 128]], A.is_ge, 0, -16)
    sel(R("ba"), R("ob"), [[-16, 8], [0, 16]], A.is_ge, 0, 1)
    sel(R("b8", rows=first8), R("b8a", rows=first8), [[-1, 128]], A.is_ge, 15, 16)
    sel(R("blk"), R("ba"), [[16, 8], [0, 16]], A.is_ge, 15, -1)
    iota(R("jc0"), [[16, 256]], -2048)
    for i, bits in enumerate((15, 7, 1, 4)):
        ts(R("ri", i, i + 1), R("pid"), bits, None, A.bitwise_and)
    fill(R("wts"), 0.0)
    cp(R("rf"), R("ri"))
    row = R("rf", 0, 1)
    for h in ("hx0", "hy0"):
        fill(R(h, 0, 512, 2), -4096.0)
    ts(R("krow"), row, 8.0, None, A.is_ge)
    ts(R("w4"), R("rf", 2, 3), -0.5, 0.25, A.mult, A.add)
    ts(R("srow"), row, 8.0, None, A.is_lt)
    ts(R("bmk", 0, 1), R("rf", 1, 2), 7.0, BIG, A.not_equal, A.mult)
    fill(R("ub", 0, 1), BIAS)
    fill(R("nst"), -STEP)
    lin(R("bs4", 0, 1), R("rf", 3, 4), OWN / 4.0)
    lin(R("wz"), R("w4"), None, 1.0)
    lin(R("bse"), R("krow"), float(OWN))
    lin(R("bs4", 1, 2), R("krow"), float(WIN), R("bs4", 0, 1))
    act(W("mx", 8, 136, 16), R("blk", 0, 128, 16), F.Copy)
    act(W("mx", 16, 144, 16), R("blk", 0, 128, 16), F.Copy, scale=R("w4"))
    act(W("zx", 16, 144, 16), R("blk", 0, 128, 16), F.Copy, scale=R("wz"))
    act(R("btab1"), R("ob", 0, 36), F.Copy, scale=R("bse"))
    act(R("bt0"), R("ob", 0, 33), F.Copy, scale=R("bs4", 1, 2))
    lin(R("jc"), R("jc0"), None, row)
    lin(R("hk"), R("krow"), 6040.0, -2040.0)
    lin(R("btab1", 16, 36, 18), R("ob", 0, 2), R("bmk", 0, 1), R("bse"))

    cp(R("nf", 0, 6, rows=first8), R("nl", 0, 6, rows=first8))
    ts(R("nf", 6, 10, rows=first8), R("nl", 0, 4, rows=first8), 1.0 / 4096, None, A.mult)
    mm(P(7, 0, 10), R("b8", rows=first8), R("nf", rows=first8), True, True)
    fill(R("stp"), STEP)
    cp(R("lbf", 0, 256), R("lb", 0, 256))
    for i, (a, b) in enumerate(((0, 3), (1, 2))):
        ts(R("wi", i, i + 1), P(7, a, a + 1), P(7, 6 + b, 7 + b), HALF, A.mult, A.add)
    cp(R("sc"), P(7, 0, 10))
    ts(R("wf"), R("wi"), 8192.0, None, A.mult)
    scan(R("ub", 1, 5), R("one8", 0, 4), P(7, 0, 4), A.mult, A.add, BIAS)
    ts(R("bx0", 0, 1), R("wi", 1, 2), 16777216.0, 2048.0, A.mult, A.add)
    tt(R("scx0"), R("wf", 0, 1), R("wf", 1, 2), A.add)
    lin(R("by0", 0, 1), R("wf", 1, 2), -2048.0, -2048.0)
    lin(R("by0", 2, 3), R("wf", 1, 2), 2048.0, -2048.0)
    lin(R("bx0", 2, 3), R("wf", 1, 2), -2048.0, 2048.0)
    lin(R("scy0"), R("scx0"), -1.0)

    def step(t, who, half, i):
        m = 2 + t
        k = 2 * half + m - 1 - i if who == "x" else 3 + t - 2 * half - i
        return k, (k if who == "x" else 2 * half + i - 1), (128 * m * half + i, 128 * m * (half + 1), m)

    def affine(t, who, half, i, q="s"):
        k, _, cols = step(t, who, half, i)
        sc_, bi = R("sc", 6 + k, 7 + k) if k < 4 else R("n4q"), R("ub", k, k + 1)
        name, a = "l" + ("a" if who == "x" else "b"), 256 * t + 128 * half
        if q == "s":
            lin(R("raw" + who if t and k < 4 else "u%s%d" % (who, t), *cols), R(name + "f", a, a + 128), sc_, bi)
        else:
            ts(R("u%s%d" % (who, t), *cols), R(name, a, a + 128), sc_, bi, A.mult, A.add)

    def hmask(t, who, half, q="s"):
        for i in range(1, 2 + t):
            _, k, cols = step(t, who, half, i)
            x = R("h%s%d" % (who, t), *cols), R("jc", 128 * half, 128 * half + 128), R("sc%s%d" % (who, t)), R("b%s%d" % (who, t), k, k + 1)
            if q == "s":
                lin(*x)
            else:
                ts(*x, A.mult, A.add)

    def places(t, *lists, between=None):
        m = 2 + t
        for who, half in lists:
            a, b = 128 * m * half, 128 * m * (half + 1)
            scan(R("so%s%d" % (who, t), a, b), R("h%s%d" % (who, t), a, b), R("u%s%d" % (who, t), a, b), A.min, A.max)
        if between:
            between()
        for who, half in lists:
            a, b = 128 * m * half, 128 * m * (half + 1)
            ts(R("l" + who, 128 * half, 128 * half + 128), R("so%s%d" % (who, t), a + m - 1, b, m), MAGIC, MAGIC - MID, A.add, A.subtract)

    def place_z():
        ts(R("lz"), R("zf"), MAGIC, MAGIC - MID, A.add, A.subtract)

    def quarter(name, q):
        return R(name, 1024 * q, 1024 * q + 1024)

    def col(who, q, wid):
        return X(R("bk", 0, wid), R("l" + who, 64 * q, 64 * q + 64))

    def first(q, wid):
        tt(quarter("fv", q), col("y", q, wid), quarter("sv", q), (A.min, A.max)[q])

    def third(q, wid, a=0, b=64):
        c, d = 1024 * q + 16 * a, 1024 * q + 16 * b
        tt(R("cand", c, d), X(R("bk", 0, wid), R("lz", 64 * q + a, 64 * q + b)), R("fv", c, d), A.min)

    def centre():
        mm(P(0, 0, 128), R("cen"), R("ob"), True, False)

    def apart(q):
        for x in range(16):
            c = 64 * (x // 8)
            mm(P(0, c, c + 64), W("mx", 8 - x % 8, 136 - x % 8), R("cand", 1024 * q + x, 1024 * q + 1024, 16), False, x == 15)

    def joined(q, k, xs=range(16)):
        for x in xs:
            mm(P(k, 0, 64), W("zx", 16 - x, 144 - x), R("cand", 1024 * q + x, 1024 * q + 1024, 16), x == 0, False)

    owners = [(rank + 1 + i) % N for i in range(N)]
    low64 = slice(0, 64)

    def judge(k, more=True):
        ts(R("cl"), P(0, 0, 128), R("lo"), R("hi"), A.max, A.min)
        mm(P(k, 0, 64), R("wc", 8, 136), R("cl", 0, 64), False, False)
        mm(P(k, 0, 64), R("wc", 0, 128), R("cl", 64, 128), False, True)
        if more:
            centre()

    def entries(q):
        wide = 32 if q < 2 else 16
        for o in range(N):
            for a in range(0, 64, wide):
                s = (64 * (q % 2) + a) // wide
                yield o, (4 * o + s if q < 2 else 8 * (o % 2) + s), o // 2, R("ind", 256 * q + 64 * o + a, 256 * q + 64 * o + a + wide)

    def count_cols(q):
        for o, i, w, x in entries(q):
            out = P(5, i, 128, 16, slice(0, 32)) if q < 2 else P(5, 128 + i, 256, 16, slice(32 * w, 32 * w + 16))
            mm(out, x, R("blk", 0, 128, 16), True, True)

    def prefix(q, last=False):
        todo = list(entries(q))
        for n, (o, i, w, x) in enumerate(todo):
            mm(P(6, i, 512, 16) if q < 2 else P(7, 256 * w + i, 256 * w + 256, 16), R("trin"), x, False, last and n == len(todo) - 1)

    def mark(q, k, who="v"):
        for i, p in enumerate(owners):
            if who == "v":
                ts(R("ind", 256 * q + 64 * i, 256 * q + 64 * i + 64), P(k, 0, 64), 504 + p / 4, None, A.is_equal)
            else:
                act(R("ab", 64 * i, 64 * i + 64), P(k, 0, 64), F.Abs, None, -504 - p / 4)
        if who == "s":
            act(R("ind", 256 * q, 256 * q + 256), R("ab"), F.Relu, -4.0, 1.0)

    def counts(q, last=False):
        count_cols(q)
        prefix(q, last)

    def add(o, i, sem):
        prepare("g", o[1], o[1] + i[1])
        g.dma_start(o[0], i[0], accum_op=A.add).then_inc(T.sem[sem], 16)
        record("g", o[1], i[1], sem, 16)

    def build(t, wid, gap0, gap1, gap2, gap3):
        def plus(h):
            act(R("xa", 512 * h, 512 * h + 512), X(R("bk", 0, wid), R("lx", 192 + 32 * h, 224 + 32 * h)), F.Copy)
            add(R("fv", 3072 + 512 * h, 3584 + 512 * h), R("xa", 512 * h, 512 * h + 512), "d_add%d%d" % (t, h))

        act(quarter("sv", 1), col("x", 1, B), F.Copy)
        first(0, wid)
        act(quarter("fv", 3), col("y", 3, B), F.Copy)
        gap0()
        plus(0)
        plus(1)
        third(0, wid)
        centre()
        mm(P(6, 0, 512), R("idp"), R("ctab0"), True, False)
        mm(P(5, 128, 256, rows=low64), W("zero", 0, 64), R("ob"), True, True)
        apart(0)
        joined(0, 4)
        mm(P(7, 0, 512), R("idp"), R("ctab1"), True, False)
        act(quarter("sv", 2), col("y", 2, B), F.Copy, -1.0)

        def gather_x2(h):
            act(R("xv", 512 * h, 512 * h + 512), X(R("bk", 0, wid), R("lx", 128 + 32 * h, 160 + 32 * h)), F.Copy)

        def differ(h):
            mm(P(2 + h, 0, 512), R("idp"), R("xv", 512 * h, 512 * h + 512), True, False)
            mm(P(2 + h, 0, 512), R("idp"), R("sv", 2048 + 512 * h, 2560 + 512 * h), False, True)

        first(1, wid)
        gap1()
        judge(4)
        gather_x2(0)
        gather_x2(1)
        third(1, wid)
        differ(0)
        apart(1)
        mark(0, 4)
        differ(1)
        joined(1, 1)
        counts(0)
        for h in range(2):
            act(R("fv", 2048 + 512 * h, 2560 + 512 * h), P(2 + h, 0, 512), F.Abs)
        third(3, wid, 0, 32)
        judge(1)
        mark(1, 1, "s")
        third(3, wid, 32, 64)
        apart(3)
        joined(3, 4)
        third(2, wid, 0, 32)
        judge(4)
        counts(1, True)
        mm(P(2, 0, 33), R("idp"), R("btab0"), True, False)
        mm(P(3, 0, 36), R("idp"), R("btab1"), True, False)
        low32 = slice(0, 32)
        act(R("t1", rows=low32), P(5, 0, 128, rows=low32), F.Copy)
        act(R("t3", rows=low32), P(5, 0, 128, rows=low32), F.Relu, -1.0, 1.0)
        lin(R("vin"), P(6, 0, 512), None, LIFT + 0.5 + STEP / 2)
        gap3()
        third(2, wid, 32, 64)
        apart(2)
        mark(3, 4)
        scan(R("t2", rows=low32), R("rst0", rows=low32), P(5, 0, 128, rows=low32), A.mult, A.add)
        joined(2, 1, range(4))
        for i, r in ((1, R("e1", rows=low32)), (3, R("e3", rows=low32)), (2, R("ob", 0, 33, rows=low32))):
            mm(P(2, 0, 33), R("t%d" % i, rows=low32), r, False, i == 2)
        joined(2, 1, range(4, 16))
        judge(1, False)
        tt(R("of", 0, 33), P(2, 0, 33), R("trs0"), A.min)
        ts(R("half"), R("ob", 0, 18), P(2, 32, 33), None, A.mult)
        cp(R("off0"), R("of", 0, 33))
        act(X(R("win"), R("off0", 0, 32)), R("vin"), F.Silu)
        counts(3)
        mark(2, 1)
        count_cols(2)
        for w in range(2):
            mm(P(3, 18 * w, 18 * w + 18), R("pick%d" % w), R("half"), False, False)
        prefix(2, True)
        gap2()

    def send(t, gap0, gap1, gap2):
        arr, snd = "arr%d" % t, "snd%d" % t
        scan(R("t2", rows=low64), R("rst1", rows=low64), P(5, 128, 256, rows=low64), A.mult, A.add)
        cp(R("t1", rows=low64), P(5, 128, 256, rows=low64))
        ts(R("t3", rows=low64), P(5, 128, 256, rows=low64), 0.0, None, A.is_equal)
        for i in (2, 1, 3):
            mm(P(3, 0, 36), R("t%d" % i, rows=low64), R("r%d" % i, rows=low64), False, i == 3)
        ts(R("vin0", 0, 256), P(7, 0, 256), LIFT + 0.5 + STEP / 2, None, A.add)
        lin(R("vin1", 0, 256), P(7, 256, 512), None, LIFT + 0.5 + STEP / 2)
        tt(R("of"), P(3, 0, 36), R("trs1"), A.min)
        cp(R("off1"), R("of"))
        scatter(R("win", 0, WIN), R("off1", 0, 17), R("vin0"))
        act(X(R("win", WIN), R("off1", 18, 35)), R("vin1"), F.Silu)
        gap0()

        def slots(a, b, k):
            for o in range(a, b):
                scan(R("fr", CAP * o, CAP * o + CAP), R("stp"), clear(o), A.add, A.max)
            listify(P(k, 6 * a, 6 * b), "onx", "fr", CAP * a, CAP * b)

        def pick(a, b, k):
            ts(R("jl", 6 * a, 6 * b), P(k, 6 * a, 6 * b), -16.0 * LIFT, float(J), A.add, A.min)

        slots(0, 3, 3)
        slots(3, 4, 2)
        pick(0, 3, 3)
        cp(R(snd, 0, 160), X(R("cand"), R("jl", 0, 10)))
        act(R(snd, 160, 288), X(R("cand"), R("jl", 10, 18)), F.Copy)
        mine = plan(core, cores, topo)
        src = [R(snd, CAP * i, CAP * i + CAP) for i in range(N - 1)]
        prepare("g", [], [x for s in src for x in s[1]])
        tr = []
        for i in range(N - 1):
            d = cores[owners[i]]
            rid, pid = topo.addr(d, core)
            tr.append(RemoteDMATransfer(dst_ids=[DstId(rid=rid, pnc=pid)], dma_engine_mask=sum(1 << e for e in mine[d]),
                                        remote_sem=T.sem["arrv%d" % t], src=src[i][0], dst=T[arr][:, CAP * rank:CAP * rank + CAP]))
        g.remote_dma_fused(tr, local_sem=T.sem["snt%d" % t])
        pick(3, 4, 2)
        gap1()
        gap2()
        act(R(arr, CAP * rank, CAP * rank + CAP), X(R("cand"), R("jl", 18, 24)), F.Copy)
        total = sum(len(plan(c, cores, topo)[core]) for c in cores if c != core)
        order[0] += 1
        tok = {"n": order[0], "sem": "arrv%d" % t, "val": total, "q": "r", "snap": {}}
        for q in range(N):
            if q != rank:
                wrote.setdefault(arr, []).append((range(CAP * q, CAP * q + CAP), tok))
        return sum(len(e) for e in mine.values()), total

    def keep(t, meanwhile):
        arr = "arr%d" % t
        mm(P(2, 0, M), R("kblk"), R(arr), True, True)
        listify(P(3, 0, 24), "kwx", arr)
        mm(P(6, 0, M), R("kblk"), R(arr), True, False)
        lin(R("fl"), P(2, 0, M), 1.0 / 16384, 128.5 + 1.0 / 32768)
        mm(P(6, 0, M), R("idn"), R("fl"), False, True)
        cp(R("ki"), P(3, 0, 24))
        ts(R("kb"), R("ki"), INV + 16380, None, A.bitwise_and)
        cp(R("kf"), R("kb"))
        ts(R("r16"), P(6, 0, M), 129.0 * 16384 - rank, None, A.add)
        ts(R("bo"), R("kf"), 0.25, float(J), A.mult, A.min)
        lin(R("nkf"), R("kf"), -1.0, 129.0 * 16384 - rank)

        def rows(name, a, b, c, d):
            return (T[name][:, a, c:d] if b == a + 1 else T[name][:, a:b, c:d], [(name, range(M * a, M * b))])

        for q in range(23, OWN_ROWS - 1, -1):
            act(rows("far", q - OWN_ROWS, q - OWN_ROWS + 1, 0, M - 16 * q), P(6, 16 * q, M), F.Abs, None, R("nkf", q, q + 1))
            if q == 20:
                act(R("us"), X(R("tbl", 0, J + 16), R("bo")), F.Copy)
        for a in (20, OWN_ROWS):
            act(rows("eq", a, a + 4, 0, M - 16 * a), rows("far", a - OWN_ROWS, a - OWN_ROWS + 4, 0, M - 16 * a), F.Relu, -1.0, 1.0)
        meanwhile()
        mm(P(0, 0, M), R("idp"), R("trow"), True, False)
        mm(P(4, 64, 88), R("idp"), R("tk"), True, False)

        def earlier(q):
            mm(P(0, 16 * q + 16, M), R("bdrop"), rows("eq", q, q + 1, 16, M - 16 * q), False, False)

        for q in range(OWN_ROWS):
            ts(rows("eq", q, q + 1, 0, M - 16 * q), R("r16", 16 * q, M), R("kf", q, q + 1), None, A.is_equal)
            earlier(q)
            if q == 4:
                mm(P(0, 0, M), R("idrop"), R("us"), False, False)
            for p in {10: range(20, 23), 13: range(OWN_ROWS, 20)}.get(q, ()):
                earlier(p)
        for x in range(1, 16):
            mm(P(0, x, M, 16), R("before", 128 * x, 128 * x + 128), (T.eq[:, :, x], [("eq", range(0, 24 * M))]), False, x == 15)
        act(R("kr"), P(0, 0, M), F.Relu, total=R("ksum"))
        if t == 0:
            mm(P(5, 200, 201), R("blkf"), R("ksum"), True, True)
        scan(R("ks"), R("hold"), R("kr"), A.mult, A.add)
        for x in range(16):
            mm(P(4, 64, 88), W("sgn", 16 - x, 144 - x), R("ks", x, M, 16), False, x == 15)

    def append(t):
        scatter(R("bk", B), R("mo"), R("arr%d" % t))

    def nothing():
        pass

    for i in range(2):
        affine(0, "x", 0, i, "v")
    hmask(0, "x", 0, "v")
    for half in range(2):
        hmask(0, "y", half)
        for i in range(2):
            affine(0, "y", half, i)
    places(0, ("x", 0), between=lambda: affine(0, "x", 1, 0, "v"))
    act(quarter("sv", 0), col("x", 0, B), F.Copy)
    affine(0, "x", 1, 1, "v")
    hmask(0, "x", 1, "v")
    places(0, ("y", 0), ("y", 1), ("x", 1))
    ts(R("zf"), R("lc", 0, 256), B / 4096.0, BIAS, A.mult, A.add)
    ts(R("lh", 0, 1), R("sc", 4, 5), R("sc", 5, 6), -5000.0, A.is_gt, A.mult)
    ts(R("lo"), R("sc", 4, 5), -2040.0, R("srow"), A.add, A.mult)
    sel(R("idp"), R("ob"), [[-1, 128]], A.is_equal, 0, 1)
    dma("g", "d_ui", R("ui"), ext(T.used[:, :]))
    iota(R("cb0"), [[0, 8], [3576, 2], [0, 8]], -2040)
    iota(R("ctab0"), [[1, 32], [0, 4], [32, 4]], 0)
    sel(R("cb1"), R("cb0"), [[-1, 128]], A.is_equal, 0, 1)
    sel(R("wca"), W("zero", 0, 144), [[-16, 9], [256, 2], [-1, 8]], A.not_equal, -256, 1, -1.0)
    sel(R("cen"), R("cb1"), [[-16, 8], [256, 2], [-1, 8]], A.not_equal, -256, 1, -0.375)
    sel(R("tra"), R("nst"), [[1, 128]], A.is_ge, 0, -1)
    sel(R("wc"), R("wca"), [[-16, 9], [256, 2], [-1, 8]], A.not_equal, -264, 1, -1.0)
    sel(R("trin"), R("tra"), [[-16, 8], [0, 16]], A.is_ge, 0, 1)
    for w in range(2):
        iota(R("ctab1", 256 * w, 256 * w + 256), [[1, 16], [0, 2], [16, 8]], 128)

    def gap0():
        ts(R("lh", 1, 2), R("lh", 0, 1), R("sc", 5, 6), R("srow"), A.add, A.mult)
        place_z()
        ts(R("hi"), R("lh", 1, 2), R("hk"), None, A.add)

    def gap1():
        blocks = [[32, 2], [0, 18]]
        sel(R("btab0"), R("bt0"), [[-1, 33]], A.is_gt, 32, 0)
        iota(R("n36"), [[0, 36]], int(BIG))
        iota(R("mob"), [[0, 36]], -1)
        sel(R("rst0"), R("ob"), [[0, 32], [1, 4]], A.is_gt, 0, 0)
        sel(R("e3"), R("n36", 0, 33), [[-1, 33]], A.is_equal, 0, 1)
        sel(R("e1"), R("mob", 0, 33), [[-1, 33]], A.is_ge, 0, 1)
        iota(R("trs0"), [[16, 33]], WIN + TRASH, 1)
        for o in (0, 1):
            iota(clear(o), [[0, CAP]], 0)
        for w in range(2):
            sel(R("pick%d" % w), R("ob"), [[-16, 8], [-4, 2], [0, 8]], A.is_equal, -8 * w - 3, 1)
        sel(R("ra0"), R("ob", 0, 36), blocks, A.is_ge, 15, -1)
        sel(R("rb0"), R("mob", 0, 36), blocks, A.is_ge, 15, -1)
        sel(R("i36"), R("n36"), blocks, A.is_ge, 15, -1)
        sel(R("r2"), R("ra0"), [[-32, 2], [0, 18]], A.is_ge, 0, 1)
        sel(R("r1"), R("rb0"), [[-32, 2], [-1, 18]], A.is_ge, 0, 1)
        sel(R("r3"), R("i36"), [[-32, 2], [-1, 18]], A.is_equal, 0, 1)
        sel(R("rst1"), R("ob"), [[0, 16], [1, 8]], A.is_gt, 0, 0)
        iota(R("trs1"), [[0, 2], [16, 18]], TRASH, 1)
        for w in range(2):
            iota(R("vin%d" % w, 256, 272), [[0, 16]], LIFT + 300)
        iota(R("cand", J, J + 16), [[0, 16]], NONE)
        iota(R("tk0"), [[16, 24]], SPARE)
        iota(R("se0"), [[1, M]], SPARE + 1)
        iota(R("i16"), [[1, 16]], 0)
        iota(R("tbl", J, J + 16), [[0, 16]], 1)
        iota(R("rawx", 384, 768, 3), [[0, 128]], 0)
        iota(R("rawy", 0, 384, 3), [[0, 128]], 0)

    def gap2():
        cp(R("uf"), R("ui"))
        prepare("y", [], R("uf")[1])
        for r in range(16):
            dma("y", "d_used", R("tbl", 0, J, rows=slice(r, 128, 16)), R("uf"), 256)

    def gap3():
        act(R("bdrop"), R("blk"), F.Copy, scale=DROP)
        lin(R("wk"), row, 14.0, 9.0)
        act(W("onx", 16, 144, 16), R("blk", 0, 128, 16), F.Copy)
        act(W("kwx", 16, 144, 16), R("blk", 0, 128, 16), F.Copy, scale=R("wk"))
        act(R("kblk"), R("blk"), F.Copy, scale=R("wk"))

    def gap4():
        for i, (a, b) in enumerate(((1, 3), (2, 2))):
            lin(R("wq", i, i + 1), R("sc", a, a + 1), R("sc", 6 + b, 7 + b), HALF)
        act(R("idn"), R("idp"), F.Copy, scale=-16384.0)
        lin(R("wm"), R("wq"), None, MAGIC)
        act(R("idrop"), R("idp"), F.Copy, scale=DROP)
        lin(R("w"), R("wm"), None, -MAGIC)
        lin(R("w8"), R("srow"), 0.25, -0.125)
        lin(R("s8"), R("srow"), 0.125)
        lin(R("tk"), R("tk0"), None, row)

    def thresholds():
        lin(R("wb"), R("w", 0, 1), 2.0, R("w", 1, 2))
        lin(R("by1", 1, 2), R("w", 1, 2), -8388608.0, -2048.0)
        lin(R("by1", 2, 3), R("w", 1, 2), 8388608.0, -2048.0)
        lin(R("k1"), R("wb"), 4096.0)
        lin(R("by1", 0, 1), R("wb"), -8388608.0, -2048.0)
        lin(R("by1", 3, 4), R("wb"), 8388608.0, -2048.0)
        lin(R("bx1"), R("by1"), -1.0)

    def rows_before(xs):
        for x in xs:
            sel(R("before", 128 * x, 128 * x + 128), R("bdrop"), [[16, 8], [0, 16]], A.is_gt, x, -1)

    build(0, B, gap0, gap1, gap2, gap3)
    sent0, got0 = send(0, gap4, nothing, nothing)

    for q in range(24 - OWN_ROWS):
        if q % 4:
            a = M - 16 * (OWN_ROWS + q)
            iota((T.far[:, q, a:a + 16 * (q % 4)], [("far", range(M * q, M * q + M))]), [[0, 16 * (q % 4)]], 1)
    rows_before(range(1, 10))
    for h in ("hx1", "hy1"):
        iota(R(h, 0, 768, 3), [[0, 256]], -4096)
    iota(R("bk", B, B + 2 * M), [[0, 2 * M]], 0)
    for o in range(N):
        iota(clear(o), [[0, CAP]], 0)
    iota(R("ud"), [[0, M]], 1)
    for name in ("la", "lb"):
        cp(R(name + "f", 256, 512), R(name, 256, 512))
    ts(R("under"), R("i16"), row, DROP, A.is_gt, A.mult)

    for n, who in enumerate("xy"):
        for half in range(2):
            for i in range(3):
                if step(1, who, half, i)[0] < 4:
                    affine(1, who, half, i)
        for x in range(10 + 3 * n, 13 + 3 * n):
            ts(R("before", 128 * x, 128 * x + 128), R("blk"), R("under", x, x + 1), None, A.mult)
        ts(R("u%s1" % who), R("raw" + who), MAGIC, MAGIC, A.add, A.subtract)
    lin(R("trow"), R("se0"), R("krow"), R("srow"))
    lin(R("hold"), R("se0"), 0.0, R("srow"))
    act(W("sgn", 16, 144, 16), R("blk", 0, 128, 16), F.Copy, scale=R("w8"))
    act(R("blkf"), R("blk"), F.Copy, scale=R("s8"))

    keep(0, thresholds)

    ts(R("w0"), P(5, 200, 201), R("sc", 6, 7), HALF, A.mult, A.add)
    lin(R("n4q"), P(5, 200, 201), 1.0 / 4096)
    ts(R("scx1"), R("w0"), 8192.0, R("k1"), A.mult, A.add)
    lin(R("scy1"), R("scx1"), -1.0)
    affine(1, "y", 0, 0)
    hmask(1, "x", 0, "v")
    hmask(1, "y", 0)
    hmask(1, "y", 1)
    places(1, ("x", 0), between=lambda: cp(R("mo"), P(4, 64, 88)))
    act(quarter("sv", 0), col("x", 0, B), F.Copy)
    lin(R("tq"), R("n4q"), None, B / 4096.0)
    affine(1, "x", 1, 0)
    hmask(1, "x", 1)
    append(0)
    places(1, ("y", 0), ("y", 1))

    def others():
        ts(R("zf"), R("lc", 256, 512), R("tq"), BIAS, A.mult, A.add)
        places(1, ("x", 1), between=place_z)

    def taken():
        ts(R("om"), R("mo"), -float(M), 11.0, A.add, A.mult)
        ts(R("bm"), R("kf"), 0.25, float(J), A.mult, A.min)
        ts(R("n4"), R("n4q"), 4096.0, None, A.mult)
        tt(R("om2"), R("om"), R("bm"), A.max)
        cp(R("mo2"), R("om2"))

    build(1, B + M, others, nothing, nothing, nothing)
    sent1, got1 = send(1, nothing, taken, nothing)
    scatter(R("tbl"), R("mo2"), R("ud"))

    keep(1, nothing)
    ts(R("mo"), P(4, 64, 88), R("n4"), None, A.add)
    append(1)
    dma("y", "d_y", ext(T.y[:, :]), R("bk", B, B + 2 * M))

    g.wait_ge(T.sem.snt0, sent0)
    g.wait_ge(T.sem.snt1, sent1)
    g.wait_ge(T.sem.arrv0, got0)
    g.wait_ge(T.sem.arrv1, got1)
    for d in DMAS:
        g.wait_ge(T.sem[d], 256 if d == "d_used" else 16)
    for q in qsem:
        g.wait_ge(T.sem[qsem[q]], count[q])
